import numpy as np, ml_dtypes
CORES = [3,7,11,15,131,135,139,143]
N = 8
import mx_ref
BF = ml_dtypes.bfloat16
def entries(a):
    return np.ascontiguousarray(a.T).reshape(-1)
def table(e):
    return np.ascontiguousarray(np.reshape(e, (-1, 16)).T).astype(np.int32)
def gcols(t, e):
    v = np.concatenate([t.reshape(8, 16, -1, 4), np.zeros((8, 16, 1, 4), BF)], axis=2)
    return np.ascontiguousarray(np.stack([v[g][:, e[g]] for g in range(8)])).reshape(128, -1)
def tile(rs):
    return np.stack(rs, axis=2).reshape(128, -1).astype(BF)
def pick(q, e):
    c = np.concatenate([q[0].reshape(128, -1, 4), np.zeros((128, 1, 4), np.uint8)], axis=1); s = np.concatenate([q[1], np.ones((16, 1), np.uint8)], axis=1)
    return (np.ascontiguousarray(c[:, e].reshape(128, -1)), np.ascontiguousarray(s[:, e]))
def join(*qs):
    return (np.concatenate([q[0] for q in qs], axis=1), np.concatenate([q[1] for q in qs], axis=1))
def put(q, e, v):
    c, s = q[0].reshape(128, -1, 4).copy(), q[1].copy(); c[:, e] = v[0].reshape(128, -1, 4); s[:, e] = v[1]
    return (c.reshape(128, -1), s)
def pk(c, s):
    return (np.ascontiguousarray(c), mx_ref.live(s))
def emit(q):
    return q[0], q[1]
def packed(v, rng):
    q = [mx_ref.quantize(np.ascontiguousarray(v[r])) for r in range(N)]
    return np.stack([a for a, b in q]), np.stack([mx_ref.plane(b, rng) for a, b in q])
def values_of_codes():
    e, c = np.zeros((128, 128, 4), np.float32), np.zeros((128, 2, 4), np.uint8)
    e[np.arange(128), np.arange(128), 0] = 1
    c[:127, :, 0] = np.arange(256).reshape(2, 128).T[:127]
    return mx_ref.matmul(mx_ref.quantize(e.reshape(128, 512).astype(BF)), (c.reshape(128, 8), np.full((16, 2), 127, np.uint8))).T.reshape(-1).astype(np.float64)
CODE_VALUE, SCALE_VALUE = values_of_codes(), 2.0 ** (np.arange(256) - 127.0)
def decode(q):
    return (CODE_VALUE[q[0]].reshape(16, 8, -1, 4) * SCALE_VALUE[q[1]][:, None, :, None] + 0.0).reshape(128, -1).astype(np.float32)
def f(rng, *shape):
    return mx_ref.flush((rng.standard_normal(shape, dtype=np.float32) * np.exp2(rng.integers(-2, 3, shape[:-1] + (1,)))).astype(BF))
def wide(rng, *shape, cols=0):
    v = rng.standard_normal(shape, dtype=np.float32) * np.exp2(rng.integers(-12, 13, shape)).astype(np.float32)
    if cols: v *= np.repeat(np.exp2(rng.integers(-cols, cols + 1, shape[:-2] + (1, shape[-1] // 4))) * (rng.random(shape[:-2] + (1, shape[-1] // 4)) > 0.0625), 4, axis=-1).astype(np.float32)
    return mx_ref.flush(v.astype(BF))
C, TH, R = 256, 192, 3
def big(v):
    v = v.astype(np.float32)
    v[np.abs(v) < np.float32(2.0 ** -16)] = 0
    return v.astype(BF)
def numbers_of(rng):
    return {"x": big(f(rng, N, 128, 4 * C)), "u": np.array(f(rng, N, 128, 512)), "v": np.array(f(rng, N, 128, 512))}
def offers(rng):
    return np.stack([table(rng.integers(0, C, 8 * R * C)) for r in range(N)])
def layers(rng):
    return big(f(rng, N, 128, 2048)).reshape(N, 8, 16, 4, 8, 16, 4)
def weights(rng, w):
    c, p = packed(np.ascontiguousarray(w).reshape(N, 128, 2048), rng)
    return {"wc": c, "ws": p}
def setup_inputs(rng):
    return {**numbers_of(rng), "cd": offers(rng), **weights(rng, layers(rng))}
def setup_inputs_ties(rng):
    d = numbers_of(rng)
    x = d["x"].astype(np.float32).reshape(N, 8, 16, C, 4)
    x[:, :, 0] = 0
    k = rng.integers(-2, 3, (N, 4, C))
    for r in range(N): x[r, :, 0, :, 0] = k[r][rng.permutation(8) % 4]
    u = d["u"].reshape(N, 128, 128, 4)
    u[:, :, ::16] = 0
    o = rng.permutation(N)
    for r in range(N):
        for h in range(0, 128, 16): u[r, h, h, 0] = 0.0 if r == o[0] else -1.0 if r == o[1] else 1.0
    w = layers(rng)
    w[:, :, :, :, :, 0] = 0
    return {"x": x.reshape(N, 128, 4 * C).astype(BF), "u": u.reshape(N, 128, 512), "v": d["v"], "cd": offers(rng), **weights(rng, w)}
def setup_inputs_near(rng):
    d = numbers_of(rng)
    x = d["x"].astype(np.float32).reshape(N, 8, 16, C, 4)
    x[:, :, 0] = 0
    x[:, :, 8:] = 0
    u = d["u"].reshape(N, 128, 128, 4)
    u[:, :, ::16] = 0
    o = rng.permutation(N) % 4
    for r in range(N):
        s = rng.integers(0, 256, (8, C))
        if o[r] < 3:
            for b in range(8): x[r, :, 8 + b // 4, :, b % 4] = ((s >> b) & 1) * 2.0 ** (b - 23)
        else: x[r, :, 10, :, 0] = (8 + s % 8) * 2.0 ** -33
        if o[r] < 2:
            x[r, :, 0, :, 0] = rng.permutation(8)[:, None] % 2 * 2.0 - 1.0
            x[r, :, 11, :, 0] = 2.0 ** -10
        for g in rng.permutation(8)[:4]:
            j = rng.integers(C)
            x[r, g, 8:, j] = 0
            x[r, g, 8 if o[r] < 3 else 10, j, 0] = rng.choice([-1.0, 1.0]) * 2.0 ** 30
        for h in range(0, 128, 16):
            k = 1.0 if o[r] == 0 else 2.0 ** -30
            if o[r] > 1: k = k * rng.choice([-1.0, 1.0])
            if o[r] < 2:
                u[r, h, h, 0] = k
                u[r, h + 11, h, 0] = k
            if o[r] < 3: u[r, h + 8:h + 10, h] = k
            else: u[r, h + 10, h, 0] = k
    w = layers(rng)
    w[:, :, 0] = 0
    w[:, :, 8:] = 0
    w[:, :, :, :, :, 0] = 0
    w[:, :, :, :, :, 8:] = 0
    return {"x": x.reshape(N, 128, 4 * C).astype(BF), "u": u.reshape(N, 128, 512), "v": d["v"], "cd": offers(rng), **weights(rng, w)}
def setup_inputs_huge(rng):
    d = numbers_of(rng)
    o = rng.permutation(N)
    c = rng.choice([-1.0, 1.0], (N, 1, 1, C, 1))
    c[o < N // 2] = c[o < N // 2][:, :, :, :1]
    x = (0.6 + 0.09 * rng.random((N, 8, 16, C, 4))) * 2.0 ** 30 * c
    u = d["u"].reshape(N, 128, 128, 4)
    for r in range(N):
        a = np.full((128, 8, 4), 2.0 ** 30)
        if 0 < o[r] < N - 1: a = 2.0 ** 29 * (1.0 - 0.1 * rng.random((128, 8, 4)))
        if o[r] < N // 2: a = a * (rng.permutation(8) % 2 * 2.0 - 1.0)[None, :, None]
        u[r, :, ::16] = a.astype(np.float32).astype(BF)
    w = np.zeros((N, 128, 4, 128, 4), np.float32)
    i = np.arange(128)
    for b in range(4): w[:, i, b, i, b] = 4
    return {"x": x.astype(np.float32).reshape(N, 128, 4 * C).astype(BF), "u": u.reshape(N, 128, 512), "v": d["v"], "cd": offers(rng), **weights(rng, w.astype(BF))}
def setup_inputs_few(rng):
    d = numbers_of(rng)
    x = np.zeros((N, 8, 16, C, 4), np.float32)
    x[:, :, 1, :, 0] = 1.96875
    x[:, :, 2:4] = (129 + 2 * rng.integers(0, 64, (N, 8, 2, C, 4))) * np.exp2(-7.0 - rng.integers(8, 15, (N, 8, 2, C, 4))) * rng.choice([-1.0, 1.0], (N, 8, 2, C, 4))
    u = d["u"].reshape(N, 128, 128, 4)
    u[:, :, ::16] = 0
    for h in range(0, 128, 16): u[:, h, h, 0] = 1
    o, lists = rng.permutation(N), []
    for r in range(N):
        p = rng.permutation(C)
        s = rng.integers(8, 16, (8, C)) * 0.125
        s[:, p[TH:]] *= -1.0
        x[r, :, 0, :, 0] = s
        k = (rng.permutation(R * C) % 4).reshape(R, 1, C)
        low, high, e = p[rng.integers(TH, C, (R, 8, C))], p[rng.integers(0, TH, (R, 8, C))], rng.integers(0, C, (R, 8, C))
        e = np.where(k == 0, low, np.where(k == 1, high, np.where(k == 2, e, e[:, :1])))
        if r == o[0]: e = np.zeros((R, 8, C), np.int64)
        if r == o[1]: e = np.full((R, 8, C), C - 1)
        lists.append(table(e))
    w = np.zeros((N, 8, 16, 4, 8, 16, 4), np.float32)
    w[:, :, 2:4, :, :, 8:] = rng.choice([-1.0, 1.0], (N, 8, 2, 4, 8, 8, 4))
    return {"x": x.reshape(N, 128, 4 * C).astype(BF), "u": u.reshape(N, 128, 512), "v": d["v"], "cd": np.stack(lists), **weights(rng, w.astype(BF))}
def setup_inputs_spread(rng):
    d = setup_inputs(rng)
    d["x"] = big(wide(rng, N, 128, 4 * C, cols=6))
    return d
def check_inputs(d):
    b = []
    for k in ("x", "u", "v"):
        a = np.abs(d[k].astype(np.float32))
        if not (np.isfinite(a).all() and ((a == 0) | (a >= 2.0 ** -30) & (a <= 2.0 ** 30)).all()): b.append("a value of " + k)
    if not ((d["cd"] >= 0) & (d["cd"] < C)).all(): b.append("an entry of cd")
    none, least, most = [emit(mx_ref.quantize(np.full((128, 16), k, np.float32).astype(BF)))[1][0, 0] for k in (0.0, 2.0 ** -30, 2.0 ** 30)]
    for r in range(N):
        if ((d["wc"][r] == 0x7F) | (d["wc"][r] == 0xFF)).any(): b.append("wc: a code that is no number")
        s = mx_ref.live(d["ws"][r])
        if ((s != none) & ((s < least) | (s > most))).any(): b.append("ws: a scale out of range")
    return b
def reference(x, u, v, cd, wc, ws):
    qu = [mx_ref.quantize(u[r]) for r in range(N)]
    lay = [pk(wc[r], ws[r]) for r in range(N)]
    give = [entries(cd[r]).reshape(R, 8, C) for r in range(N)]
    now = [x[r] for r in range(N)]
    lead, i = np.zeros((N, 8, C), np.int64), np.arange(C)
    for t in range(R):
        q = [mx_ref.quantize(now[r]) for r in range(N)]
        own = [decode(q[r]) for r in range(N)]
        place = np.zeros((N, 8, C), np.int64)
        for r in range(N):
            s = mx_ref.matmul(qu[r], q[r])[::16] + np.float32(0.0)
            np.put_along_axis(place[r], np.argsort(-s, axis=1, kind="stable"), i[None, :], axis=1)
        made = [None] * N
        for d in range(N):
            r = (d - 1 - t) % N
            c = give[d][t]
            p = place[d][:, c]
            visit = np.argsort(place[r], axis=0, kind="stable")
            left = np.ones((8, C), bool)
            for g in visit:
                a = p[g, :, i].T
                stay = left & (a < TH)
                left = np.where(np.any(stay, axis=0), stay, left)
                k = np.argmin(np.where(left, a, C), axis=0)
                lead[d, g, i] = c[k, i]
            z = mx_ref.quantize(gcols(own[d].astype(BF), lead[d]))
            h = tile([np.maximum(mx_ref.matmul(pick(lay[d], np.arange(128 * b, 128 * b + 128)), z), np.float32(0.0)) * np.float32(0.015625) for b in range(4)])
            made[r] = (own[r] + decode(mx_ref.quantize(h))).astype(BF)
        now = made
    y, el = np.zeros((N, 128, C), np.float32), np.zeros((N, 8, C), np.float32)
    oc, osc = np.zeros((N, 128, 4 * C), np.uint8), np.zeros((N, 16, C), np.uint8)
    for r in range(N):
        q = mx_ref.quantize(now[r])
        y[r] = mx_ref.matmul(mx_ref.quantize(v[r]), q)
        el[r] = lead[r]
        oc[r], osc[r] = emit(q)
    return {"y": y, "el": el, "oc": oc, "osc": osc}

@@ -1,0 +1,569 @@
+import math
+from concourse.mybir import dt, AluOpType as ALU, ActivationFunctionType as ACT
+
+C, R, N, HC = 256, 3, 8, 128
+F32, BF, I32, U16, CODE, U8 = "float32", "bfloat16", "int32", "uint16", "float8_e4m3fn_x4", "uint8"
+_SIZES = {
+    BF: dict(xin=1024, uin=512, vin=512, ones=528, ebig=528, gi=136, bt=544, yi=128, thr=128, mi=64, rst8=128, da=256, sg=2048,
+             fl=4096, bf=128, oo=128, o2=128, f1=256, uu=256, nb=128, dw=1024, zt=1024, ht=1024, xt=1024),
+    F32: dict(pf=16, pc=16, pat=64, of=64, ci=256, iw=256, mk=64, cm=192, c2=96, c1=48, big8=128, ta=256, tb=256, w1=256, w2=256,
+              g32=32, lt=32, ga=128, dd=32, gk=256, kt=256, kf=128, sc=128, ms=128, cp=64, eg=1024, eb=256, yb=256),
+    I32: dict(cdr=384, pi=1, pb=16, ui=16, dg=64, ea=64, et=64),
+    U16: dict(off=64, uo=16, cand=48, zo=64, eo=64),
+    CODE: dict(uc=128, upc=256, vc=128, wq=512, ec=512, bc=256, fc=1024, zc=256),
+    U8: dict(us=128, ups=256, vs=128, wp=512, es=512, bs=256, fs=1024, zs=256),
+}
+SCRATCH = {"ps": ("psum", [128, 4096], F32)}
+for _d, _b in _SIZES.items():
+    for _k, _n in _b.items():
+        SCRATCH[_k] = ("sbuf", [128, _n], _d)
+for _t in range(R + 1):
+    for _k, _n, _d in (("tc", C, CODE), ("ts", C, U8), ("rs", 64, BF), ("rl", 64, BF), ("hc", C, CODE), ("hs", C, U8), ("lc", C, CODE), ("ls", C, U8)):
+        if _t < R or _k[0] == "t":
+            SCRATCH["%s%d" % (_k, _t)] = ("sbuf", [128, _n], _d)
+
+SEMAPHORES = ["V", "S", "P", "G", "dx0", "dx1", "du", "dcd", "dw", "dv", "dout", "sent"] + \
+    ["ra%d" % t for t in range(R)] + ["ha%d_%d" % (t, h) for t in range(R) for h in range(2)]
+
+
+def A(name, c0=0, c1=None, step=1, p0=0, p1=128):
+    if c1 is None:
+        c1 = SCRATCH[name][1][1]
+    return (name, p0, p1, c0, c1, step)
+
+
+def bank(k, c0=0, c1=C):
+    return A("ps", 512 * k + c0, 512 * k + c1)
+
+
+def _meet(a, b):
+    if a[2] <= b[1] or b[2] <= a[1] or a[4] <= b[3] or b[4] <= a[3]:
+        return False
+    if a[5] == b[5] and a[5] > 1:
+        return (a[3] - b[3]) % a[5] == 0
+    return True
+
+
+def _emit(g, T, ops):
+    queues = {"V": g.vector, "S": g.scalar, "P": g.tensor, "G": g, "Y": g.sync}
+    deps, seen = [], {}
+    for i, o in enumerate(ops):
+        d = set()
+        mine = [(a, False) for a in o["r"]] + [(a, True) for a in o["w"]]
+        for a, wa in mine:
+            for j, b, wb in seen.get(a[0], []):
+                if a[0] == "ps":
+                    if a[3] // 512 == b[3] // 512 and (o["q"] != ops[j]["q"] or (o["q"] != "P" and (wa or wb))):
+                        d.add(j)
+                elif (wa or wb) and _meet(a, b):
+                    d.add(j)
+        for a, wa in mine:
+            seen.setdefault(a[0], []).append((i, a, wa))
+        deps.append(d)
+    clock, known, need = [None] * len(ops), {q: {} for q in queues}, []
+    for i, o in enumerate(ops):
+        waits = []
+        if o["q"] is not None:
+            k = known[o["q"]]
+            for j in sorted(deps[i], reverse=True):
+                e = ops[j]
+                key, val = (e["sem"], 0) if "sem" in e else (e["q"], j)
+                if k.get(key, -1) >= val:
+                    continue
+                waits.append(j)
+                k[key] = val
+                for kk, vv in clock[j].items():
+                    if k.get(kk, -1) < vv:
+                        k[kk] = vv
+            clock[i] = dict(k)
+        else:
+            clock[i] = {}
+        need.append(waits)
+    signal = set(j for w in need for j in w if "sem" not in ops[j])
+    count, value, total = {}, {}, {}
+    for i, o in enumerate(ops):
+        if i in signal:
+            count[o["q"]] = count.get(o["q"], 0) + 1
+            value[i] = count[o["q"]]
+        if "sem" in o:
+            total[o["sem"]] = total.get(o["sem"], 0) + o["n"]
+    for i, o in enumerate(ops):
+        if o["q"] is None:
+            continue
+        q = queues[o["q"]]
+        for j in need[i]:
+            e = ops[j]
+            if "sem" in e:
+                q.wait_ge(T.sem[e["sem"]], total[e["sem"]])
+            else:
+                q.wait_ge(T.sem[e["q"]], value[j])
+        ins = o["f"](q)
+        if i in signal:
+            ins.then_inc(T.sem[o["q"]], 1)
+        elif o.get("dma"):
+            ins.then_inc(T.sem[o["sem"]], 16)
+    for s in ("sent", "dout"):
+        g.wait_ge(T.sem[s], total[s])
+
+
+def rank_program(g, core, T, topo):
+    rank = T.rank_of(core)
+    if rank is None:
+        return
+    ops = []
+
+    def v(a):
+        if not isinstance(a, tuple):
+            return a
+        if a[0] == "ind":
+            return v(a[1]).indirect(v(a[2]))
+        if a[5] == 1:
+            return T[a[0]][a[1]:a[2], a[3]:a[4]]
+        return T[a[0]][a[1]:a[2], a[3]:a[4]:a[5]]
+
+    def ind(win, offs):
+        return ("ind", win, offs)
+
+    def op(q, f, w, r, **more):
+        reads = []
+        for a in r:
+            if isinstance(a, tuple):
+                reads += [a[1], a[2]] if a[0] == "ind" else [a]
+        ops.append(dict(q=q, f=f, w=list(w), r=reads, **more))
+
+    def copy(out, in_):
+        op("V", lambda q: q.tensor_copy(v(out), v(in_)), [out], [in_])
+
+    def tt(out, a, b, o):
+        op("V", lambda q: q.tensor_tensor(v(out), v(a), v(b), o), [out], [a, b])
+
+    def ts(out, a, s1, o1, s2=None, o2=None):
+        if o2 is None:
+            op("V", lambda q: q.tensor_scalar(v(out), v(a), v(s1), None, o1), [out], [a, s1])
+        else:
+            op("V", lambda q: q.tensor_scalar(v(out), v(a), v(s1), v(s2), o1, o2), [out], [a, s1, s2])
+
+    def scan(out, d0, d1, o0, o1):
+        op("V", lambda q: q.tensor_tensor_scan(v(out), v(d0), v(d1), 0.0, o0, o1), [out], [d0, d1])
+
+    def turn(out, in_):
+        op("V", lambda q: q.transpose(v(out), v(in_)), [out], [in_])
+
+    def fill(out, c):
+        op("V", lambda q: q.memset(v(out), c), [out], [])
+
+    def quant(c, s, in_):
+        op("V", lambda q: q.quantize_mx(v(c), v(s), v(in_)), [c, s], [in_])
+
+    def act(out, in_, f, **kw):
+        op("S", lambda q: q.activation(v(out), v(in_), f, **{k: v(x) for k, x in kw.items()}), [out], [in_] + list(kw.values()))
+
+    def mm(out, lc, ls, rc, rs, start=True, stop=True):
+        op("P", lambda q: q.matmul_mx(v(out), v(lc), v(ls), v(rc), v(rs), start, stop), [out], [lc, ls, rc, rs])
+
+    def iota(out, pattern, base=0, cm=0):
+        if SCRATCH[out[0]][2] == I32:
+            op("G", lambda q: q.iota(v(out), pattern, base, cm), [out], [])
+        else:
+            op("G", lambda q: q.iota(v(out), pattern, base, cm, allow_small_or_imprecise_dtypes=True), [out], [])
+
+    def dma(q, sem, out, in_, w, r):
+        op(q, lambda e: e.dma_start(out, in_), w, r, sem=sem, n=16, dma=True)
+
+    def raw(a):
+        return v(a).bitcast(dt.uint8)
+
+    peers = [T.cores[(rank + d) % N] for d in range(1, R + 1)] + [T.cores[(rank - d) % N] for d in range(1, R + 1)]
+    mask = topo.mask(core, peers[0])
+    for p in peers:
+        mask = mask & topo.mask(core, p)
+    nen = bin(mask).count("1")
+
+    def send(dst, out, in_, src, sem):
+        rid, pid = topo.addr(dst, core)
+        op("G", lambda q: q.remote_dma(out, in_, T.sem[sem], T.sem.sent, pid, rid, mask), [], [src], sem="sent", n=nen)
+
+    def arrive(views, sem, calls):
+        op(None, None, views, [], sem=sem, n=nen * calls)
+
+    def pair(c, s, c0=0, c1=C):
+        return A(c, c0, c1), A(s, c0, c1)
+
+    def half(c, s, h):
+        return pair(c, s, HC * h, HC * h + HC)
+
+    def pf(c):
+        return A("pf", c, c + 1)
+
+    def pc(c):
+        return A("pc", c, c + 1)
+
+    def pb(c):
+        return A("pb", c, c + 1)
+
+    def offs(o, k):
+        return A("off", o, o + k)
+
+    def of(o, k):
+        return A("of", o, o + k)
+
+    def pat(o, k):
+        return A("pat", o, o + k)
+
+    dma("S", "du", T.uin[:, :], T.u[:, :], [A("uin")], [])
+    for h in range(2):
+        dma("Y", "dx%d" % h, T.xin[:, 512 * h:512 * h + 512], T.x[:, 512 * h:512 * h + 512], [A("xin", 512 * h, 512 * h + 512)], [])
+    for a in range(4):
+        for m in range(8):
+            p0 = 32 * a + 4 * m
+            dma("Y", "dcd", T.cdr[p0:p0 + 4, :], T.cd[a:16:4, :], [A("cdr", p0=p0, p1=p0 + 4)], [])
+    dma("Y", "dw", raw(A("wq")), T.wc[:, :], [A("wq")], [])
+    dma("Y", "dw", T.wp[:, :], T.ws[:, :], [A("wp")], [])
+    dma("Y", "dv", T.vin[:, :], T.v[:, :], [A("vin")], [])
+
+    O_DIAG, O_OWN, O_G, O_GP, O_PREV, O_EXP, O_NK, O_KF, O_DUP, O_CD = 0, 8, 10, 18, 26, 28, 32, 40, 48, 52
+    iota(A("pi"), [[0, 1]], 0, 1)
+    iota(A("ui"), [[16, 2], [32, 4], [0, 2]])
+    iota(A("gi"), [[0, 17], [1, 8]])
+    iota(A("yi"), [[0, 4], [1, 32]])
+    iota(pat(O_DIAG, 8), [[C + 32, 4], [16, 2]])
+    iota(pat(O_OWN, 2), [[64, 2]])
+    iota(pat(O_G, 8), [[16, 2], [2, 4]])
+    iota(pat(O_GP, 8), [[16, 2], [0, 4]])
+    iota(pat(O_EXP, 4), [[0, 2], [8, 2]])
+    iota(pat(O_DUP, 4), [[8, 2], [1, 2]])
+    iota(pat(O_CD, 12), [[32, 12]])
+    fill(A("big8"), 0.0)
+    fill(A("ones"), 1.0)
+    fill(A("big8", 0, 128, 8), 1000.0)
+    op("G", lambda q: q.affine_select(v(A("ebig")), v(A("ones")), [[-1, 528]], ALU.is_equal, 0.0, 3, 4), [A("ebig")], [A("ones")])
+    iota(A("ci"), [[1, 256]])
+    iota(A("mi"), [[0, 16], [1, 4]])
+    act(A("rst8"), A("big8"), ACT.Exp, scale=-1.0)
+    S7, S3, N4, BA, S15, B3, SA, X31 = range(8)
+    for col, sh, bits in ((BA, 5, 3), (X31, 0, 31), (S7, 0, 7), (S3, 3, 1), (N4, 4, 1), (S15, 0, 15), (B3, 0, 3), (SA, 2, 3)):
+        ts(pb(col), A("pi"), sh, ALU.logical_shift_right, bits, ALU.bitwise_and)
+    copy(A("uo"), A("ui"))
+    copy(A("pf", 0, 8), A("pb", 0, 8))
+    fill(A("dd"), 200.0)
+    ts(pc(5), pf(BA), 2.0, ALU.mult, 1.0, ALU.add)
+    ts(A("thr"), A("yi"), pf(X31), ALU.is_gt, -2.0 ** -120, ALU.mult)
+    ts(pc(0), pf(S15), 4.0, ALU.mult, pf(BA), ALU.add)
+    ts(pb(10), pf(S7), 7.0, ALU.add)
+    for k in range(4):
+        ts(A("bt", k, 544, 4), A("gi"), pc(5), ALU.is_equal, 1.0 / 256, ALU.mult)
+    ts(pc(2), pf(S15), 0.0, ALU.is_equal, 8.0, ALU.mult)
+    ts(pc(9), pf(N4), 128.0, ALU.mult, pc(0), ALU.add)
+    ts(pb(12), pb(10), 7, ALU.bitwise_and)
+    ts(pc(11), pf(S3), 64.0, ALU.mult, 7.0, ALU.add)
+    ts(of(O_DIAG, 8), pat(O_DIAG, 8), pf(S15), ALU.add)
+    quant(*pair("bc", "bs", 0, 128), A("bt", 4, 516))
+    quant(*pair("bc", "bs", 128, 256), A("bt", 0, 512))
+    copy(offs(O_DIAG, 8), of(O_DIAG, 8))
+    quant(A("uc"), A("us"), A("uin"))
+    quant(*half("tc0", "ts0", 0), A("xin", 0, 512))
+    act(A("ups"), ind(A("us"), A("uo")), ACT.Copy)
+    op("V", lambda q: q.tensor_copy(T.upc[:, :].bitcast(dt.uint32), T.uc[:, :].bitcast(dt.uint32).indirect(T.uo[:, :])), [A("upc")], [A("uc"), A("uo")])
+    quant(*half("tc0", "ts0", 1), A("xin", 512, 1024))
+    ts(pc(12), pc(2), pf(S7), ALU.add)
+    ts(of(O_PREV, 2), A("pb", 11, 13, 1), 8.0, ALU.mult, pc(11), ALU.add) if False else ts(of(O_PREV, 1), pb(12), 8.0, ALU.mult, pc(11), ALU.add)
+
+    def e_(b):
+        return pair("ec", "es", 128 * b, 128 * b + 128)
+
+    DB = (0, 1, 2, 7)
+
+    def unit(b):
+        quant(*e_(b), A("ebig", 3 - b, 515 - b))
+        mm(bank(DB[b]), *e_(b), *pair("tc0", "ts0"))
+
+    later = [lambda: unit(0), lambda: unit(1), lambda: unit(2), lambda: unit(3),
+             lambda: ts(pc(3), pf(S3), 16.0, ALU.mult, pf(S7), ALU.add),
+             lambda: ts(pc(1), pf(S7), 32.0, ALU.mult, pf(S3), ALU.add),
+             lambda: ts(pc(10), pf(N4), 8.0, ALU.mult, pc(3), ALU.add),
+             lambda: ts(pb(9), pf(SA), pf(BA), ALU.subtract, 4.0, ALU.add),
+             lambda: ts(of(O_CD, 12), pat(O_CD, 12), pc(10), ALU.add),
+             lambda: ts(A("mk"), A("mi"), pf(SA), ALU.is_equal),
+             lambda: copy(offs(O_CD, 12), of(O_CD, 12)),
+             lambda: ts(offs(O_NK, 8), pat(O_G, 8), pc(1), ALU.add, 8.0, ALU.add),
+             lambda: ts(offs(O_KF, 8), pat(O_G, 8), pc(1), ALU.add)]
+    latest = [lambda: ts(pb(11), pb(9), 3, ALU.bitwise_and),
+              lambda: ts(pc(4), pf(BA), 2.0, ALU.mult),
+              lambda: ts(pc(6), pf(B3), 256.0, ALU.mult),
+              lambda: ts(pc(13), pb(11), 16.0, ALU.mult, pc(4), ALU.add),
+              lambda: ts(offs(O_DUP, 4), pat(O_DUP, 4), pc(13), ALU.add)]
+
+    def spare(k, todo=later):
+        for _ in range(k):
+            if todo:
+                todo.pop(0)()
+
+    def candidates(t, step):
+        if step == 0:
+            tt(A("cm", 64 * t, 64 * t + 64), ind(A("cdr"), offs(O_CD + 4 * t, 4)), A("mk"), ALU.mult)
+        elif step == 1:
+            tt(A("c2", 32 * t, 32 * t + 32), A("cm", 64 * t, 64 * t + 64, 2), A("cm", 64 * t + 1, 64 * t + 64, 2), ALU.add)
+        elif step == 2:
+            tt(A("c1", 16 * t, 16 * t + 16), A("c2", 32 * t, 32 * t + 32, 2), A("c2", 32 * t + 1, 32 * t + 32, 2), ALU.add)
+        else:
+            copy(A("cand", 16 * t, 16 * t + 16), A("c1", 16 * t, 16 * t + 16))
+
+    def slot(tile, t, c0, c1):
+        return A("fl", 1024 * tile + 4 * c0 + t, 1024 * tile + 4 * c1, 4)
+
+    def place(base, s, c0, c1):
+        return slot(base, s, c0, c1) if s < 3 else slot(base + 1, s - 3, c0, c1)
+
+    def pack(tile, c0, c1):
+        quant(*pair("fc", "fs", C * tile + c0, C * tile + c1), A("fl", 1024 * tile + 4 * c0, 1024 * tile + 4 * c1))
+
+    def count(tile, first=False, last=False):
+        b = 128 * (tile // 2)
+        mm(bank(3), *pair("bc", "bs", b, b + 128), *pair("fc", "fs", C * tile, C * tile + C), first, last)
+
+    def row(t, k, odd, c0, c1):
+        mm(bank(k, 0, c1 - c0), *half("upc", "ups", odd), *pair("tc%d" % t, "ts%d" % t, c0, c1))
+
+    def le_v(bk, s, c0, c1):
+        ts(place(0, s, c0, c1), bank(bk, c0, c1), A("ta", 32 * s, 32 * s + 1), ALU.is_le)
+
+    def lt_v(bk, s):
+        ts(place(0, s, 0, 32 * (s + 1)), bank(bk, 0, 32 * (s + 1)), A("ta", 32 * (s + 1), 32 * (s + 1) + 1), ALU.is_lt)
+
+    def sign(bk, b, c0, c1):
+        act(A("sg", C * b + c0, C * b + c1), bank(bk, c0, c1), ACT.Sign, scale=-1.0, bias=A("tb", 32 * b, 32 * b + 1))
+
+    def le_s(s, c0, c1):
+        act(place(2, s, c0, c1), A("sg", C * s + c0, C * s + c1), ACT.Sign, bias=1.0)
+
+    def lt_s(s, c0=0, c1=C):
+        c1 = min(c1, 32 * (s + 1))
+        act(place(2, s, c0, c1), A("sg", C * (s + 1) + c0, C * (s + 1) + c1), ACT.Relu)
+
+    def diagonal(h, bk, part):
+        c0, c1 = HC * h, HC * h + HC
+        if part == 0:
+            tt(A("da", c0, c1), A("ta", c0, c1), bank(bk, c0, c1), ALU.subtract)
+        elif part == 1:
+            tt(slot(0, 3, c0, c1), A("da", c0, c1), A("thr"), ALU.is_gt)
+        else:
+            w0 = (4 * C + HC) * h
+            tt(slot(2, 3, c0, c1), ind(A("sg", w0, w0 + 3 * C + HC), offs(O_DIAG, 8)), A("thr"), ALU.is_gt)
+
+    def new_state(t, h, part):
+        x0 = 512 * h
+        if t == 0:
+            return
+        if part == "p":
+            for b in (0, 2, 1, 3):
+                mm(bank(4 * h + b, 0, HC), *e_(b), *half("lc%d" % (t - 1), "ls%d" % (t - 1), h), False, True)
+        elif part == "v":
+            for b in (0, 1):
+                copy(A("xt", x0 + b, x0 + 512, 4), bank(4 * h + b, 0, HC))
+        elif part == "s":
+            for b in (2, 3):
+                act(A("xt", x0 + b, x0 + 512, 4), bank(4 * h + b, 0, HC), ACT.Copy)
+        else:
+            quant(*half("tc%d" % t, "ts%d" % t, h), A("xt", x0, x0 + 512))
+
+    for t in range(R):
+        donor, child = T.cores[(rank + 1 + t) % N], T.cores[(rank - 1 - t) % N]
+        tc, tsc = "tc%d" % t, "ts%d" % t
+        for part in "pvsq":
+            new_state(t, 0, part)
+        row(t, 1, 1, 0, HC)
+        row(t, 0, 0, 0, HC)
+        row(t, 2, 1, 0, HC)
+        new_state(t, 1, "p")
+        turn(A("tb", 0, HC), bank(1, 0, HC))
+        turn(A("ta", 0, HC), bank(0, 0, HC))
+        for b in range(4):
+            sign(2, b, 0, HC)
+        if t == 0:
+            ts(of(O_OWN, 2), pat(O_OWN, 2), pc(9), ALU.add)
+        for s in range(3):
+            le_v(0, s, 32 * (s + 1), HC)
+            lt_v(0, s)
+        diagonal(0, 0, 0)
+        new_state(t, 1, "s")
+        new_state(t, 1, "v")
+        for s in range(3):
+            le_s(s, 32 * (s + 1), HC)
+            lt_s(s)
+        diagonal(0, 0, 2)
+        new_state(t, 1, "q")
+        row(t, 4, 0, 0, C)
+        row(t, 6, 1, 0, C)
+        row(t, 5, 1, HC, C)
+        diagonal(0, 0, 1)
+        pack(2, 0, HC)
+        if t == 0:
+            ts(of(O_G, 8), pat(O_G, 8), pf(S3), ALU.add)
+            ts(of(O_GP, 8), pat(O_GP, 8), pf(S7), ALU.add)
+            ts(A("of", O_EXP + 1, O_EXP + 4, 2), A("pat", O_EXP + 1, O_EXP + 4, 2), pc(12), ALU.add)
+            ts(A("of", O_EXP, O_EXP + 4, 2), A("pat", O_EXP, O_EXP + 4, 2), pc(12), ALU.add, pc(2), ALU.add)
+            ts(pc(8), pf(S7), 1.0 / 2048.0, ALU.mult)
+        pack(0, 0, HC)
+        if t > 0:
+            for b in range(4):
+                mm(bank(DB[b]), *e_(b), *pair(tc, tsc))
+        for b in range(4):
+            sign(6, b, HC, C)
+        le_v(4, 0, HC, C)
+        turn(A("tb", HC, C), bank(5, 0, HC))
+        turn(A("ta", HC, C), bank(4, HC, C))
+        for s in range(3):
+            le_s(s, HC, C)
+        for b in range(4, 8):
+            sign(6, b, 0, C)
+        for s in range(3, 7):
+            lt_s(s, 0, HC)
+        for s in range(3, 7):
+            le_s(s, 32 * (s + 1), C)
+            if s > 3:
+                lt_s(s, HC, C)
+        for s in range(1, 3):
+            le_v(4, s, HC, C)
+        diagonal(1, 4, 0)
+        le_v(4, 3, HC, C)
+        lt_v(4, 3)
+        diagonal(1, 4, 1)
+        if t == 0:
+            copy(offs(O_OWN, O_PREV + 1 - O_OWN), of(O_OWN, O_PREV + 1 - O_OWN))
+            copy(offs(O_EXP, 4), of(O_EXP, 4))
+        le_v(4, 4, 160, C)
+        lt_v(4, 4)
+        pack(0, HC, C)
+        count(0, first=True)
+        for s in range(5, 7):
+            le_v(4, s, 32 * (s + 1), C)
+            lt_v(4, s)
+        diagonal(1, 4, 2)
+        pack(1, 0, C)
+        count(1)
+        pack(2, HC, C)
+        count(2)
+        pack(3, 0, HC)
+        pack(3, HC, C)
+        count(3, last=True)
+        if t == 0:
+            act(A("iw"), A("ci"), ACT.Identity, scale=1.0 / 65536, bias=pf(S3))
+        else:
+            for b in range(4):
+                act(A("dw", C * b, C * b + C), bank(DB[b]), ACT.Copy)
+        spare(1)
+        ts(A("w1"), bank(3), pc(8), ALU.add)
+        spare(1)
+        copy(A("g32"), ind(A("w1"), offs(O_OWN, 2)))
+        spare(1)
+        turn(A("lt"), A("g32"))
+        spare(1)
+        copy(A("ga"), ind(A("lt"), offs(O_G, 8)))
+        spare(1)
+        tt(A("bf"), ind(A("lt"), offs(O_GP, 8)), A("ga"), ALU.is_lt)
+        spare(1)
+        scan(A("oo"), A("rst8"), A("bf"), ALU.mult, ALU.add)
+        scan(A("o2"), A("rst8"), A("bf"), ALU.mult, ALU.add)
+        spare(1)
+        tt(A("dd", 0, 16), ind(A("oo"), offs(O_PREV, 1)), A("o2", 7, 128, 8), ALU.subtract)
+        act(A("rs%d" % t), ind(A("dd"), offs(O_EXP, 4)), ACT.Exp, scale=-math.log(2.0))
+        send(donor, v(A("rl%d" % t)), v(A("rs%d" % t)), A("rs%d" % t), "ra%d" % t)
+        arrive([A("rl%d" % t)], "ra%d" % t, 1)
+        if t == 0:
+            for b in range(4):
+                act(A("dw", C * b, C * b + C), bank(DB[b]), ACT.Copy)
+            spare(4)
+            tt(A("w2"), A("iw"), bank(3), ALU.add)
+            for step in range(4):
+                candidates(0, step)
+                spare(1)
+                spare(1, latest)
+            copy(A("gk"), ind(A("w2"), A("cand", 0, 16)))
+            spare(1, latest)
+        else:
+            tt(A("w2"), A("iw"), bank(3), ALU.add)
+            copy(A("gk", 0, HC), ind(A("w2"), A("cand", 16 * t, 16 * t + 8)))
+            act(A("gk", HC, C), ind(A("w2"), A("cand", 16 * t + 8, 16 * t + 16)), ACT.Copy)
+        turn(A("kt"), A("gk"))
+        act(A("kf"), ind(A("kt"), offs(O_KF, 8)), ACT.Copy)
+        ts(A("f1"), A("kt"), 192.0 / 256, ALU.is_lt)
+        for k in range(4):
+            scan(A("uu", 64 * k, 64 * k + 64), A("rl%d" % t), A("f1", 64 * k, 64 * k + 64), ALU.mult, ALU.add)
+        ts(A("nb", 0, 64), ind(A("uu"), offs(O_NK, 4)), 0.5, ALU.mult, 128.5 + 2.0 ** -9, ALU.add)
+        act(A("nb", 64, 128), ind(A("uu"), offs(O_NK + 4, 4)), ACT.Identity, scale=0.5, bias=128.5 + 2.0 ** -9)
+        tt(A("sc"), A("kf"), A("nb"), ALU.subtract)
+        scan(A("ms"), A("big8"), A("sc"), ALU.add, ALU.min)
+        moves = [(0, 0, 0, 128), (2, 0, 64, 64), (2, 64, 0, 64)]
+        moves += [(d, 32 * a, 32 * ((a + d) % 4), 32) for d in (1, 3) for a in range(4)]
+        for k, (d, to, fr, n) in enumerate(moves):
+            o_, i_ = A("cp", 16 * d, 16 * d + 16, 1, to, to + n), A("ms", 7, 128, 8, fr, fr + n)
+            if k % 2 == 0:
+                ts(o_, i_, 65536.0, ALU.mult)
+            else:
+                act(o_, i_, ACT.Copy, scale=65536.0)
+        copy(A("dg"), ind(A("cp"), offs(O_DUP, 4)))
+        ts(A("ea"), A("dg"), C - 1, ALU.bitwise_and)
+        turn(A("et"), A("ea"))
+        ts(A("zo"), A("et"), pc(6), ALU.add)
+
+        def mosaic(q):
+            o_, i_ = A("zt", 256 * q, 256 * q + 256), ind(A("dw"), A("zo", 16 * q, 16 * q + 16))
+            if q % 2 == 0:
+                copy(o_, i_)
+            else:
+                act(o_, i_, ACT.Copy)
+
+        def layer(h):
+            quant(*half("zc", "zs", h), A("zt", 512 * h, 512 * h + 512))
+            for b in (0, 2, 1, 3):
+                mm(bank(4 * h + b, 0, HC), *pair("wq", "wp", 128 * b, 128 * b + 128), *half("zc", "zs", h))
+
+        def relu(h):
+            for b in (0, 1):
+                ts(A("ht", 512 * h + b, 512 * h + 512, 4), bank(4 * h + b, 0, HC), 0.0, ALU.max, 0.015625, ALU.mult)
+                act(A("ht", 512 * h + b + 2, 512 * h + 512, 4), bank(4 * h + b + 2, 0, HC), ACT.Relu, scale=0.015625)
+
+        def ship(h):
+            hc, hs = half("hc%d" % t, "hs%d" % t, h)
+            lc, ls = half("lc%d" % t, "ls%d" % t, h)
+            quant(hc, hs, A("ht", 512 * h, 512 * h + 512))
+            send(child, raw(lc), raw(hc), hc, "ha%d_%d" % (t, h))
+            send(child, v(ls), v(hs), hs, "ha%d_%d" % (t, h))
+            arrive([lc, ls], "ha%d_%d" % (t, h), 2)
+
+        mosaic(0)
+        mosaic(1)
+        mosaic(3)
+        layer(0)
+        mosaic(2)
+        relu(0)
+        layer(1)
+        ship(0)
+        relu(1)
+        ship(1)
+        for h in range(2):
+            for b in range(4):
+                mm(bank(4 * h + b, 0, HC), *e_(b), *half(tc, tsc, h), True, False)
+        if t < R - 1:
+            for step in range(4):
+                candidates(t + 1, step)
+        else:
+            copy(A("eo"), A("et"))
+            quant(A("vc"), A("vs"), A("vin"))
+            act(A("eg"), ind(A("ci"), A("eo")), ACT.Copy)
+            act(A("eb"), A("eg", 0, 1024, 4), ACT.Copy)
+            for k in range(8):
+                dma("Y", "dout", T.el[k:k + 1, :], T.eb[16 * k:16 * k + 1, :], [], [A("eb")])
+    tc, tsc = "tc%d" % R, "ts%d" % R
+    for h in range(2):
+        for part in "pvsq":
+            new_state(R, h, part)
+        c0, c1 = HC * h, HC * h + HC
+        mm(bank(4 * h, 0, HC), A("vc"), A("vs"), *half(tc, tsc, h))
+        dma("Y", "dout", T.oc[:, 4 * c0:4 * c1], raw(A(tc, c0, c1)), [], [A(tc, c0, c1)])
+        if h == 1:
+            for k in range(4):
+                dma("S" if k % 2 else "Y", "dout", T.osc[4 * k:4 * k + 4, :], T[tsc][32 * k:32 * k + 4, :], [], [A(tsc)])
+        copy(A("yb", c0, c1), bank(4 * h, 0, HC))
+        dma("Y" if h == 0 else "S", "dout", T.y[:, c0:c1], T.yb[:, c0:c1], [], [A("yb", c0, c1)])
+    _emit(g, T, ops)

@@ -4,14 +4,14 @@ from concourse.mybir import dt, AluOpType as ALU, ActivationFunctionType as ACT
 C, R, N, HC = 256, 3, 8, 128
 F32, BF, I32, U16, CODE, U8 = "float32", "bfloat16", "int32", "uint16", "float8_e4m3fn_x4", "uint8"
 _SIZES = {
-    BF: dict(xin=1024, uin=512, vin=512, ones=528, ebig=528, gi=136, bt=544, yi=128, thr=128, mi=64, rst8=128, da=256, sg=2048,
-             fl=4096, bf=128, oo=128, o2=128, f1=256, uu=256, nb=128, dw=1024, zt=1024, ht=1024, xt=1024),
-    F32: dict(pf=16, pc=16, pat=64, of=64, ci=256, iw=256, mk=64, cm=192, c2=96, c1=48, big8=128, ta=256, tb=256, w1=256, w2=256,
-              g32=32, lt=32, ga=128, dd=32, gk=256, kt=256, kf=128, sc=128, ms=128, cp=64, eg=1024, eb=256, yb=256),
-    I32: dict(cdr=384, pi=1, pb=16, ui=16, dg=64, ea=64, et=64),
-    U16: dict(off=64, uo=16, cand=48, zo=64, eo=64),
-    CODE: dict(uc=128, upc=256, vc=128, wq=512, ec=512, bc=256, fc=1024, zc=256),
-    U8: dict(us=128, ups=256, vs=128, wp=512, es=512, bs=256, fs=1024, zs=256),
+    BF: dict(xin=1024, uin=512, vin=512, ones=528, ebig=528, gi=136, bt=544, yi=128, thr=128, mi=64, da=256, sg=2048, pa=160, x1=160, x2=160,
+             x3=132, bd=528, ex=256, rr=256, th64=64, thj=256, bf=256, oo=272, fl=4096, f1=256, nb=128, dw=1024, zt=1024, ht=1024, xt=1024),
+    F32: dict(pf=16, pc=16, pat=64, ci=256, iw=256, mk=64, cm=192, c2=96, c1=48, big8=128, ta=256, tb=256, w2=256, zi=32, zt32=32,
+              lt=64, uu=256, gk=256, kt=256, kf=128, sc=128, ms=128, cp=64, eb=16, yb=256),
+    I32: dict(cdr=384, pi=1, pb=16, ui=16, pb1=160, pbm=160, oi=8, oj=8, dg=64, ea=64, et=64),
+    U16: dict(off=64, uo=16, cand=48, zo=64),
+    CODE: dict(uc=128, upc=256, vc=128, wq=512, ec=512, bc=256, dc=256, fc=1024, zc=256),
+    U8: dict(us=128, ups=256, vs=128, wp=512, es=512, bs=256, ds=256, fs=1024, zs=256),
 }
 SCRATCH = {"ps": ("psum", [128, 4096], F32)}
 for _d, _b in _SIZES.items():
@@ -204,9 +204,6 @@ def rank_program(g, core, T, topo):
     def offs(o, k):
         return A("off", o, o + k)
 
-    def of(o, k):
-        return A("of", o, o + k)
-
     def pat(o, k):
         return A("pat", o, o + k)
 
@@ -221,52 +218,51 @@ def rank_program(g, core, T, topo):
     dma("Y", "dw", T.wp[:, :], T.ws[:, :], [A("wp")], [])
     dma("Y", "dv", T.vin[:, :], T.v[:, :], [A("vin")], [])
 
-    O_DIAG, O_OWN, O_G, O_GP, O_PREV, O_EXP, O_NK, O_KF, O_DUP, O_CD = 0, 8, 10, 18, 26, 28, 32, 40, 48, 52
+    O_DIAG, O_ORD, O_EXP, O_NK, O_KF, O_DUP, O_CD = 0, 8, 24, 28, 36, 44, 48
+    S7, S3, N4, BA, S15, B3, SA, X31 = range(8)
     iota(A("pi"), [[0, 1]], 0, 1)
     iota(A("ui"), [[16, 2], [32, 4], [0, 2]])
-    iota(A("gi"), [[0, 17], [1, 8]])
+    iota(A("pb1"), [[0, 5], [1, 8], [1, 4]], 1)
+    iota(A("pa"), [[0, 5], [1, 8], [0, 4]])
     iota(A("yi"), [[0, 4], [1, 32]])
     iota(pat(O_DIAG, 8), [[C + 32, 4], [16, 2]])
-    iota(pat(O_OWN, 2), [[64, 2]])
-    iota(pat(O_G, 8), [[16, 2], [2, 4]])
-    iota(pat(O_GP, 8), [[16, 2], [0, 4]])
-    iota(pat(O_EXP, 4), [[0, 2], [8, 2]])
-    iota(pat(O_DUP, 4), [[8, 2], [1, 2]])
-    iota(pat(O_CD, 12), [[32, 12]])
-    fill(A("big8"), 0.0)
-    fill(A("ones"), 1.0)
-    fill(A("big8", 0, 128, 8), 1000.0)
-    op("G", lambda q: q.affine_select(v(A("ebig")), v(A("ones")), [[-1, 528]], ALU.is_equal, 0.0, 3, 4), [A("ebig")], [A("ones")])
-    iota(A("ci"), [[1, 256]])
-    iota(A("mi"), [[0, 16], [1, 4]])
-    act(A("rst8"), A("big8"), ACT.Exp, scale=-1.0)
-    S7, S3, N4, BA, S15, B3, SA, X31 = range(8)
-    for col, sh, bits in ((BA, 5, 3), (X31, 0, 31), (S7, 0, 7), (S3, 3, 1), (N4, 4, 1), (S15, 0, 15), (B3, 0, 3), (SA, 2, 3)):
+    iota(A("zi"), [[0, 2], [20, 4], [-3, 4]], 28)
+    iota(A("zi", 4, 12), [[1, 8]], 28)
+    iota(A("zi", 20, 28), [[1, 8]], 28)
+    iota(pat(O_ORD, 8), [[4, 8]])
+    iota(pat(O_EXP, 4), [[0, 2], [128, 2]], 15)
+    iota(A("gi"), [[0, 17], [1, 8]])
+    fill(A("ex"), 0.0)
+    fill(A("ex", 0, C, 4), -1.0)
+    fill(A("ex", 3, C, 4), 1.0)
+    act(A("rr"), A("ex"), ACT.Exp, scale=math.log(2.0))
+    for col, sh, bits in ((BA, 5, 3), (X31, 0, 31), (S7, 0, 7), (S15, 0, 15), (S3, 3, 1), (N4, 4, 1), (B3, 0, 3), (SA, 2, 3)):
         ts(pb(col), A("pi"), sh, ALU.logical_shift_right, bits, ALU.bitwise_and)
     copy(A("uo"), A("ui"))
     copy(A("pf", 0, 8), A("pb", 0, 8))
-    fill(A("dd"), 200.0)
+    fill(A("ones"), 1.0)
+    op("G", lambda q: q.affine_select(v(A("ebig")), v(A("ones")), [[-1, 528]], ALU.is_equal, 0.0, 3, 4), [A("ebig")], [A("ones")])
+    iota(A("ci"), [[1, 256]])
+    iota(A("mi"), [[0, 16], [1, 4]])
+    iota(pat(O_NK, 8), [[16, 2], [2, 4]])
+    iota(pat(O_DUP, 4), [[8, 2], [1, 2]])
+    iota(pat(O_CD, 12), [[32, 12]])
     ts(pc(5), pf(BA), 2.0, ALU.mult, 1.0, ALU.add)
+    ts(A("pbm"), A("pb1"), 7, ALU.bitwise_and)
+    fill(A("oo", C, C + 16), -400.0)
+    ts(pc(2), pf(S15), 0.0, ALU.is_equal, 1000.0, ALU.mult)
+    ts(A("x1"), A("pa"), pc(5), ALU.is_equal)
+    ts(A("x2"), A("pbm"), pc(5), ALU.is_equal)
     ts(A("thr"), A("yi"), pf(X31), ALU.is_gt, -2.0 ** -120, ALU.mult)
-    ts(pc(0), pf(S15), 4.0, ALU.mult, pf(BA), ALU.add)
-    ts(pb(10), pf(S7), 7.0, ALU.add)
-    for k in range(4):
-        ts(A("bt", k, 544, 4), A("gi"), pc(5), ALU.is_equal, 1.0 / 256, ALU.mult)
-    ts(pc(2), pf(S15), 0.0, ALU.is_equal, 8.0, ALU.mult)
-    ts(pc(9), pf(N4), 128.0, ALU.mult, pc(0), ALU.add)
-    ts(pb(12), pb(10), 7, ALU.bitwise_and)
-    ts(pc(11), pf(S3), 64.0, ALU.mult, 7.0, ALU.add)
-    ts(of(O_DIAG, 8), pat(O_DIAG, 8), pf(S15), ALU.add)
-    quant(*pair("bc", "bs", 0, 128), A("bt", 4, 516))
-    quant(*pair("bc", "bs", 128, 256), A("bt", 0, 512))
-    copy(offs(O_DIAG, 8), of(O_DIAG, 8))
+    ts(offs(O_DIAG, 8), pat(O_DIAG, 8), pf(S15), ALU.add)
     quant(A("uc"), A("us"), A("uin"))
     quant(*half("tc0", "ts0", 0), A("xin", 0, 512))
     act(A("ups"), ind(A("us"), A("uo")), ACT.Copy)
     op("V", lambda q: q.tensor_copy(T.upc[:, :].bitcast(dt.uint32), T.uc[:, :].bitcast(dt.uint32).indirect(T.uo[:, :])), [A("upc")], [A("uc"), A("uo")])
     quant(*half("tc0", "ts0", 1), A("xin", 512, 1024))
-    ts(pc(12), pc(2), pf(S7), ALU.add)
-    ts(of(O_PREV, 2), A("pb", 11, 13, 1), 8.0, ALU.mult, pc(11), ALU.add) if False else ts(of(O_PREV, 1), pb(12), 8.0, ALU.mult, pc(11), ALU.add)
+    tt(A("x3"), A("x1", 0, 132), A("x2", 0, 132), ALU.subtract)
+    for k in range(4):
+        act(A("bd", k, 528, 4), A("x3"), ACT.Copy)
 
     def e_(b):
         return pair("ec", "es", 128 * b, 128 * b + 128)
@@ -277,23 +273,42 @@ def rank_program(g, core, T, topo):
         quant(*e_(b), A("ebig", 3 - b, 515 - b))
         mm(bank(DB[b]), *e_(b), *pair("tc0", "ts0"))
 
-    later = [lambda: unit(0), lambda: unit(1), lambda: unit(2), lambda: unit(3),
+    def table(k):
+        ts(A("bt", k, 544, 4), A("gi"), pc(5), ALU.is_equal, 1.0 / 256, ALU.mult)
+
+    soon = [lambda: quant(*pair("dc", "ds", 0, 128), A("bd", 16, 528)),
+            lambda: quant(*pair("dc", "ds", 128, 256), A("bd", 0, 512)),
+            lambda: turn(A("zt32"), A("zi")),
+            lambda: ts(pc(12), pf(S7), 16.0, ALU.mult, pc(2), ALU.add),
+            lambda: ts(A("th64"), A("pb1", 0, 64), 8.0, ALU.is_lt, 0.5, ALU.subtract),
+            lambda: ts(A("oi"), pat(O_ORD, 8), A("zt32", 0, 1), ALU.add),
+            lambda: ts(offs(O_EXP, 4), pat(O_EXP, 4), pc(12), ALU.add, float(C), ALU.min),
+            lambda: ts(A("oj"), A("oi"), 31, ALU.bitwise_and),
+            lambda: fill(A("rr", 0, C, 16), 0.0),
+            lambda: fill(A("rr", 8, C, 16), -0.5),
+            lambda: copy(offs(O_ORD, 8), A("oj")),
+            lambda: ts(offs(O_ORD + 8, 8), A("oj"), 32.0, ALU.add)]
+    later = [lambda: table(0), lambda: table(1), lambda: table(2), lambda: table(3),
+             lambda: quant(*pair("bc", "bs", 0, 128), A("bt", 4, 516)),
+             lambda: quant(*pair("bc", "bs", 128, 256), A("bt", 0, 512)),
              lambda: ts(pc(3), pf(S3), 16.0, ALU.mult, pf(S7), ALU.add),
              lambda: ts(pc(1), pf(S7), 32.0, ALU.mult, pf(S3), ALU.add),
-             lambda: ts(pc(10), pf(N4), 8.0, ALU.mult, pc(3), ALU.add),
-             lambda: ts(pb(9), pf(SA), pf(BA), ALU.subtract, 4.0, ALU.add),
-             lambda: ts(of(O_CD, 12), pat(O_CD, 12), pc(10), ALU.add),
              lambda: ts(A("mk"), A("mi"), pf(SA), ALU.is_equal),
-             lambda: copy(offs(O_CD, 12), of(O_CD, 12)),
-             lambda: ts(offs(O_NK, 8), pat(O_G, 8), pc(1), ALU.add, 8.0, ALU.add),
-             lambda: ts(offs(O_KF, 8), pat(O_G, 8), pc(1), ALU.add)]
-    latest = [lambda: ts(pb(11), pb(9), 3, ALU.bitwise_and),
+             lambda: ts(pc(10), pf(N4), 8.0, ALU.mult, pc(3), ALU.add),
+             lambda: ts(offs(O_CD, 12), pat(O_CD, 12), pc(10), ALU.add)]
+    latest = [lambda: unit(0), lambda: unit(1), lambda: unit(2), lambda: unit(3),
+              lambda: ts(pb(9), pf(SA), pf(BA), ALU.subtract, 4.0, ALU.add),
+              lambda: ts(offs(O_NK, 8), pat(O_NK, 8), pc(1), ALU.add, 8.0, ALU.add),
+              lambda: ts(offs(O_KF, 8), pat(O_NK, 8), pc(1), ALU.add),
+              lambda: ts(pb(11), pb(9), 3, ALU.bitwise_and),
               lambda: ts(pc(4), pf(BA), 2.0, ALU.mult),
               lambda: ts(pc(6), pf(B3), 256.0, ALU.mult),
+              lambda: fill(A("big8"), 0.0),
               lambda: ts(pc(13), pb(11), 16.0, ALU.mult, pc(4), ALU.add),
+              lambda: fill(A("big8", 0, 128, 8), 1000.0),
               lambda: ts(offs(O_DUP, 4), pat(O_DUP, 4), pc(13), ALU.add)]
 
-    def spare(k, todo=later):
+    def spare(k, todo):
         for _ in range(k):
             if todo:
                 todo.pop(0)()
@@ -317,9 +332,9 @@ def rank_program(g, core, T, topo):
     def pack(tile, c0, c1):
         quant(*pair("fc", "fs", C * tile + c0, C * tile + c1), A("fl", 1024 * tile + 4 * c0, 1024 * tile + 4 * c1))
 
-    def count(tile, first=False, last=False):
+    def count(tile, bk=3, c="dc", s="ds"):
         b = 128 * (tile // 2)
-        mm(bank(3), *pair("bc", "bs", b, b + 128), *pair("fc", "fs", C * tile, C * tile + C), first, last)
+        mm(bank(bk), *pair(c, s, b, b + 128), *pair("fc", "fs", C * tile, C * tile + C), tile == 0, tile == 3)
 
     def row(t, k, odd, c0, c1):
         mm(bank(k, 0, c1 - c0), *half("upc", "ups", odd), *pair("tc%d" % t, "ts%d" % t, c0, c1))
@@ -379,8 +394,6 @@ def rank_program(g, core, T, topo):
         turn(A("ta", 0, HC), bank(0, 0, HC))
         for b in range(4):
             sign(2, b, 0, HC)
-        if t == 0:
-            ts(of(O_OWN, 2), pat(O_OWN, 2), pc(9), ALU.add)
         for s in range(3):
             le_v(0, s, 32 * (s + 1), HC)
             lt_v(0, s)
@@ -397,12 +410,7 @@ def rank_program(g, core, T, topo):
         row(t, 5, 1, HC, C)
         diagonal(0, 0, 1)
         pack(2, 0, HC)
-        if t == 0:
-            ts(of(O_G, 8), pat(O_G, 8), pf(S3), ALU.add)
-            ts(of(O_GP, 8), pat(O_GP, 8), pf(S7), ALU.add)
-            ts(A("of", O_EXP + 1, O_EXP + 4, 2), A("pat", O_EXP + 1, O_EXP + 4, 2), pc(12), ALU.add)
-            ts(A("of", O_EXP, O_EXP + 4, 2), A("pat", O_EXP, O_EXP + 4, 2), pc(12), ALU.add, pc(2), ALU.add)
-            ts(pc(8), pf(S7), 1.0 / 2048.0, ALU.mult)
+        spare(6, soon)
         pack(0, 0, HC)
         if t > 0:
             for b in range(4):
@@ -428,13 +436,11 @@ def rank_program(g, core, T, topo):
         le_v(4, 3, HC, C)
         lt_v(4, 3)
         diagonal(1, 4, 1)
-        if t == 0:
-            copy(offs(O_OWN, O_PREV + 1 - O_OWN), of(O_OWN, O_PREV + 1 - O_OWN))
-            copy(offs(O_EXP, 4), of(O_EXP, 4))
+        spare(6, soon)
         le_v(4, 4, 160, C)
         lt_v(4, 4)
         pack(0, HC, C)
-        count(0, first=True)
+        count(0)
         for s in range(5, 7):
             le_v(4, s, 32 * (s + 1), C)
             lt_v(4, s)
@@ -445,48 +451,49 @@ def rank_program(g, core, T, topo):
         count(2)
         pack(3, 0, HC)
         pack(3, HC, C)
-        count(3, last=True)
+        count(3)
         if t == 0:
+            act(A("thj"), ind(A("th64"), offs(O_ORD, 16)), ACT.Copy)
             act(A("iw"), A("ci"), ACT.Identity, scale=1.0 / 65536, bias=pf(S3))
         else:
+            for tile in range(4):
+                count(tile, 5, "bc", "bs")
             for b in range(4):
                 act(A("dw", C * b, C * b + C), bank(DB[b]), ACT.Copy)
-        spare(1)
-        ts(A("w1"), bank(3), pc(8), ALU.add)
-        spare(1)
-        copy(A("g32"), ind(A("w1"), offs(O_OWN, 2)))
-        spare(1)
-        turn(A("lt"), A("g32"))
-        spare(1)
-        copy(A("ga"), ind(A("lt"), offs(O_G, 8)))
-        spare(1)
-        tt(A("bf"), ind(A("lt"), offs(O_GP, 8)), A("ga"), ALU.is_lt)
-        spare(1)
-        scan(A("oo"), A("rst8"), A("bf"), ALU.mult, ALU.add)
-        scan(A("o2"), A("rst8"), A("bf"), ALU.mult, ALU.add)
-        spare(1)
-        tt(A("dd", 0, 16), ind(A("oo"), offs(O_PREV, 1)), A("o2", 7, 128, 8), ALU.subtract)
-        act(A("rs%d" % t), ind(A("dd"), offs(O_EXP, 4)), ACT.Exp, scale=-math.log(2.0))
+        spare(4, later)
+        for a in range(4):
+            turn(A("lt", p0=32 * a, p1=32 * a + 32), A("ps", 512 * 3 + a, 512 * 3 + C, 4, 32 * a, 32 * a + 32))
+        spare(2, later)
+        if t == 0:
+            for tile in range(4):
+                count(tile, 5, "bc", "bs")
+        tt(A("bf"), ind(A("lt"), offs(O_ORD, 16)), A("thj"), ALU.is_gt)
+        spare(2, later)
+        scan(A("oo", 0, C), A("rr"), A("bf"), ALU.mult, ALU.add)
+        act(A("rs%d" % t), ind(A("oo"), offs(O_EXP, 4)), ACT.Exp, scale=math.log(2.0) / 2)
         send(donor, v(A("rl%d" % t)), v(A("rs%d" % t)), A("rs%d" % t), "ra%d" % t)
         arrive([A("rl%d" % t)], "ra%d" % t, 1)
         if t == 0:
-            for b in range(4):
-                act(A("dw", C * b, C * b + C), bank(DB[b]), ACT.Copy)
-            spare(4)
-            tt(A("w2"), A("iw"), bank(3), ALU.add)
+            spare(2, later)
+            tt(A("w2"), A("iw"), bank(5), ALU.add)
+            spare(1, later)
+            spare(1, latest)
             for step in range(4):
                 candidates(0, step)
-                spare(1)
                 spare(1, latest)
+            for b in range(4):
+                act(A("dw", C * b, C * b + C), bank(DB[b]), ACT.Copy)
             copy(A("gk"), ind(A("w2"), A("cand", 0, 16)))
-            spare(1, latest)
+            spare(3, latest)
         else:
-            tt(A("w2"), A("iw"), bank(3), ALU.add)
+            tt(A("w2"), A("iw"), bank(5), ALU.add)
             copy(A("gk", 0, HC), ind(A("w2"), A("cand", 16 * t, 16 * t + 8)))
             act(A("gk", HC, C), ind(A("w2"), A("cand", 16 * t + 8, 16 * t + 16)), ACT.Copy)
         turn(A("kt"), A("gk"))
+        spare(3, latest)
         act(A("kf"), ind(A("kt"), offs(O_KF, 8)), ACT.Copy)
         ts(A("f1"), A("kt"), 192.0 / 256, ALU.is_lt)
+        spare(3, latest)
         for k in range(4):
             scan(A("uu", 64 * k, 64 * k + 64), A("rl%d" % t), A("f1", 64 * k, 64 * k + 64), ALU.mult, ALU.add)
         ts(A("nb", 0, 64), ind(A("uu"), offs(O_NK, 4)), 0.5, ALU.mult, 128.5 + 2.0 ** -9, ALU.add)
@@ -548,12 +555,11 @@ def rank_program(g, core, T, topo):
             for step in range(4):
                 candidates(t + 1, step)
         else:
-            copy(A("eo"), A("et"))
+            copy(A("eb"), A("ea", 0, 64, 4))
             quant(A("vc"), A("vs"), A("vin"))
-            act(A("eg"), ind(A("ci"), A("eo")), ACT.Copy)
-            act(A("eb"), A("eg", 0, 1024, 4), ACT.Copy)
-            for k in range(8):
-                dma("Y", "dout", T.el[k:k + 1, :], T.eb[16 * k:16 * k + 1, :], [], [A("eb")])
+            for n in range(2):
+                for s in range(2):
+                    dma("Y", "dout", T.el[s:8:2, HC * n:HC * n + HC], T.eb[:, 8 * n + 4 * s:8 * n + 4 * s + 4], [], [A("eb")])
     tc, tsc = "tc%d" % R, "ts%d" % R
     for h in range(2):
         for part in "pvsq":

@@ -4,26 +4,30 @@ from concourse.mybir import dt, AluOpType as ALU, ActivationFunctionType as ACT
 C, R, N, HC = 256, 3, 8, 128
 F32, BF, I32, U16, CODE, U8 = "float32", "bfloat16", "int32", "uint16", "float8_e4m3fn_x4", "uint8"
 _SIZES = {
-    BF: dict(xin=1024, uin=512, vin=512, ones=528, ebig=528, gi=136, bt=544, yi=128, thr=128, mi=64, da=256, sg=2048, pa=160, x1=160, x2=160,
-             x3=132, bd=528, ex=256, rr=256, th64=64, thj=256, bf=256, oo=272, fl=4096, f1=256, nb=128, dw=1024, zt=1024, ht=1024, xt=1024),
-    F32: dict(pf=16, pc=16, pat=64, ci=256, iw=256, mk=64, cm=192, c2=96, c1=48, big8=128, ta=256, tb=256, w2=256, zi=32, zt32=32,
-              lt=64, uu=256, gk=256, kt=256, kf=128, sc=128, ms=128, cp=64, eb=16, yb=256),
-    I32: dict(cdr=384, pi=1, pb=16, ui=16, pb1=160, pbm=160, oi=8, oj=8, dg=64, ea=64, et=64),
-    U16: dict(off=64, uo=16, cand=48, zo=64),
-    CODE: dict(uc=128, upc=256, vc=128, wq=512, ec=512, bc=256, dc=256, fc=1024, zc=256),
-    U8: dict(us=128, ups=256, vs=128, wp=512, es=512, bs=256, ds=256, fs=1024, zs=256),
+    BF: dict(xin=1024, uin=512, vin=512, ones=528, ebig=528, gi=136, bt=544, yi=128, thr=128, mi=64, sd=256, sg=2048, pa=160, x1=160, x2=160,
+             x3=132, bd=528, ex=128, rr=128, th32=32, thj=128, bf=256, oo=288, fl=4096, f1=256, nb=256, dw=1024, zt=1024, ht=1024, xt=1024),
+    F32: dict(pf=16, pc=16, pat=48, ci=256, iw=256, mk=64, cm=192, c2=96, c1=48, tm=256, w2=256, zi=32, zt32=32,
+              lt=64, uu=272, gk=256, kt=256, kf=256, ms=256, cp=64, eb=16, yb=256),
+    I32: dict(cdr=384, pi=1, pb=16, ui=24, pb1=160, pbm=160, oi=8, oj=8, dg=64, ea=64, et=64),
+    U16: dict(off=48, uo=24, cand=48, zo=64),
+    CODE: dict(uc=128, upc=384, vc=128, wq=512, ec=512, bc=256, dc=256, fc=1024, zc=256),
+    U8: dict(us=128, ups=384, vs=128, wp=512, es=512, bs=256, ds=256, fs=1024, zs=256),
 }
 SCRATCH = {"ps": ("psum", [128, 4096], F32)}
 for _d, _b in _SIZES.items():
     for _k, _n in _b.items():
         SCRATCH[_k] = ("sbuf", [128, _n], _d)
 for _t in range(R + 1):
-    for _k, _n, _d in (("tc", C, CODE), ("ts", C, U8), ("rs", 64, BF), ("rl", 64, BF), ("hc", C, CODE), ("hs", C, U8), ("lc", C, CODE), ("ls", C, U8)):
+    for _k, _n, _d in (("tc", C, CODE), ("ts", C, U8), ("rs", 96, BF), ("rl", 96, BF), ("hc", C, CODE), ("hs", C, U8), ("lc", C, CODE), ("ls", C, U8)):
         if _t < R or _k[0] == "t":
             SCRATCH["%s%d" % (_k, _t)] = ("sbuf", [128, _n], _d)
 
 SEMAPHORES = ["V", "S", "P", "G", "dx0", "dx1", "du", "dcd", "dw", "dv", "dout", "sent"] + \
-    ["ra%d" % t for t in range(R)] + ["ha%d_%d" % (t, h) for t in range(R) for h in range(2)]
+    ["%s%d_%d" % (k, t, h) for k in ("ra", "ha") for t in range(R) for h in range(2)]
+
+CYCLE, COLUMN, WAKE, CALL, HOP, LOAD = 0.0009, 0.0006, 0.19, 0.4, 1.25, 1.9
+RATIOS = ((0, 32), (32, 96))
+ON_VECTOR = dict(state=(0, 1), late_state=(0, 1), below=(3, 4), above=())
 
 
 def A(name, c0=0, c1=None, step=1, p0=0, p1=128):
@@ -32,34 +36,104 @@ def A(name, c0=0, c1=None, step=1, p0=0, p1=128):
     return (name, p0, p1, c0, c1, step)
 
 
-def bank(k, c0=0, c1=C):
+def bank(k, c0=0, c1=HC):
     return A("ps", 512 * k + c0, 512 * k + c1)
 
 
 def _meet(a, b):
     if a[2] <= b[1] or b[2] <= a[1] or a[4] <= b[3] or b[4] <= a[3]:
         return False
-    if a[5] == b[5] and a[5] > 1:
-        return (a[3] - b[3]) % a[5] == 0
-    return True
+    return (a[3] - b[3]) % math.gcd(a[5], b[5]) == 0
 
 
-def _emit(g, T, ops):
-    queues = {"V": g.vector, "S": g.scalar, "P": g.tensor, "G": g, "Y": g.sync}
-    deps, seen = [], {}
+def _width(a):
+    return 16 * (a[2][4] - a[2][3]) if a[0] == "ind" else len(range(a[3], a[4], a[5]))
+
+
+def _length(out, ins, twice=False):
+    if any(a[0] == "ind" for a in ins):
+        return 0.06 + 1.5 * CYCLE * _width(out)
+    narrow = all(SCRATCH[a[0]][2] in (BF, U16) for a in [out] + ins)
+    return CYCLE * max(64, _width(out) * (0.5 if narrow else 1) * (2 if twice else 1))
+
+
+def _touch(ops):
+    deps, behind, seen = [], [], {}
     for i, o in enumerate(ops):
-        d = set()
+        d, k = set(), set()
         mine = [(a, False) for a in o["r"]] + [(a, True) for a in o["w"]]
         for a, wa in mine:
             for j, b, wb in seen.get(a[0], []):
                 if a[0] == "ps":
-                    if a[3] // 512 == b[3] // 512 and (o["q"] != ops[j]["q"] or (o["q"] != "P" and (wa or wb))):
-                        d.add(j)
+                    if a[3] // 512 == b[3] // 512:
+                        if o["q"] != ops[j]["q"]:
+                            d.add(j)
+                        elif o["q"] == "P":
+                            k.add(j)
                 elif (wa or wb) and _meet(a, b):
                     d.add(j)
         for a, wa in mine:
             seen.setdefault(a[0], []).append((i, a, wa))
         deps.append(d)
+        behind.append(k)
+    return deps, behind
+
+
+def _arrange(ops):
+    deps, behind = _touch(ops)
+    last = {}
+    for i, o in enumerate(ops):
+        if o["q"] is None:
+            behind[i] |= set(j for j in range(i) if ops[j].get("to") == o["sem"])
+        elif o.get("dma") or "to" in o:
+            if o["q"] in last:
+                behind[i].add(last[o["q"]])
+            last[o["q"]] = i
+    after = [[] for _ in ops]
+    for i in range(len(ops)):
+        for j in deps[i] | behind[i]:
+            after[j].append(i)
+    chain = [0.0] * len(ops)
+    for i in range(len(ops) - 1, -1, -1):
+        chain[i] = ops[i]["c"] + ops[i].get("lag", 0.0) + max([chain[k] + (WAKE if i in deps[k] else 0.0) for k in after[i]] + [0.0])
+    left = [len(deps[i] | behind[i]) for i in range(len(ops))]
+    ready, start, end = {}, {}, {}
+    free = dict.fromkeys("VSPGY", 0.0)
+    pool = [i for i in range(len(ops)) if left[i] == 0]
+    for i in pool:
+        ready[i] = 0.0
+
+    def run(i, at):
+        start[i], end[i] = at, at + ops[i]["c"] + ops[i].get("lag", 0.0)
+        pool.remove(i)
+        for k in after[i]:
+            left[k] -= 1
+            if left[k] == 0:
+                ready[k] = max([end[j] + WAKE for j in deps[k]] + [start[j] + ops[j]["c"] for j in behind[k]])
+                pool.append(k)
+
+    while pool:
+        for i in [i for i in pool if ops[i]["q"] is None]:
+            run(i, ready[i])
+        if not pool:
+            break
+        q = min(set(ops[i]["q"] for i in pool), key=lambda q: (max(free[q], min(ready[i] for i in pool if ops[i]["q"] == q)), q))
+        mine = [i for i in pool if ops[i]["q"] == q]
+        now = max(free[q], min(ready[i] for i in mine))
+        best = max(mine, key=lambda i: (chain[i] - max(0.0, ready[i] - now), -i))
+        if ready[best] > now:
+            fits = [i for i in mine if max(ready[i], now) + ops[i]["c"] <= ready[best] + 0.03]
+            if fits:
+                best = max(fits, key=lambda i: (chain[i], -i))
+        at = max(now, ready[best])
+        free[q] = at + ops[best]["c"]
+        run(best, at)
+    return [ops[i] for i in sorted(range(len(ops)), key=lambda i: (start[i], i))]
+
+
+def _emit(g, T, ops):
+    queues = {"V": g.vector, "S": g.scalar, "P": g.tensor, "G": g, "Y": g.sync}
+    deps = _touch(ops)[0]
     clock, known, need = [None] * len(ops), {q: {} for q in queues}, []
     for i, o in enumerate(ops):
         waits = []
@@ -124,51 +198,62 @@ def rank_program(g, core, T, topo):
     def ind(win, offs):
         return ("ind", win, offs)
 
-    def op(q, f, w, r, **more):
+    def op(q, f, c, w, r, **more):
         reads = []
         for a in r:
             if isinstance(a, tuple):
                 reads += [a[1], a[2]] if a[0] == "ind" else [a]
-        ops.append(dict(q=q, f=f, w=list(w), r=reads, **more))
+        ops.append(dict(q=q, f=f, c=c, w=list(w), r=reads, **more))
 
     def copy(out, in_):
-        op("V", lambda q: q.tensor_copy(v(out), v(in_)), [out], [in_])
+        op("V", lambda q: q.tensor_copy(v(out), v(in_)), _length(out, [in_]), [out], [in_])
 
     def tt(out, a, b, o):
-        op("V", lambda q: q.tensor_tensor(v(out), v(a), v(b), o), [out], [a, b])
+        op("V", lambda q: q.tensor_tensor(v(out), v(a), v(b), o), _length(out, [a, b], b[0] != "ps"), [out], [a, b])
 
     def ts(out, a, s1, o1, s2=None, o2=None):
         if o2 is None:
-            op("V", lambda q: q.tensor_scalar(v(out), v(a), v(s1), None, o1), [out], [a, s1])
+            op("V", lambda q: q.tensor_scalar(v(out), v(a), v(s1), None, o1), _length(out, [a]), [out], [a, s1])
         else:
-            op("V", lambda q: q.tensor_scalar(v(out), v(a), v(s1), v(s2), o1, o2), [out], [a, s1, s2])
+            op("V", lambda q: q.tensor_scalar(v(out), v(a), v(s1), v(s2), o1, o2), _length(out, [a]), [out], [a, s1, s2])
 
     def scan(out, d0, d1, o0, o1):
-        op("V", lambda q: q.tensor_tensor_scan(v(out), v(d0), v(d1), 0.0, o0, o1), [out], [d0, d1])
+        op("V", lambda q: q.tensor_tensor_scan(v(out), v(d0), v(d1), 0.0, o0, o1), _length(out, [d0, d1]), [out], [d0, d1])
 
     def turn(out, in_):
-        op("V", lambda q: q.transpose(v(out), v(in_)), [out], [in_])
+        op("V", lambda q: q.transpose(v(out), v(in_)), _length(out, [in_]), [out], [in_])
 
     def fill(out, c):
-        op("V", lambda q: q.memset(v(out), c), [out], [])
+        op("V", lambda q: q.memset(v(out), c), _length(out, []), [out], [])
 
     def quant(c, s, in_):
-        op("V", lambda q: q.quantize_mx(v(c), v(s), v(in_)), [c, s], [in_])
+        op("V", lambda q: q.quantize_mx(v(c), v(s), v(in_)), 0.012 + 0.27 * CYCLE * _width(in_), [c, s], [in_])
 
-    def act(out, in_, f, **kw):
-        op("S", lambda q: q.activation(v(out), v(in_), f, **{k: v(x) for k, x in kw.items()}), [out], [in_] + list(kw.values()))
+    def act(out, in_, f, more=0.0, **kw):
+        c = _length(out, [in_]) if in_[0] == "ind" else CYCLE * max(64, _width(out))
+        op("S", lambda q: q.activation(v(out), v(in_), f, **{k: v(x) for k, x in kw.items()}), c + more, [out], [in_] + list(kw.values()))
+
+    def move(on_vector, out, in_):
+        if on_vector:
+            copy(out, in_)
+        else:
+            act(out, in_, ACT.Copy)
 
     def mm(out, lc, ls, rc, rs, start=True, stop=True):
-        op("P", lambda q: q.matmul_mx(v(out), v(lc), v(ls), v(rc), v(rs), start, stop), [out], [lc, ls, rc, rs])
+        op("P", lambda q: q.matmul_mx(v(out), v(lc), v(ls), v(rc), v(rs), start, stop), COLUMN * (_width(out) + 16), [out], [lc, ls, rc, rs])
 
     def iota(out, pattern, base=0, cm=0):
+        c = 0.13 + 2 * CYCLE * _width(out)
         if SCRATCH[out[0]][2] == I32:
-            op("G", lambda q: q.iota(v(out), pattern, base, cm), [out], [])
+            op("G", lambda q: q.iota(v(out), pattern, base, cm), c, [out], [])
         else:
-            op("G", lambda q: q.iota(v(out), pattern, base, cm, allow_small_or_imprecise_dtypes=True), [out], [])
+            op("G", lambda q: q.iota(v(out), pattern, base, cm, allow_small_or_imprecise_dtypes=True), c, [out], [])
+
+    def select(out, in_, pattern, o, base, cm):
+        op("G", lambda q: q.affine_select(v(out), v(in_), pattern, o, 0.0, base, cm), 0.17 + 2 * CYCLE * _width(out), [out], [in_])
 
     def dma(q, sem, out, in_, w, r):
-        op(q, lambda e: e.dma_start(out, in_), w, r, sem=sem, n=16, dma=True)
+        op(q, lambda e: e.dma_start(out, in_), 0.05, w, r, sem=sem, n=16, dma=True, lag=LOAD - 0.2)
 
     def raw(a):
         return v(a).bitcast(dt.uint8)
@@ -181,10 +266,10 @@ def rank_program(g, core, T, topo):
 
     def send(dst, out, in_, src, sem):
         rid, pid = topo.addr(dst, core)
-        op("G", lambda q: q.remote_dma(out, in_, T.sem[sem], T.sem.sent, pid, rid, mask), [], [src], sem="sent", n=nen)
+        op("G", lambda q: q.remote_dma(out, in_, T.sem[sem], T.sem.sent, pid, rid, mask), CALL, [], [src], sem="sent", n=nen, to=sem)
 
     def arrive(views, sem, calls):
-        op(None, None, views, [], sem=sem, n=nen * calls)
+        op(None, None, HOP, views, [], sem=sem, n=nen * calls)
 
     def pair(c, s, c0=0, c1=C):
         return A(c, c0, c1), A(s, c0, c1)
@@ -218,358 +303,245 @@ def rank_program(g, core, T, topo):
     dma("Y", "dw", T.wp[:, :], T.ws[:, :], [A("wp")], [])
     dma("Y", "dv", T.vin[:, :], T.v[:, :], [A("vin")], [])
 
-    O_DIAG, O_ORD, O_EXP, O_NK, O_KF, O_DUP, O_CD = 0, 8, 24, 28, 36, 44, 48
-    S7, S3, N4, BA, S15, B3, SA, X31 = range(8)
+    O_DIAG, O_ORD, O_EXP, O_NK, O_KF, O_UP, O_DUP, O_CD = 0, 8, 16, 20, 24, 28, 32, 34
+    BA, X31, S7, S15, S3, N4, B3, SA = range(8)
     iota(A("pi"), [[0, 1]], 0, 1)
-    iota(A("ui"), [[16, 2], [32, 4], [0, 2]])
+    for col, sh, keep in ((BA, 5, 3), (X31, 0, 31), (S7, 0, 7), (S15, 0, 15), (S3, 3, 1), (N4, 4, 1), (B3, 0, 3), (SA, 2, 3)):
+        ts(pb(col), A("pi"), sh, ALU.logical_shift_right, keep, ALU.bitwise_and)
+    copy(A("pf", 0, 4), A("pb", 0, 4))
+    copy(A("pf", 4, 8), A("pb", 4, 8))
+    ts(pc(5), pf(BA), 2.0, ALU.mult, 1.0, ALU.add)
+    iota(A("ui", 0, 8), [[16, 8]])
+    iota(A("ui", 8, 24), [[16, 2], [32, 4], [0, 2]])
+    copy(A("uo"), A("ui"))
+    quant(A("uc"), A("us"), A("uin"))
+    for c0, c1 in ((0, HC), (HC, 3 * HC)):
+        o, w, lst = A("upc", c0, c1), A("uc"), A("uo", c0 // 16, c1 // 16)
+        act(A("ups", c0, c1), ind(A("us"), lst), ACT.Copy)
+        op("V", lambda q, o=o, w=w, lst=lst: q.tensor_copy(v(o).bitcast(dt.uint32), v(w).bitcast(dt.uint32).indirect(v(lst))),
+           _length(o, [ind(w, lst)]), [o], [w, lst])
+    iota(A("yi"), [[0, 4], [1, 32]])
+    ts(A("thr"), A("yi"), pf(X31), ALU.is_gt, -2.0 ** -120, ALU.mult)
+    iota(pat(O_DIAG, 8), [[HC + 32, 4], [16, 2]])
+    ts(offs(O_DIAG, 8), pat(O_DIAG, 8), pf(S15), ALU.add)
     iota(A("pb1"), [[0, 5], [1, 8], [1, 4]], 1)
     iota(A("pa"), [[0, 5], [1, 8], [0, 4]])
-    iota(A("yi"), [[0, 4], [1, 32]])
-    iota(pat(O_DIAG, 8), [[C + 32, 4], [16, 2]])
+    ts(A("pbm"), A("pb1"), 7, ALU.bitwise_and)
+    ts(A("x2"), A("pbm"), pc(5), ALU.is_equal)
+    ts(A("x1"), A("pa"), pc(5), ALU.is_equal)
+    tt(A("x3"), A("x1", 0, 132), A("x2", 0, 132), ALU.subtract)
+    iota(A("gi"), [[0, 17], [1, 8]])
+    for k in range(4):
+        act(A("bd", k, 528, 4), A("x3"), ACT.Copy)
+        ts(A("bt", k, 544, 4), A("gi"), pc(5), ALU.is_equal, 1.0 / 256, ALU.mult)
+    for odd in range(2):
+        quant(*half("dc", "ds", odd), A("bd", 16 - 16 * odd, 528 - 16 * odd))
+        quant(*half("bc", "bs", odd), A("bt", 4 - 4 * odd, 516 - 4 * odd))
     iota(A("zi"), [[0, 2], [20, 4], [-3, 4]], 28)
     iota(A("zi", 4, 12), [[1, 8]], 28)
     iota(A("zi", 20, 28), [[1, 8]], 28)
-    iota(pat(O_ORD, 8), [[4, 8]])
-    iota(pat(O_EXP, 4), [[0, 2], [128, 2]], 15)
-    iota(A("gi"), [[0, 17], [1, 8]])
+    turn(A("zt32"), A("zi"))
+    ts(A("oi"), A("pa", 0, 32, 4), 4.0, ALU.mult, A("zt32", 0, 1), ALU.add)
+    ts(A("oj"), A("oi"), 31, ALU.bitwise_and)
+    copy(offs(O_ORD, 8), A("oj"))
+    ts(A("th32"), A("pb1", 0, 32), 8.0, ALU.is_lt, 0.5, ALU.subtract)
+    act(A("thj"), ind(A("th32"), offs(O_ORD, 8)), ACT.Copy)
     fill(A("ex"), 0.0)
-    fill(A("ex", 0, C, 4), -1.0)
-    fill(A("ex", 3, C, 4), 1.0)
-    act(A("rr"), A("ex"), ACT.Exp, scale=math.log(2.0))
-    for col, sh, bits in ((BA, 5, 3), (X31, 0, 31), (S7, 0, 7), (S15, 0, 15), (S3, 3, 1), (N4, 4, 1), (B3, 0, 3), (SA, 2, 3)):
-        ts(pb(col), A("pi"), sh, ALU.logical_shift_right, bits, ALU.bitwise_and)
-    copy(A("uo"), A("ui"))
-    copy(A("pf", 0, 8), A("pb", 0, 8))
+    fill(A("ex", 3, HC, 4), 1.0)
+    fill(A("ex", 4, HC, 8), -1.0)
+    fill(A("ex", 0, HC, 16), -200.0)
+    act(A("rr"), A("ex"), ACT.Exp, more=1.4, scale=math.log(2.0))
+    fill(A("rr", 8, HC, 16), -0.5)
+    fill(A("oo", HC, 288, 144), -400.0)
+    ts(pc(2), pf(S15), 0.0, ALU.is_equal, float(HC - 15), ALU.mult)
+    ts(pc(12), pf(S7), 16.0, ALU.mult, pc(2), ALU.add)
+    ts(offs(O_EXP, 4), A("pa", 0, 4), pc(12), ALU.add, 15.0, ALU.add)
     fill(A("ones"), 1.0)
-    op("G", lambda q: q.affine_select(v(A("ebig")), v(A("ones")), [[-1, 528]], ALU.is_equal, 0.0, 3, 4), [A("ebig")], [A("ones")])
-    iota(A("ci"), [[1, 256]])
-    iota(A("mi"), [[0, 16], [1, 4]])
-    iota(pat(O_NK, 8), [[16, 2], [2, 4]])
-    iota(pat(O_DUP, 4), [[8, 2], [1, 2]])
-    iota(pat(O_CD, 12), [[32, 12]])
-    ts(pc(5), pf(BA), 2.0, ALU.mult, 1.0, ALU.add)
-    ts(A("pbm"), A("pb1"), 7, ALU.bitwise_and)
-    fill(A("oo", C, C + 16), -400.0)
-    ts(pc(2), pf(S15), 0.0, ALU.is_equal, 1000.0, ALU.mult)
-    ts(A("x1"), A("pa"), pc(5), ALU.is_equal)
-    ts(A("x2"), A("pbm"), pc(5), ALU.is_equal)
-    ts(A("thr"), A("yi"), pf(X31), ALU.is_gt, -2.0 ** -120, ALU.mult)
-    ts(offs(O_DIAG, 8), pat(O_DIAG, 8), pf(S15), ALU.add)
-    quant(A("uc"), A("us"), A("uin"))
-    quant(*half("tc0", "ts0", 0), A("xin", 0, 512))
-    act(A("ups"), ind(A("us"), A("uo")), ACT.Copy)
-    op("V", lambda q: q.tensor_copy(T.upc[:, :].bitcast(dt.uint32), T.uc[:, :].bitcast(dt.uint32).indirect(T.uo[:, :])), [A("upc")], [A("uc"), A("uo")])
-    quant(*half("tc0", "ts0", 1), A("xin", 512, 1024))
-    tt(A("x3"), A("x1", 0, 132), A("x2", 0, 132), ALU.subtract)
-    for k in range(4):
-        act(A("bd", k, 528, 4), A("x3"), ACT.Copy)
+    select(A("ebig"), A("ones"), [[-1, 528]], ALU.is_equal, 3, 4)
 
     def e_(b):
         return pair("ec", "es", 128 * b, 128 * b + 128)
 
-    DB = (0, 1, 2, 7)
-
-    def unit(b):
+    for b in range(4):
         quant(*e_(b), A("ebig", 3 - b, 515 - b))
-        mm(bank(DB[b]), *e_(b), *pair("tc0", "ts0"))
+    iota(A("ci"), [[1, 256]])
+    act(A("iw"), A("ci"), ACT.Identity, scale=1.0 / 65536, bias=pf(S3))
+    iota(A("mi"), [[0, 16], [1, 4]])
+    ts(A("mk"), A("mi"), pf(SA), ALU.is_equal)
+    iota(pat(O_CD, 12), [[128, 3], [8, 2], [64, 2]])
+    ts(pc(3), pf(S3), 32.0, ALU.mult, pf(S7), ALU.add)
+    ts(pc(10), pf(N4), 16.0, ALU.mult, pc(3), ALU.add)
+    ts(offs(O_CD, 12), pat(O_CD, 12), pc(10), ALU.add)
+    iota(pat(O_NK, 4), [[2, 4]])
+    ts(pc(1), pf(S7), 16.0, ALU.mult, pf(S3), ALU.add)
+    ts(offs(O_NK, 4), pat(O_NK, 4), pc(1), ALU.add, 8.0, ALU.add)
+    ts(offs(O_KF, 4), pat(O_NK, 4), pc(1), ALU.add)
+    ts(pc(14), pf(S7), 0.0, ALU.is_equal, 1000.0, ALU.mult)
+    ts(offs(O_UP, 4), offs(O_NK, 4), pc(14), ALU.add, float(HC), ALU.min)
+    fill(A("kf", 1, C, 2), 1000.0)
+    fill(A("uu", HC, 272, 136), 4000.0)
+    iota(pat(O_DUP, 2), [[1, 2]])
+    ts(pb(9), pf(SA), pf(BA), ALU.subtract, 4.0, ALU.add)
+    ts(pb(11), pb(9), 3, ALU.bitwise_and)
+    ts(pc(4), pf(BA), 2.0, ALU.mult)
+    ts(pc(13), pb(11), 8.0, ALU.mult, pc(4), ALU.add)
+    ts(offs(O_DUP, 2), pat(O_DUP, 2), pc(13), ALU.add)
+    ts(pc(6), pf(B3), 256.0, ALU.mult)
+    quant(A("vc"), A("vs"), A("vin"))
+    for t in range(R):
+        tt(A("cm", 64 * t, 64 * t + 64), ind(A("cdr"), offs(O_CD + 4 * t, 4)), A("mk"), ALU.mult)
+        tt(A("c2", 32 * t, 32 * t + 32), A("cm", 64 * t, 64 * t + 64, 2), A("cm", 64 * t + 1, 64 * t + 64, 2), ALU.add)
+        tt(A("c1", 16 * t, 16 * t + 16), A("c2", 32 * t, 32 * t + 32, 2), A("c2", 32 * t + 1, 32 * t + 32, 2), ALU.add)
+        copy(A("cand", 16 * t, 16 * t + 16), A("c1", 16 * t, 16 * t + 16))
 
-    def table(k):
-        ts(A("bt", k, 544, 4), A("gi"), pc(5), ALU.is_equal, 1.0 / 256, ALU.mult)
+    MIXED, EVEN, ODD = range(3)
+    UNPACKED = (7, 0, 2, 1)
 
-    soon = [lambda: quant(*pair("dc", "ds", 0, 128), A("bd", 16, 528)),
-            lambda: quant(*pair("dc", "ds", 128, 256), A("bd", 0, 512)),
-            lambda: turn(A("zt32"), A("zi")),
-            lambda: ts(pc(12), pf(S7), 16.0, ALU.mult, pc(2), ALU.add),
-            lambda: ts(A("th64"), A("pb1", 0, 64), 8.0, ALU.is_lt, 0.5, ALU.subtract),
-            lambda: ts(A("oi"), pat(O_ORD, 8), A("zt32", 0, 1), ALU.add),
-            lambda: ts(offs(O_EXP, 4), pat(O_EXP, 4), pc(12), ALU.add, float(C), ALU.min),
-            lambda: ts(A("oj"), A("oi"), 31, ALU.bitwise_and),
-            lambda: fill(A("rr", 0, C, 16), 0.0),
-            lambda: fill(A("rr", 8, C, 16), -0.5),
-            lambda: copy(offs(O_ORD, 8), A("oj")),
-            lambda: ts(offs(O_ORD + 8, 8), A("oj"), 32.0, ALU.add)]
-    later = [lambda: table(0), lambda: table(1), lambda: table(2), lambda: table(3),
-             lambda: quant(*pair("bc", "bs", 0, 128), A("bt", 4, 516)),
-             lambda: quant(*pair("bc", "bs", 128, 256), A("bt", 0, 512)),
-             lambda: ts(pc(3), pf(S3), 16.0, ALU.mult, pf(S7), ALU.add),
-             lambda: ts(pc(1), pf(S7), 32.0, ALU.mult, pf(S3), ALU.add),
-             lambda: ts(A("mk"), A("mi"), pf(SA), ALU.is_equal),
-             lambda: ts(pc(10), pf(N4), 8.0, ALU.mult, pc(3), ALU.add),
-             lambda: ts(offs(O_CD, 12), pat(O_CD, 12), pc(10), ALU.add)]
-    latest = [lambda: unit(0), lambda: unit(1), lambda: unit(2), lambda: unit(3),
-              lambda: ts(pb(9), pf(SA), pf(BA), ALU.subtract, 4.0, ALU.add),
-              lambda: ts(offs(O_NK, 8), pat(O_NK, 8), pc(1), ALU.add, 8.0, ALU.add),
-              lambda: ts(offs(O_KF, 8), pat(O_NK, 8), pc(1), ALU.add),
-              lambda: ts(pb(11), pb(9), 3, ALU.bitwise_and),
-              lambda: ts(pc(4), pf(BA), 2.0, ALU.mult),
-              lambda: ts(pc(6), pf(B3), 256.0, ALU.mult),
-              lambda: fill(A("big8"), 0.0),
-              lambda: ts(pc(13), pb(11), 16.0, ALU.mult, pc(4), ALU.add),
-              lambda: fill(A("big8", 0, 128, 8), 1000.0),
-              lambda: ts(offs(O_DUP, 4), pat(O_DUP, 4), pc(13), ALU.add)]
+    def slot(tile, k, c0, c1):
+        return A("fl", 1024 * tile + 4 * c0 + k, 1024 * tile + 4 * c1, 4)
 
-    def spare(k, todo):
-        for _ in range(k):
-            if todo:
-                todo.pop(0)()
+    def place(odd, s, c0, c1):
+        return slot(2 * odd, s, c0, c1) if s < 3 else slot(2 * odd + 1, s - 3, c0, c1)
 
-    def candidates(t, step):
-        if step == 0:
-            tt(A("cm", 64 * t, 64 * t + 64), ind(A("cdr"), offs(O_CD + 4 * t, 4)), A("mk"), ALU.mult)
-        elif step == 1:
-            tt(A("c2", 32 * t, 32 * t + 32), A("cm", 64 * t, 64 * t + 64, 2), A("cm", 64 * t + 1, 64 * t + 64, 2), ALU.add)
-        elif step == 2:
-            tt(A("c1", 16 * t, 16 * t + 16), A("c2", 32 * t, 32 * t + 32, 2), A("c2", 32 * t + 1, 32 * t + 32, 2), ALU.add)
-        else:
-            copy(A("cand", 16 * t, 16 * t + 16), A("c1", 16 * t, 16 * t + 16))
+    def own(b, odd):
+        return A("tm", 32 * b + 16 * odd, 32 * b + 16 * odd + 1)
 
-    def slot(tile, t, c0, c1):
-        return A("fl", 1024 * tile + 4 * c0 + t, 1024 * tile + 4 * c1, 4)
+    def signs(b, c0, c1):
+        at = 7 * HC * (c0 // HC) + HC * b
+        return A("sg", at + c0, at + c1)
 
-    def place(base, s, c0, c1):
-        return slot(base, s, c0, c1) if s < 3 else slot(base + 1, s - 3, c0, c1)
-
-    def pack(tile, c0, c1):
-        quant(*pair("fc", "fs", C * tile + c0, C * tile + c1), A("fl", 1024 * tile + 4 * c0, 1024 * tile + 4 * c1))
-
-    def count(tile, bk=3, c="dc", s="ds"):
-        b = 128 * (tile // 2)
-        mm(bank(bk), *pair(c, s, b, b + 128), *pair("fc", "fs", C * tile, C * tile + C), tile == 0, tile == 3)
-
-    def row(t, k, odd, c0, c1):
-        mm(bank(k, 0, c1 - c0), *half("upc", "ups", odd), *pair("tc%d" % t, "ts%d" % t, c0, c1))
-
-    def le_v(bk, s, c0, c1):
-        ts(place(0, s, c0, c1), bank(bk, c0, c1), A("ta", 32 * s, 32 * s + 1), ALU.is_le)
-
-    def lt_v(bk, s):
-        ts(place(0, s, 0, 32 * (s + 1)), bank(bk, 0, 32 * (s + 1)), A("ta", 32 * (s + 1), 32 * (s + 1) + 1), ALU.is_lt)
-
-    def sign(bk, b, c0, c1):
-        act(A("sg", C * b + c0, C * b + c1), bank(bk, c0, c1), ACT.Sign, scale=-1.0, bias=A("tb", 32 * b, 32 * b + 1))
-
-    def le_s(s, c0, c1):
-        act(place(2, s, c0, c1), A("sg", C * s + c0, C * s + c1), ACT.Sign, bias=1.0)
-
-    def lt_s(s, c0=0, c1=C):
-        c1 = min(c1, 32 * (s + 1))
-        act(place(2, s, c0, c1), A("sg", C * (s + 1) + c0, C * (s + 1) + c1), ACT.Relu)
-
-    def diagonal(h, bk, part):
-        c0, c1 = HC * h, HC * h + HC
-        if part == 0:
-            tt(A("da", c0, c1), A("ta", c0, c1), bank(bk, c0, c1), ALU.subtract)
-        elif part == 1:
-            tt(slot(0, 3, c0, c1), A("da", c0, c1), A("thr"), ALU.is_gt)
-        else:
-            w0 = (4 * C + HC) * h
-            tt(slot(2, 3, c0, c1), ind(A("sg", w0, w0 + 3 * C + HC), offs(O_DIAG, 8)), A("thr"), ALU.is_gt)
-
-    def new_state(t, h, part):
-        x0 = 512 * h
-        if t == 0:
-            return
-        if part == "p":
+    def state(t, h):
+        x0, c0, c1 = 512 * h, HC * h, HC * h + HC
+        mine = half("tc%d" % t, "ts%d" % t, h)
+        if t > 0:
             for b in (0, 2, 1, 3):
-                mm(bank(4 * h + b, 0, HC), *e_(b), *half("lc%d" % (t - 1), "ls%d" % (t - 1), h), False, True)
-        elif part == "v":
-            for b in (0, 1):
-                copy(A("xt", x0 + b, x0 + 512, 4), bank(4 * h + b, 0, HC))
-        elif part == "s":
-            for b in (2, 3):
-                act(A("xt", x0 + b, x0 + 512, 4), bank(4 * h + b, 0, HC), ACT.Copy)
-        else:
-            quant(*half("tc%d" % t, "ts%d" % t, h), A("xt", x0, x0 + 512))
+                mm(bank(4 * h + b), *e_(b), *half("lc%d" % (t - 1), "ls%d" % (t - 1), h), False, True)
+            for b in range(4):
+                move(b in ON_VECTOR["late_state" if h and t < R else "state"], A("xt", x0 + b, x0 + 512, 4), bank(4 * h + b))
+        quant(*mine, A("xt" if t else "xin", x0, x0 + 512))
+        if t < R:
+            for k, kind in ((1, MIXED), (2, ODD), (0, EVEN), (3, EVEN)):
+                mm(bank(4 * h + k), *half("upc", "ups", kind), *mine)
+            turn(A("tm", c0, c1), bank(4 * h + 1))
+
+    def compare(h, blocks):
+        c0, c1 = HC * h, HC * h + HC
+        for b in blocks:
+            act(signs(b, c0, c1), bank(4 * h + 2), ACT.Sign, scale=-1.0, bias=own(b, 1))
+        for b in blocks:
+            lo, hi = min(max(32 * b, c0), c1), min(max(32 * b + 32, c0), c1)
+            if lo < hi:
+                act(A("sd", lo, hi), bank(4 * h + 3, lo - c0, hi - c0), ACT.Sign, scale=-1.0, bias=own(b, 0))
+            if hi < c1:
+                ts(place(0, b, hi, c1), bank(4 * h, hi - c0, HC), own(b, 0), ALU.is_le)
+                if h == 1 and b in ON_VECTOR["above"]:
+                    ts(place(1, b, hi, c1), signs(b, hi, c1), 0.0, ALU.is_ge)
+                else:
+                    act(place(1, b, hi, c1), signs(b, hi, c1), ACT.Sign, bias=1.0)
+            if c0 < lo:
+                ts(place(0, b - 1, c0, lo), bank(4 * h, 0, lo - c0), own(b, 0), ALU.is_lt)
+                if h == 0 and b - 1 in ON_VECTOR["below"]:
+                    ts(place(1, b - 1, c0, lo), signs(b, c0, lo), 0.0, ALU.is_gt)
+                else:
+                    act(place(1, b - 1, c0, lo), signs(b, c0, lo), ACT.Relu)
+
+    def diagonal(h):
+        c0, c1 = HC * h, HC * h + HC
+        tt(slot(0, 3, c0, c1), A("sd", c0, c1), A("thr"), ALU.is_gt)
+        tt(slot(2, 3, c0, c1), ind(A("sg", 12 * HC * h, 12 * HC * h + 4 * HC), offs(O_DIAG, 8)), A("thr"), ALU.is_gt)
+
+    def count(h, tiles):
+        for tile in tiles:
+            c0 = C * tile + HC * h
+            quant(*pair("fc", "fs", c0, c0 + HC), A("fl", 4 * c0, 4 * c0 + 512))
+            mm(bank(4 * h + 1), *half("dc", "ds", tile // 2), *pair("fc", "fs", c0, c0 + HC), tile == 0, tile == 3)
+
+    def order(t, h, donor):
+        r0, r1 = RATIOS[h]
+        mine, theirs, at = A("rs%d" % t, r0, r1), A("rl%d" % t, r0, r1), 512 * (4 * h + 1)
+        for a in range(4):
+            turn(A("lt", 32 * h, 32 * h + 32, 1, 32 * a, 32 * a + 32), A("ps", at + a, at + HC, 4, 32 * a, 32 * a + 32))
+        tt(A("bf", HC * h, HC * h + HC), ind(A("lt", 32 * h, 32 * h + 32), offs(O_ORD, 8)), A("thj"), ALU.is_gt)
+        scan(A("oo", 144 * h, 144 * h + HC), A("rr"), A("bf", HC * h, HC * h + HC), ALU.mult, ALU.add)
+        act(mine, ind(A("oo", 144 * h, 144 * h + 144), offs(O_EXP, (r1 - r0) // 16)), ACT.Exp, scale=math.log(2.0) / 2)
+        send(donor, v(theirs), v(mine), mine, "ra%d_%d" % (t, h))
+        arrive([theirs], "ra%d_%d" % (t, h), 1)
+
+    def leaders(t, h):
+        c0, c1, u0, q0, q1 = HC * h, HC * h + HC, 136 * h, 32 * h, 32 * h + 32
+        r0, r1 = RATIOS[h]
+        move(h == 0, A("gk", c0, c1), ind(A("w2"), A("cand", 16 * t + 8 * h, 16 * t + 8 * h + 8)))
+        turn(A("kt", c0, c1), A("gk", c0, c1))
+        act(A("kf", c0, c1, 2), ind(A("kt", c0, c1), offs(O_KF, 4)), ACT.Copy)
+        ts(A("f1", c0, c1), A("kt", c0, c1), 192.0 / 256, ALU.is_lt)
+        for c in range(0, HC, r1 - r0):
+            scan(A("uu", u0 + c, u0 + c + r1 - r0), A("rl%d" % t, r0, r1), A("f1", c0 + c, c0 + c + r1 - r0), ALU.mult, ALU.add)
+        ts(A("nb", c0, c1, 2), ind(A("uu", u0, u0 + 136), offs(O_UP, 4)), 0.5, ALU.mult, 128.5 + 2.0 ** -9, ALU.add)
+        act(A("nb", c0 + 1, c1, 2), ind(A("uu", u0, u0 + 136), offs(O_NK, 4)), ACT.Identity, scale=-0.5, bias=-128.5 - 2.0 ** -9)
+        scan(A("ms", c0, c1), A("nb", c0, c1), A("kf", c0, c1), ALU.add, ALU.min)
+        select(A("cp", q0, q0 + 8), A("ms", c0 + 15, c1, 16), [[0, 8]], ALU.is_ge, 0, 0)
+        moves = [(2, 0, 64, 64), (2, 64, 0, 64)] + [(d, 32 * a, 32 * ((a + d) % 4), 32) for d in (1, 3) for a in range(4)]
+        for k, (d, to, fr, n) in enumerate(moves):
+            move(k % 2 == 0, A("cp", q0 + 8 * d, q0 + 8 * d + 8, 1, to, to + n), A("ms", c0 + 15, c1, 16, fr, fr + n))
+        ts(A("dg", q0, q1), ind(A("cp", q0, q1), offs(O_DUP, 2)), 65536.0, ALU.mult)
+        ts(A("ea", q0, q1), A("dg", q0, q1), C - 1, ALU.bitwise_and)
+        turn(A("et", q0, q1), A("ea", q0, q1))
+        ts(A("zo", q0, q1), A("et", q0, q1), pc(6), ALU.add)
+
+    def layer(t, h, child):
+        x0, q0 = 512 * h, 32 * h
+        hc, hs = half("hc%d" % t, "hs%d" % t, h)
+        lc, ls = half("lc%d" % t, "ls%d" % t, h)
+        for k in range(2):
+            move(k == 0, A("zt", x0 + C * k, x0 + C * k + C), ind(A("dw"), A("zo", q0 + 16 * k, q0 + 16 * k + 16)))
+        quant(*half("zc", "zs", h), A("zt", x0, x0 + 512))
+        for b in (0, 2, 1, 3):
+            mm(bank(4 * h + b), *pair("wq", "wp", 128 * b, 128 * b + 128), *half("zc", "zs", h))
+        for b in (0, 1):
+            ts(A("ht", x0 + b, x0 + 512, 4), bank(4 * h + b), 0.0, ALU.max, 0.015625, ALU.mult)
+            act(A("ht", x0 + b + 2, x0 + 512, 4), bank(4 * h + b + 2), ACT.Relu, scale=0.015625)
+        quant(hc, hs, A("ht", x0, x0 + 512))
+        send(child, raw(lc), raw(hc), hc, "ha%d_%d" % (t, h))
+        send(child, v(ls), v(hs), hs, "ha%d_%d" % (t, h))
+        arrive([lc, ls], "ha%d_%d" % (t, h), 2)
+        for b in range(4):
+            mm(bank(4 * h + b), *e_(b), *half("tc%d" % t, "ts%d" % t, h), True, False)
 
     for t in range(R):
         donor, child = T.cores[(rank + 1 + t) % N], T.cores[(rank - 1 - t) % N]
-        tc, tsc = "tc%d" % t, "ts%d" % t
-        for part in "pvsq":
-            new_state(t, 0, part)
-        row(t, 1, 1, 0, HC)
-        row(t, 0, 0, 0, HC)
-        row(t, 2, 1, 0, HC)
-        new_state(t, 1, "p")
-        turn(A("tb", 0, HC), bank(1, 0, HC))
-        turn(A("ta", 0, HC), bank(0, 0, HC))
+        state(t, 0)
+        compare(0, range(4))
+        diagonal(0)
+        count(0, (0, 2))
+        state(t, 1)
+        compare(0, range(4, 8))
+        count(0, (1, 3))
+        order(t, 0, donor)
+        compare(1, range(8))
+        diagonal(1)
+        count(1, (0, 2, 1, 3))
+        order(t, 1, donor)
+        for tile in (0, 2, 1, 3):
+            mm(bank(3, 0, C), *half("bc", "bs", tile // 2), *pair("fc", "fs", C * tile, C * tile + C), tile == 0, tile == 3)
+        tt(A("w2"), A("iw"), bank(3, 0, C), ALU.add)
         for b in range(4):
-            sign(2, b, 0, HC)
-        for s in range(3):
-            le_v(0, s, 32 * (s + 1), HC)
-            lt_v(0, s)
-        diagonal(0, 0, 0)
-        new_state(t, 1, "s")
-        new_state(t, 1, "v")
-        for s in range(3):
-            le_s(s, 32 * (s + 1), HC)
-            lt_s(s)
-        diagonal(0, 0, 2)
-        new_state(t, 1, "q")
-        row(t, 4, 0, 0, C)
-        row(t, 6, 1, 0, C)
-        row(t, 5, 1, HC, C)
-        diagonal(0, 0, 1)
-        pack(2, 0, HC)
-        spare(6, soon)
-        pack(0, 0, HC)
-        if t > 0:
-            for b in range(4):
-                mm(bank(DB[b]), *e_(b), *pair(tc, tsc))
-        for b in range(4):
-            sign(6, b, HC, C)
-        le_v(4, 0, HC, C)
-        turn(A("tb", HC, C), bank(5, 0, HC))
-        turn(A("ta", HC, C), bank(4, HC, C))
-        for s in range(3):
-            le_s(s, HC, C)
-        for b in range(4, 8):
-            sign(6, b, 0, C)
-        for s in range(3, 7):
-            lt_s(s, 0, HC)
-        for s in range(3, 7):
-            le_s(s, 32 * (s + 1), C)
-            if s > 3:
-                lt_s(s, HC, C)
-        for s in range(1, 3):
-            le_v(4, s, HC, C)
-        diagonal(1, 4, 0)
-        le_v(4, 3, HC, C)
-        lt_v(4, 3)
-        diagonal(1, 4, 1)
-        spare(6, soon)
-        le_v(4, 4, 160, C)
-        lt_v(4, 4)
-        pack(0, HC, C)
-        count(0)
-        for s in range(5, 7):
-            le_v(4, s, 32 * (s + 1), C)
-            lt_v(4, s)
-        diagonal(1, 4, 2)
-        pack(1, 0, C)
-        count(1)
-        pack(2, HC, C)
-        count(2)
-        pack(3, 0, HC)
-        pack(3, HC, C)
-        count(3)
-        if t == 0:
-            act(A("thj"), ind(A("th64"), offs(O_ORD, 16)), ACT.Copy)
-            act(A("iw"), A("ci"), ACT.Identity, scale=1.0 / 65536, bias=pf(S3))
-        else:
-            for tile in range(4):
-                count(tile, 5, "bc", "bs")
-            for b in range(4):
-                act(A("dw", C * b, C * b + C), bank(DB[b]), ACT.Copy)
-        spare(4, later)
-        for a in range(4):
-            turn(A("lt", p0=32 * a, p1=32 * a + 32), A("ps", 512 * 3 + a, 512 * 3 + C, 4, 32 * a, 32 * a + 32))
-        spare(2, later)
-        if t == 0:
-            for tile in range(4):
-                count(tile, 5, "bc", "bs")
-        tt(A("bf"), ind(A("lt"), offs(O_ORD, 16)), A("thj"), ALU.is_gt)
-        spare(2, later)
-        scan(A("oo", 0, C), A("rr"), A("bf"), ALU.mult, ALU.add)
-        act(A("rs%d" % t), ind(A("oo"), offs(O_EXP, 4)), ACT.Exp, scale=math.log(2.0) / 2)
-        send(donor, v(A("rl%d" % t)), v(A("rs%d" % t)), A("rs%d" % t), "ra%d" % t)
-        arrive([A("rl%d" % t)], "ra%d" % t, 1)
-        if t == 0:
-            spare(2, later)
-            tt(A("w2"), A("iw"), bank(5), ALU.add)
-            spare(1, later)
-            spare(1, latest)
-            for step in range(4):
-                candidates(0, step)
-                spare(1, latest)
-            for b in range(4):
-                act(A("dw", C * b, C * b + C), bank(DB[b]), ACT.Copy)
-            copy(A("gk"), ind(A("w2"), A("cand", 0, 16)))
-            spare(3, latest)
-        else:
-            tt(A("w2"), A("iw"), bank(5), ALU.add)
-            copy(A("gk", 0, HC), ind(A("w2"), A("cand", 16 * t, 16 * t + 8)))
-            act(A("gk", HC, C), ind(A("w2"), A("cand", 16 * t + 8, 16 * t + 16)), ACT.Copy)
-        turn(A("kt"), A("gk"))
-        spare(3, latest)
-        act(A("kf"), ind(A("kt"), offs(O_KF, 8)), ACT.Copy)
-        ts(A("f1"), A("kt"), 192.0 / 256, ALU.is_lt)
-        spare(3, latest)
-        for k in range(4):
-            scan(A("uu", 64 * k, 64 * k + 64), A("rl%d" % t), A("f1", 64 * k, 64 * k + 64), ALU.mult, ALU.add)
-        ts(A("nb", 0, 64), ind(A("uu"), offs(O_NK, 4)), 0.5, ALU.mult, 128.5 + 2.0 ** -9, ALU.add)
-        act(A("nb", 64, 128), ind(A("uu"), offs(O_NK + 4, 4)), ACT.Identity, scale=0.5, bias=128.5 + 2.0 ** -9)
-        tt(A("sc"), A("kf"), A("nb"), ALU.subtract)
-        scan(A("ms"), A("big8"), A("sc"), ALU.add, ALU.min)
-        moves = [(0, 0, 0, 128), (2, 0, 64, 64), (2, 64, 0, 64)]
-        moves += [(d, 32 * a, 32 * ((a + d) % 4), 32) for d in (1, 3) for a in range(4)]
-        for k, (d, to, fr, n) in enumerate(moves):
-            o_, i_ = A("cp", 16 * d, 16 * d + 16, 1, to, to + n), A("ms", 7, 128, 8, fr, fr + n)
-            if k % 2 == 0:
-                ts(o_, i_, 65536.0, ALU.mult)
-            else:
-                act(o_, i_, ACT.Copy, scale=65536.0)
-        copy(A("dg"), ind(A("cp"), offs(O_DUP, 4)))
-        ts(A("ea"), A("dg"), C - 1, ALU.bitwise_and)
-        turn(A("et"), A("ea"))
-        ts(A("zo"), A("et"), pc(6), ALU.add)
-
-        def mosaic(q):
-            o_, i_ = A("zt", 256 * q, 256 * q + 256), ind(A("dw"), A("zo", 16 * q, 16 * q + 16))
-            if q % 2 == 0:
-                copy(o_, i_)
-            else:
-                act(o_, i_, ACT.Copy)
-
-        def layer(h):
-            quant(*half("zc", "zs", h), A("zt", 512 * h, 512 * h + 512))
-            for b in (0, 2, 1, 3):
-                mm(bank(4 * h + b, 0, HC), *pair("wq", "wp", 128 * b, 128 * b + 128), *half("zc", "zs", h))
-
-        def relu(h):
-            for b in (0, 1):
-                ts(A("ht", 512 * h + b, 512 * h + 512, 4), bank(4 * h + b, 0, HC), 0.0, ALU.max, 0.015625, ALU.mult)
-                act(A("ht", 512 * h + b + 2, 512 * h + 512, 4), bank(4 * h + b + 2, 0, HC), ACT.Relu, scale=0.015625)
-
-        def ship(h):
-            hc, hs = half("hc%d" % t, "hs%d" % t, h)
-            lc, ls = half("lc%d" % t, "ls%d" % t, h)
-            quant(hc, hs, A("ht", 512 * h, 512 * h + 512))
-            send(child, raw(lc), raw(hc), hc, "ha%d_%d" % (t, h))
-            send(child, v(ls), v(hs), hs, "ha%d_%d" % (t, h))
-            arrive([lc, ls], "ha%d_%d" % (t, h), 2)
-
-        mosaic(0)
-        mosaic(1)
-        mosaic(3)
-        layer(0)
-        mosaic(2)
-        relu(0)
-        layer(1)
-        ship(0)
-        relu(1)
-        ship(1)
+            mm(bank(UNPACKED[b], 0, C), *e_(b), *pair("tc%d" % t, "ts%d" % t))
+            act(A("dw", C * b, C * b + C), bank(UNPACKED[b], 0, C), ACT.Copy)
         for h in range(2):
-            for b in range(4):
-                mm(bank(4 * h + b, 0, HC), *e_(b), *half(tc, tsc, h), True, False)
-        if t < R - 1:
-            for step in range(4):
-                candidates(t + 1, step)
-        else:
-            copy(A("eb"), A("ea", 0, 64, 4))
-            quant(A("vc"), A("vs"), A("vin"))
-            for n in range(2):
-                for s in range(2):
-                    dma("Y", "dout", T.el[s:8:2, HC * n:HC * n + HC], T.eb[:, 8 * n + 4 * s:8 * n + 4 * s + 4], [], [A("eb")])
+            leaders(t, h)
+            layer(t, h, child)
+    copy(A("eb"), A("ea", 0, 64, 4))
+    for n in range(2):
+        for s in range(2):
+            dma("Y", "dout", T.el[s:8:2, HC * n:HC * n + HC], T.eb[:, 8 * n + 4 * s:8 * n + 4 * s + 4], [], [A("eb")])
     tc, tsc = "tc%d" % R, "ts%d" % R
     for h in range(2):
-        for part in "pvsq":
-            new_state(R, h, part)
         c0, c1 = HC * h, HC * h + HC
-        mm(bank(4 * h, 0, HC), A("vc"), A("vs"), *half(tc, tsc, h))
+        state(R, h)
+        mm(bank(4 * h), A("vc"), A("vs"), *half(tc, tsc, h))
         dma("Y", "dout", T.oc[:, 4 * c0:4 * c1], raw(A(tc, c0, c1)), [], [A(tc, c0, c1)])
-        if h == 1:
-            for k in range(4):
-                dma("S" if k % 2 else "Y", "dout", T.osc[4 * k:4 * k + 4, :], T[tsc][32 * k:32 * k + 4, :], [], [A(tsc)])
-        copy(A("yb", c0, c1), bank(4 * h, 0, HC))
-        dma("Y" if h == 0 else "S", "dout", T.y[:, c0:c1], T.yb[:, c0:c1], [], [A("yb", c0, c1)])
-    _emit(g, T, ops)
+        move(h == 1, A("yb", c0, c1), bank(4 * h))
+        dma("S", "dout", T.y[:, c0:c1], T.yb[:, c0:c1], [], [A("yb", c0, c1)])
+    for k in range(4):
+        dma("Y", "dout", T.osc[4 * k:4 * k + 4, :], T[tsc][32 * k:32 * k + 4, :], [], [A(tsc)])
+    _emit(g, T, _arrange(ops))

@@ -4,11 +4,10 @@ from concourse.mybir import dt, AluOpType as ALU, ActivationFunctionType as ACT
 C, R, N, HC = 256, 3, 8, 128
 F32, BF, I32, U16, CODE, U8 = "float32", "bfloat16", "int32", "uint16", "float8_e4m3fn_x4", "uint8"
 _SIZES = {
-    BF: dict(xin=1024, uin=512, vin=512, ones=528, ebig=528, gi=136, bt=544, yi=128, thr=128, mi=64, sd=256, sg=2048, pa=160, x1=160, x2=160,
-             x3=132, bd=528, ex=128, rr=128, th32=32, thj=128, bf=256, oo=288, fl=4096, f1=256, nb=256, dw=1024, zt=1024, ht=1024, xt=1024),
-    F32: dict(pf=16, pc=16, pat=48, ci=256, iw=256, mk=64, cm=192, c2=96, c1=48, tm=256, w2=256, zi=32, zt32=32,
-              lt=64, uu=272, gk=256, kt=256, kf=256, ms=256, cp=64, eb=16, yb=256),
-    I32: dict(cdr=384, pi=1, pb=16, ui=24, pb1=160, pbm=160, oi=8, oj=8, dg=64, ea=64, et=64),
+    BF: dict(xin=1024, uin=512, vin=512, ones=528, ebig=528, gi=136, gc=128, gd=64, bt=544, yi=128, thr=128, sd=256, sg=2048, eq=384,
+             x3=256, bd=1024, ex=128, rr=128, thj=128, bf=256, oo=288, fl=4096, f1=256, nb=256, dw=1024, zt=1024, ht=1024, xt=1024),
+    F32: dict(pf=16, pc=16, pat=48, ci=256, iw=256, tm=256, w2=256, uu=272, gk=256, kt=256, kf=256, ms=256, cp=64, eb=64, yb=256),
+    I32: dict(cdr=384, pi=1, pb=16, ui=24, dg=64, ea=64, et=64),
     U16: dict(off=48, uo=24, cand=48, zo=64),
     CODE: dict(uc=128, upc=384, vc=128, wq=512, ec=512, bc=256, dc=256, fc=1024, zc=256),
     U8: dict(us=128, ups=384, vs=128, wp=512, es=512, bs=256, ds=256, fs=1024, zs=256),
@@ -25,9 +24,9 @@ for _t in range(R + 1):
 SEMAPHORES = ["V", "S", "P", "G", "dx0", "dx1", "du", "dcd", "dw", "dv", "dout", "sent"] + \
     ["%s%d_%d" % (k, t, h) for k in ("ra", "ha") for t in range(R) for h in range(2)]
 
-CYCLE, COLUMN, WAKE, CALL, HOP, LOAD = 0.0009, 0.0006, 0.19, 0.4, 1.25, 1.9
+CYCLE, COLUMN, WAKE, CALL, HOP, LOAD = 0.0009, 0.0006, 0.22, 0.4, 1.25, 1.9
 RATIOS = ((0, 32), (32, 96))
-ON_VECTOR = dict(state=(0, 1), late_state=(0, 1), below=(3, 4), above=())
+BELOW = (3, 4)
 
 
 def A(name, c0=0, c1=None, step=1, p0=0, p1=128):
@@ -36,8 +35,8 @@ def A(name, c0=0, c1=None, step=1, p0=0, p1=128):
     return (name, p0, p1, c0, c1, step)
 
 
-def bank(k, c0=0, c1=HC):
-    return A("ps", 512 * k + c0, 512 * k + c1)
+def bank(k, c0=0, c1=HC, step=1):
+    return A("ps", 512 * k + c0, 512 * k + c1, step)
 
 
 def _meet(a, b):
@@ -81,7 +80,7 @@ def _touch(ops):
 
 def _arrange(ops):
     deps, behind = _touch(ops)
-    last = {}
+    n, last = len(ops), {}
     for i, o in enumerate(ops):
         if o["q"] is None:
             behind[i] |= set(j for j in range(i) if ops[j].get("to") == o["sem"])
@@ -89,46 +88,40 @@ def _arrange(ops):
             if o["q"] in last:
                 behind[i].add(last[o["q"]])
             last[o["q"]] = i
-    after = [[] for _ in ops]
-    for i in range(len(ops)):
-        for j in deps[i] | behind[i]:
-            after[j].append(i)
-    chain = [0.0] * len(ops)
-    for i in range(len(ops) - 1, -1, -1):
-        chain[i] = ops[i]["c"] + ops[i].get("lag", 0.0) + max([chain[k] + (WAKE if i in deps[k] else 0.0) for k in after[i]] + [0.0])
-    left = [len(deps[i] | behind[i]) for i in range(len(ops))]
-    ready, start, end = {}, {}, {}
-    free = dict.fromkeys("VSPGY", 0.0)
-    pool = [i for i in range(len(ops)) if left[i] == 0]
-    for i in pool:
-        ready[i] = 0.0
+    before = [{j: ops[j]["c"] for j in behind[i]} for i in range(n)]
+    for i in range(n):
+        for j in deps[i]:
+            before[i][j] = ops[j]["c"] + ops[j].get("lag", 0.0) + WAKE
+    after = [{} for _ in ops]
+    for i in range(n):
+        for j, gap in before[i].items():
+            after[j][i] = gap - ops[j]["c"] + ops[i]["c"]
+    tail = [o.get("lag", 0.0) for o in ops]
 
-    def run(i, at):
-        start[i], end[i] = at, at + ops[i]["c"] + ops[i].get("lag", 0.0)
-        pool.remove(i)
-        for k in after[i]:
-            left[k] -= 1
-            if left[k] == 0:
-                ready[k] = max([end[j] + WAKE for j in deps[k]] + [start[j] + ops[j]["c"] for j in behind[k]])
-                pool.append(k)
+    def lay(order, edges, first):
+        at, taken = [0.0] * n, {q: [] for q in "VSPGY"}
+        for i in order:
+            t, c = max([first[i]] + [at[j] + gap for j, gap in edges[i].items()]), ops[i]["c"]
+            if ops[i]["q"] is not None:
+                busy, k = taken[ops[i]["q"]], 0
+                while k < len(busy) and busy[k][0] < t + c - 1e-9:
+                    t = max(t, busy[k][1])
+                    k += 1
+                busy.insert(k, (t, t + c))
+            at[i] = t
+        return at
 
-    while pool:
-        for i in [i for i in pool if ops[i]["q"] is None]:
-            run(i, ready[i])
-        if not pool:
-            break
-        q = min(set(ops[i]["q"] for i in pool), key=lambda q: (max(free[q], min(ready[i] for i in pool if ops[i]["q"] == q)), q))
-        mine = [i for i in pool if ops[i]["q"] == q]
-        now = max(free[q], min(ready[i] for i in mine))
-        best = max(mine, key=lambda i: (chain[i] - max(0.0, ready[i] - now), -i))
-        if ready[best] > now:
-            fits = [i for i in mine if max(ready[i], now) + ops[i]["c"] <= ready[best] + 0.03]
-            if fits:
-                best = max(fits, key=lambda i: (chain[i], -i))
-        at = max(now, ready[best])
-        free[q] = at + ops[best]["c"]
-        run(best, at)
-    return [ops[i] for i in sorted(range(len(ops)), key=lambda i: (start[i], i))]
+    back = [0.0] * n
+    for i in range(n - 1, -1, -1):
+        back[i] = max([tail[i]] + [back[j] + gap for j, gap in after[i].items()])
+    best = None
+    for _ in range(3):
+        start = lay(sorted(range(n), key=lambda i: (-back[i] - ops[i]["c"], i)), before, [0.0] * n)
+        span = max(start[i] + ops[i]["c"] + tail[i] for i in range(n))
+        if best is None or span < best[0]:
+            best = (span, start)
+        back = lay(sorted(range(n), key=lambda i: (-start[i] - ops[i]["c"], -i)), after, tail)
+    return [ops[i] for i in sorted(range(n), key=lambda i: (best[1][i], i))]
 
 
 def _emit(g, T, ops):
@@ -209,7 +202,7 @@ def rank_program(g, core, T, topo):
         op("V", lambda q: q.tensor_copy(v(out), v(in_)), _length(out, [in_]), [out], [in_])
 
     def tt(out, a, b, o):
-        op("V", lambda q: q.tensor_tensor(v(out), v(a), v(b), o), _length(out, [a, b], b[0] != "ps"), [out], [a, b])
+        op("V", lambda q: q.tensor_tensor(v(out), v(a), v(b), o), _length(out, [a, b], "ps" not in (a[0], b[0])), [out], [a, b])
 
     def ts(out, a, s1, o1, s2=None, o2=None):
         if o2 is None:
@@ -266,7 +259,8 @@ def rank_program(g, core, T, topo):
 
     def send(dst, out, in_, src, sem):
         rid, pid = topo.addr(dst, core)
-        op("G", lambda q: q.remote_dma(out, in_, T.sem[sem], T.sem.sent, pid, rid, mask), CALL, [], [src], sem="sent", n=nen, to=sem)
+        length = CALL + (1.0 if sem == "ra0_0" else 0.0)
+        op("G", lambda q: q.remote_dma(out, in_, T.sem[sem], T.sem.sent, pid, rid, mask), length, [], [src], sem="sent", n=nen, to=sem)
 
     def arrive(views, sem, calls):
         op(None, None, HOP, views, [], sem=sem, n=nen * calls)
@@ -292,24 +286,23 @@ def rank_program(g, core, T, topo):
     def pat(o, k):
         return A("pat", o, o + k)
 
-    dma("S", "du", T.uin[:, :], T.u[:, :], [A("uin")], [])
+    dma("Y", "du", T.uin[:, :], T.u[:, :], [A("uin")], [])
     for h in range(2):
         dma("Y", "dx%d" % h, T.xin[:, 512 * h:512 * h + 512], T.x[:, 512 * h:512 * h + 512], [A("xin", 512 * h, 512 * h + 512)], [])
-    for a in range(4):
-        for m in range(8):
-            p0 = 32 * a + 4 * m
-            dma("Y", "dcd", T.cdr[p0:p0 + 4, :], T.cd[a:16:4, :], [A("cdr", p0=p0, p1=p0 + 4)], [])
+    for k in range(8):
+        dma("Y", "dcd", T.cdr[16 * k:16 * k + 16, :], T.cd[:, :], [A("cdr", p0=16 * k, p1=16 * k + 16)], [])
     dma("Y", "dw", raw(A("wq")), T.wc[:, :], [A("wq")], [])
     dma("Y", "dw", T.wp[:, :], T.ws[:, :], [A("wp")], [])
     dma("Y", "dv", T.vin[:, :], T.v[:, :], [A("vin")], [])
 
-    O_DIAG, O_ORD, O_EXP, O_NK, O_KF, O_UP, O_DUP, O_CD = 0, 8, 16, 20, 24, 28, 32, 34
-    BA, X31, S7, S15, S3, N4, B3, SA = range(8)
+    O_DIAG, O_EXP, O_NK, O_KF, O_UP, O_DUP, O_CD = 0, 8, 12, 16, 20, 24, 26
+    BA, X31, S7, S15, S3, N4, B3, SA, K1, B0 = range(10)
     iota(A("pi"), [[0, 1]], 0, 1)
-    for col, sh, keep in ((BA, 5, 3), (X31, 0, 31), (S7, 0, 7), (S15, 0, 15), (S3, 3, 1), (N4, 4, 1), (B3, 0, 3), (SA, 2, 3)):
+    for col, sh, keep in ((BA, 5, 3), (X31, 0, 31), (S7, 0, 7), (S15, 0, 15), (S3, 3, 1), (N4, 4, 1), (B3, 0, 3), (SA, 2, 3), (K1, 1, 3), (B0, 0, 1)):
         ts(pb(col), A("pi"), sh, ALU.logical_shift_right, keep, ALU.bitwise_and)
     copy(A("pf", 0, 4), A("pb", 0, 4))
-    copy(A("pf", 4, 8), A("pb", 4, 8))
+    copy(A("pf", 4, 10), A("pb", 4, 10))
+    ts(pc(4), pf(BA), 2.0, ALU.mult)
     ts(pc(5), pf(BA), 2.0, ALU.mult, 1.0, ALU.add)
     iota(A("ui", 0, 8), [[16, 8]])
     iota(A("ui", 8, 24), [[16, 2], [32, 4], [0, 2]])
@@ -324,39 +317,35 @@ def rank_program(g, core, T, topo):
     ts(A("thr"), A("yi"), pf(X31), ALU.is_gt, -2.0 ** -120, ALU.mult)
     iota(pat(O_DIAG, 8), [[HC + 32, 4], [16, 2]])
     ts(offs(O_DIAG, 8), pat(O_DIAG, 8), pf(S15), ALU.add)
-    iota(A("pb1"), [[0, 5], [1, 8], [1, 4]], 1)
-    iota(A("pa"), [[0, 5], [1, 8], [0, 4]])
-    ts(A("pbm"), A("pb1"), 7, ALU.bitwise_and)
-    ts(A("x2"), A("pbm"), pc(5), ALU.is_equal)
-    ts(A("x1"), A("pa"), pc(5), ALU.is_equal)
-    tt(A("x3"), A("x1", 0, 132), A("x2", 0, 132), ALU.subtract)
     iota(A("gi"), [[0, 17], [1, 8]])
+    iota(A("gc"), [[0, 2], [1, 8], [0, 8]])
+    iota(A("gd"), [[1, 8], [-1, 8]])
+    for odd in range(2):
+        this, other, prior = [A("eq", 192 * odd + 64 * k, 192 * odd + 64 * k + 64) for k in range(3)]
+        ts(this, A("gc", 0, 64), pc(4 + odd), ALU.is_equal)
+        ts(other, A("gi", 0, 64), pc(4 + odd), ALU.is_equal)
+        ts(prior, A("gc", 56, 120), pc(4 + odd), ALU.is_equal)
+        tt(A("x3", HC * odd, HC * odd + HC, 2), this, other, ALU.subtract)
+        tt(A("x3", HC * odd + 1, HC * odd + HC, 2), other, prior, ALU.subtract)
+        for k in range(4):
+            act(A("bd", 512 * odd + k, 512 * odd + 512, 4), A("x3", HC * odd, HC * odd + HC), ACT.Copy)
     for k in range(4):
-        act(A("bd", k, 528, 4), A("x3"), ACT.Copy)
         ts(A("bt", k, 544, 4), A("gi"), pc(5), ALU.is_equal, 1.0 / 256, ALU.mult)
     for odd in range(2):
-        quant(*half("dc", "ds", odd), A("bd", 16 - 16 * odd, 528 - 16 * odd))
+        quant(*half("dc", "ds", odd), A("bd", 512 * odd, 512 * odd + 512))
         quant(*half("bc", "bs", odd), A("bt", 4 - 4 * odd, 516 - 4 * odd))
-    iota(A("zi"), [[0, 2], [20, 4], [-3, 4]], 28)
-    iota(A("zi", 4, 12), [[1, 8]], 28)
-    iota(A("zi", 20, 28), [[1, 8]], 28)
-    turn(A("zt32"), A("zi"))
-    ts(A("oi"), A("pa", 0, 32, 4), 4.0, ALU.mult, A("zt32", 0, 1), ALU.add)
-    ts(A("oj"), A("oi"), 31, ALU.bitwise_and)
-    copy(offs(O_ORD, 8), A("oj"))
-    ts(A("th32"), A("pb1", 0, 32), 8.0, ALU.is_lt, 0.5, ALU.subtract)
-    act(A("thj"), ind(A("th32"), offs(O_ORD, 8)), ACT.Copy)
+    ts(A("thj", 0, HC, 2), A("gd"), 0.0, ALU.is_le, 0.5, ALU.subtract)
+    ts(A("thj", 17, HC, 2), A("gd", 8, 64), 0.0, ALU.is_gt, 0.5, ALU.subtract)
+    fill(A("thj", 1, 16, 2), 0.5)
     fill(A("ex"), 0.0)
-    fill(A("ex", 3, HC, 4), 1.0)
-    fill(A("ex", 4, HC, 8), -1.0)
     fill(A("ex", 0, HC, 16), -200.0)
-    act(A("rr"), A("ex"), ACT.Exp, more=1.4, scale=math.log(2.0))
-    fill(A("rr", 8, HC, 16), -0.5)
+    act(A("rr"), A("ex"), ACT.Exp, more=1.4)
     fill(A("oo", HC, 288, 144), -400.0)
     ts(pc(2), pf(S15), 0.0, ALU.is_equal, float(HC - 15), ALU.mult)
     ts(pc(12), pf(S7), 16.0, ALU.mult, pc(2), ALU.add)
-    ts(offs(O_EXP, 4), A("pa", 0, 4), pc(12), ALU.add, 15.0, ALU.add)
-    fill(A("ones"), 1.0)
+    ts(offs(O_EXP, 4), A("gc", 0, 4), pc(12), ALU.add, 15.0, ALU.add)
+    for k in range(4):
+        fill(A("ones", 132 * k, 132 * k + 132), 1.0)
     select(A("ebig"), A("ones"), [[-1, 528]], ALU.is_equal, 3, 4)
 
     def e_(b):
@@ -366,12 +355,11 @@ def rank_program(g, core, T, topo):
         quant(*e_(b), A("ebig", 3 - b, 515 - b))
     iota(A("ci"), [[1, 256]])
     act(A("iw"), A("ci"), ACT.Identity, scale=1.0 / 65536, bias=pf(S3))
-    iota(A("mi"), [[0, 16], [1, 4]])
-    ts(A("mk"), A("mi"), pf(SA), ALU.is_equal)
-    iota(pat(O_CD, 12), [[128, 3], [8, 2], [64, 2]])
-    ts(pc(3), pf(S3), 32.0, ALU.mult, pf(S7), ALU.add)
-    ts(pc(10), pf(N4), 16.0, ALU.mult, pc(3), ALU.add)
-    ts(offs(O_CD, 12), pat(O_CD, 12), pc(10), ALU.add)
+    iota(pat(O_CD, 4), [[128, 4]])
+    ts(pc(3), pf(S3), 8.0, ALU.mult, pf(B0), ALU.add)
+    ts(pc(8), pf(N4), 16.0, ALU.mult, pc(4), ALU.add)
+    ts(pc(9), pf(K1), 32.0, ALU.mult, pc(3), ALU.add)
+    ts(offs(O_CD, 4), pat(O_CD, 4), pc(8), ALU.add, pc(9), ALU.add)
     iota(pat(O_NK, 4), [[2, 4]])
     ts(pc(1), pf(S7), 16.0, ALU.mult, pf(S3), ALU.add)
     ts(offs(O_NK, 4), pat(O_NK, 4), pc(1), ALU.add, 8.0, ALU.add)
@@ -381,21 +369,16 @@ def rank_program(g, core, T, topo):
     fill(A("kf", 1, C, 2), 1000.0)
     fill(A("uu", HC, 272, 136), 4000.0)
     iota(pat(O_DUP, 2), [[1, 2]])
-    ts(pb(9), pf(SA), pf(BA), ALU.subtract, 4.0, ALU.add)
-    ts(pb(11), pb(9), 3, ALU.bitwise_and)
-    ts(pc(4), pf(BA), 2.0, ALU.mult)
+    ts(pb(12), pf(SA), pf(BA), ALU.subtract, 4.0, ALU.add)
+    ts(pb(11), pb(12), 3, ALU.bitwise_and)
     ts(pc(13), pb(11), 8.0, ALU.mult, pc(4), ALU.add)
     ts(offs(O_DUP, 2), pat(O_DUP, 2), pc(13), ALU.add)
     ts(pc(6), pf(B3), 256.0, ALU.mult)
     quant(A("vc"), A("vs"), A("vin"))
-    for t in range(R):
-        tt(A("cm", 64 * t, 64 * t + 64), ind(A("cdr"), offs(O_CD + 4 * t, 4)), A("mk"), ALU.mult)
-        tt(A("c2", 32 * t, 32 * t + 32), A("cm", 64 * t, 64 * t + 64, 2), A("cm", 64 * t + 1, 64 * t + 64, 2), ALU.add)
-        tt(A("c1", 16 * t, 16 * t + 16), A("c2", 32 * t, 32 * t + 32, 2), A("c2", 32 * t + 1, 32 * t + 32, 2), ALU.add)
-        copy(A("cand", 16 * t, 16 * t + 16), A("c1", 16 * t, 16 * t + 16))
+    copy(A("cand"), ind(A("cdr"), offs(O_CD, 3)))
 
     MIXED, EVEN, ODD = range(3)
-    UNPACKED = (7, 0, 2, 1)
+    UNPACKED = (3, 0, 2, 1)
 
     def slot(tile, k, c0, c1):
         return A("fl", 1024 * tile + 4 * c0 + k, 1024 * tile + 4 * c1, 4)
@@ -417,7 +400,7 @@ def rank_program(g, core, T, topo):
             for b in (0, 2, 1, 3):
                 mm(bank(4 * h + b), *e_(b), *half("lc%d" % (t - 1), "ls%d" % (t - 1), h), False, True)
             for b in range(4):
-                move(b in ON_VECTOR["late_state" if h and t < R else "state"], A("xt", x0 + b, x0 + 512, 4), bank(4 * h + b))
+                move(b < 2, A("xt", x0 + b, x0 + 512, 4), bank(4 * h + b))
         quant(*mine, A("xt" if t else "xin", x0, x0 + 512))
         if t < R:
             for k, kind in ((1, MIXED), (2, ODD), (0, EVEN), (3, EVEN)):
@@ -434,13 +417,10 @@ def rank_program(g, core, T, topo):
                 act(A("sd", lo, hi), bank(4 * h + 3, lo - c0, hi - c0), ACT.Sign, scale=-1.0, bias=own(b, 0))
             if hi < c1:
                 ts(place(0, b, hi, c1), bank(4 * h, hi - c0, HC), own(b, 0), ALU.is_le)
-                if h == 1 and b in ON_VECTOR["above"]:
-                    ts(place(1, b, hi, c1), signs(b, hi, c1), 0.0, ALU.is_ge)
-                else:
-                    act(place(1, b, hi, c1), signs(b, hi, c1), ACT.Sign, bias=1.0)
+                act(place(1, b, hi, c1), signs(b, hi, c1), ACT.Sign, bias=1.0)
             if c0 < lo:
                 ts(place(0, b - 1, c0, lo), bank(4 * h, 0, lo - c0), own(b, 0), ALU.is_lt)
-                if h == 0 and b - 1 in ON_VECTOR["below"]:
+                if h == 0 and b - 1 in BELOW:
                     ts(place(1, b - 1, c0, lo), signs(b, c0, lo), 0.0, ALU.is_gt)
                 else:
                     act(place(1, b - 1, c0, lo), signs(b, c0, lo), ACT.Relu)
@@ -454,16 +434,20 @@ def rank_program(g, core, T, topo):
         for tile in tiles:
             c0 = C * tile + HC * h
             quant(*pair("fc", "fs", c0, c0 + HC), A("fl", 4 * c0, 4 * c0 + 512))
-            mm(bank(4 * h + 1), *half("dc", "ds", tile // 2), *pair("fc", "fs", c0, c0 + HC), tile == 0, tile == 3)
+            mm(bank(4 * h + 1), *pair("fc", "fs", c0, c0 + HC), *half("dc", "ds", tile // 2), tile == 0, tile == 3)
+
+    def places(h):
+        c0, c1 = HC * h, HC * h + HC
+        for tile in (0, 2, 1, 3):
+            mm(bank(4 * h + 3), *half("bc", "bs", tile // 2), *pair("fc", "fs", C * tile + c0, C * tile + c1), tile == 0, tile == 3)
+        tt(A("w2", c0, c1), A("iw", c0, c1), bank(4 * h + 3), ALU.add)
 
     def order(t, h, donor):
         r0, r1 = RATIOS[h]
-        mine, theirs, at = A("rs%d" % t, r0, r1), A("rl%d" % t, r0, r1), 512 * (4 * h + 1)
-        for a in range(4):
-            turn(A("lt", 32 * h, 32 * h + 32, 1, 32 * a, 32 * a + 32), A("ps", at + a, at + HC, 4, 32 * a, 32 * a + 32))
-        tt(A("bf", HC * h, HC * h + HC), ind(A("lt", 32 * h, 32 * h + 32), offs(O_ORD, 8)), A("thj"), ALU.is_gt)
+        mine, theirs = A("rs%d" % t, r0, r1), A("rl%d" % t, r0, r1)
+        tt(A("bf", HC * h, HC * h + HC), bank(4 * h + 1), A("thj"), ALU.is_gt)
         scan(A("oo", 144 * h, 144 * h + HC), A("rr"), A("bf", HC * h, HC * h + HC), ALU.mult, ALU.add)
-        act(mine, ind(A("oo", 144 * h, 144 * h + 144), offs(O_EXP, (r1 - r0) // 16)), ACT.Exp, scale=math.log(2.0) / 2)
+        act(mine, ind(A("oo", 144 * h, 144 * h + 144), offs(O_EXP, (r1 - r0) // 16)), ACT.Exp, scale=math.log(2.0), bias=-7 * math.log(2.0))
         send(donor, v(theirs), v(mine), mine, "ra%d_%d" % (t, h))
         arrive([theirs], "ra%d_%d" % (t, h), 1)
 
@@ -497,9 +481,13 @@ def rank_program(g, core, T, topo):
         quant(*half("zc", "zs", h), A("zt", x0, x0 + 512))
         for b in (0, 2, 1, 3):
             mm(bank(4 * h + b), *pair("wq", "wp", 128 * b, 128 * b + 128), *half("zc", "zs", h))
-        for b in (0, 1):
-            ts(A("ht", x0 + b, x0 + 512, 4), bank(4 * h + b), 0.0, ALU.max, 0.015625, ALU.mult)
-            act(A("ht", x0 + b + 2, x0 + 512, 4), bank(4 * h + b + 2), ACT.Relu, scale=0.015625)
+        for b in range(4):
+            for a in range(4):
+                o, i = A("ht", x0 + 128 * a + b, x0 + 128 * a + 128, 4), bank(4 * h + b, a, HC, 4)
+                if b < 2:
+                    ts(o, i, 0.0, ALU.max, 0.015625, ALU.mult)
+                else:
+                    act(o, i, ACT.Relu, scale=0.015625)
         quant(hc, hs, A("ht", x0, x0 + 512))
         send(child, raw(lc), raw(hc), hc, "ha%d_%d" % (t, h))
         send(child, v(ls), v(hs), hs, "ha%d_%d" % (t, h))
@@ -517,23 +505,21 @@ def rank_program(g, core, T, topo):
         compare(0, range(4, 8))
         count(0, (1, 3))
         order(t, 0, donor)
+        places(0)
         compare(1, range(8))
         diagonal(1)
         count(1, (0, 2, 1, 3))
         order(t, 1, donor)
-        for tile in (0, 2, 1, 3):
-            mm(bank(3, 0, C), *half("bc", "bs", tile // 2), *pair("fc", "fs", C * tile, C * tile + C), tile == 0, tile == 3)
-        tt(A("w2"), A("iw"), bank(3, 0, C), ALU.add)
+        places(1)
         for b in range(4):
             mm(bank(UNPACKED[b], 0, C), *e_(b), *pair("tc%d" % t, "ts%d" % t))
             act(A("dw", C * b, C * b + C), bank(UNPACKED[b], 0, C), ACT.Copy)
         for h in range(2):
             leaders(t, h)
             layer(t, h, child)
-    copy(A("eb"), A("ea", 0, 64, 4))
+    copy(A("eb"), A("et"))
     for n in range(2):
-        for s in range(2):
-            dma("Y", "dout", T.el[s:8:2, HC * n:HC * n + HC], T.eb[:, 8 * n + 4 * s:8 * n + 4 * s + 4], [], [A("eb")])
+        dma("Y", "dout", T.el[:, HC * n:HC * n + HC], T.eb[0:128:4, 32 * n:32 * n + 32], [], [A("eb")])
     tc, tsc = "tc%d" % R, "ts%d" % R
     for h in range(2):
         c0, c1 = HC * h, HC * h + HC

@@ -4,20 +4,21 @@ from concourse.mybir import dt, AluOpType as ALU, ActivationFunctionType as ACT
 C, R, N, HC = 256, 3, 8, 128
 F32, BF, I32, U16, CODE, U8 = "float32", "bfloat16", "int32", "uint16", "float8_e4m3fn_x4", "uint8"
 _SIZES = {
-    BF: dict(xin=1024, uin=512, vin=512, ones=528, ebig=528, gi=136, gc=128, gd=64, bt=544, yi=128, thr=128, sd=256, sg=2048, eq=384,
-             x3=256, bd=1024, ex=128, rr=128, thj=128, bf=256, oo=288, fl=4096, f1=256, nb=256, dw=1024, zt=1024, ht=1024, xt=1024),
-    F32: dict(pf=16, pc=16, pat=48, ci=256, iw=256, tm=256, w2=256, uu=272, gk=256, kt=256, kf=256, ms=256, cp=64, eb=64, yb=256),
-    I32: dict(cdr=384, pi=1, pb=16, ui=24, dg=64, ea=64, et=64),
-    U16: dict(off=48, uo=24, cand=48, zo=64),
-    CODE: dict(uc=128, upc=384, vc=128, wq=512, ec=512, bc=256, dc=256, fc=1024, zc=256),
-    U8: dict(us=128, ups=384, vs=128, wp=512, es=512, bs=256, ds=256, fs=1024, zs=256),
+    BF: dict(xin=1024, uin=512, vin=512, ones=528, ebig=528, gg=256, gd=64, fr=288, tf=288, bt=512, yi=128, thr=128, sd=256, sg=2048,
+             eq=512, bd=512, ex=256, rr=256, thj=128, bf=256, oo=288, fl=3584, su=1024, gf=256, f1=256, nb=256, dw=1024, zt=1024, ht=1024, xt=1024),
+    F32: dict(pat=16, ci=256, iw=256, tm=256, w2=256, uu=272, gk=256, kt=256, kf=256, ms=256, cp=128, eb=64, yb=256),
+    I32: dict(cdr=368, ui=16, dg=64, ea=64, et=64),
+    U16: dict(off=40, uo=16, cand=48, zo=64),
+    CODE: dict(uc=128, upc=256, vc=128, wq=512, ec=512, bc=128, dc=128, fc=896, zc=256),
+    U8: dict(us=128, ups=256, vs=128, wp=512, es=512, bs=128, ds=128, fs=896, zs=256),
 }
 SCRATCH = {"ps": ("psum", [128, 4096], F32)}
 for _d, _b in _SIZES.items():
     for _k, _n in _b.items():
         SCRATCH[_k] = ("sbuf", [128, _n], _d)
 for _t in range(R + 1):
-    for _k, _n, _d in (("tc", C, CODE), ("ts", C, U8), ("rs", 96, BF), ("rl", 96, BF), ("hc", C, CODE), ("hs", C, U8), ("lc", C, CODE), ("ls", C, U8)):
+    for _k, _n, _d in (("tc", C, CODE), ("ts", C, U8), ("rs", 96, BF), ("rl", 96, BF), ("hc", C, CODE), ("hs", C, U8), ("lc", C, CODE), ("ls", C, U8),
+                       ("pc", C, CODE), ("pz", C, U8)):
         if _t < R or _k[0] == "t":
             SCRATCH["%s%d" % (_k, _t)] = ("sbuf", [128, _n], _d)
 
@@ -26,7 +27,9 @@ SEMAPHORES = ["V", "S", "P", "G", "dx0", "dx1", "du", "dcd", "dw", "dv", "dout",
 
 CYCLE, COLUMN, WAKE, CALL, HOP, LOAD = 0.0009, 0.0006, 0.22, 0.4, 1.25, 1.9
 RATIOS = ((0, 32), (32, 96))
-BELOW = (3, 4)
+MOVES, SLACK = 30000, 0.04
+ACROSS = ("VVVV", "SSSS")
+UNPACK = "SSSS"
 
 
 def A(name, c0=0, c1=None, step=1, p0=0, p1=128):
@@ -121,7 +124,76 @@ def _arrange(ops):
         if best is None or span < best[0]:
             best = (span, start)
         back = lay(sorted(range(n), key=lambda i: (-start[i] - ops[i]["c"], -i)), after, tail)
-    return [ops[i] for i in sorted(range(n), key=lambda i: (best[1][i], i))]
+    if not _ORDER:
+        _ORDER.append(_shorten(ops, before, after, tail, best[1]))
+    return [ops[i] for i in _ORDER[0]]
+
+
+_ORDER = []
+
+
+def _shorten(ops, before, after, tail, start):
+    n = len(ops)
+    reach, needs = [0] * n, []
+    for i in range(n):
+        keep, seen = [], 0
+        for j in sorted(before[i], reverse=True):
+            if not seen >> j & 1 or before[i][j] > ops[j]["c"] + WAKE + 1e-9:
+                keep.append((j, before[i][j]))
+            seen |= reach[j] | 1 << j
+        reach[i] = seen
+        needs.append(keep)
+    c, q = [o["c"] for o in ops], [o["q"] for o in ops]
+
+    def play(order):
+        at, why, last, span, end = [0.0] * n, [None] * n, {}, 0.0, 0
+        for i in order:
+            t, w = 0.0, None
+            for j, gap in needs[i]:
+                if at[j] + gap > t:
+                    t, w = at[j] + gap, (j, False)
+            if q[i] is not None:
+                j = last.get(q[i])
+                if j is not None and at[j] + c[j] >= t:
+                    t, w = at[j] + c[j], (j, True)
+                last[q[i]] = i
+            at[i], why[i] = t, w
+            if t + c[i] + tail[i] > span:
+                span, end = t + c[i] + tail[i], i
+        return span, at, why, end
+
+    seed = [1]
+
+    def draw():
+        seed[0] = seed[0] * 48271 % 2147483647
+        return seed[0] / 2147483647
+
+    now = best = play(sorted(range(n), key=lambda i: (start[i], i)))
+    for step in range(MOVES):
+        pairs, i = [], now[3]
+        while now[2][i] is not None:
+            j, neighbour = now[2][i]
+            if neighbour and not reach[i] >> j & 1:
+                pairs.append((j, i))
+            i = j
+        if not pairs:
+            break
+        a, b = pairs[int(draw() * len(pairs))]
+        order = sorted(range(n), key=lambda i: now[1][i])
+        pos = {x: p for p, x in enumerate(order)}
+        if draw() < 0.5:
+            who, lo, hi = b, max([pos[j] + 1 for j, gap in needs[b]] + [pos[a] - 25, 0]), pos[a]
+        else:
+            who, lo, hi = a, pos[b], min([pos[j] - 1 for j in after[a]] + [pos[b] + 25, n - 1])
+        if lo > hi:
+            continue
+        order.insert(lo + int(draw() * (hi + 1 - lo)), order.pop(pos[who]))
+        new = play(order)
+        if new[0] <= now[0] - SLACK * (1 - step / MOVES) * math.log(draw()):
+            now = new
+            if new[0] < best[0]:
+                best = new
+    return sorted(range(n), key=lambda i: (best[1][i], i))
 
 
 def _emit(g, T, ops):
@@ -271,81 +343,89 @@ def rank_program(g, core, T, topo):
     def half(c, s, h):
         return pair(c, s, HC * h, HC * h + HC)
 
-    def pf(c):
-        return A("pf", c, c + 1)
-
-    def pc(c):
-        return A("pc", c, c + 1)
-
-    def pb(c):
-        return A("pb", c, c + 1)
-
     def offs(o, k):
         return A("off", o, o + k)
 
-    def pat(o, k):
-        return A("pat", o, o + k)
+    def pick(out, win, lst):
+        act(out[1], ind(win[1], lst), ACT.Copy)
+        op("V", lambda q: q.tensor_copy(v(out[0]).bitcast(dt.uint32), v(win[0]).bitcast(dt.uint32).indirect(v(lst))),
+           _length(out[0], [ind(win[0], lst)]), [out[0]], [win[0], lst])
 
     dma("Y", "du", T.uin[:, :], T.u[:, :], [A("uin")], [])
     for h in range(2):
         dma("Y", "dx%d" % h, T.xin[:, 512 * h:512 * h + 512], T.x[:, 512 * h:512 * h + 512], [A("xin", 512 * h, 512 * h + 512)], [])
     for k in range(8):
-        dma("Y", "dcd", T.cdr[16 * k:16 * k + 16, :], T.cd[:, :], [A("cdr", p0=16 * k, p1=16 * k + 16)], [])
+        o = 16 * (k % 2) + 2 * (k // 2)
+        dma("Y", "dcd", T.cdr[16 * k:16 * k + 16, 0:362], T.cd[:, o:o + 362], [A("cdr", p0=16 * k, p1=16 * k + 16)], [])
     dma("Y", "dw", raw(A("wq")), T.wc[:, :], [A("wq")], [])
     dma("Y", "dw", T.wp[:, :], T.ws[:, :], [A("wp")], [])
     dma("Y", "dv", T.vin[:, :], T.v[:, :], [A("vin")], [])
 
-    O_DIAG, O_EXP, O_NK, O_KF, O_UP, O_DUP, O_CD = 0, 8, 12, 16, 20, 24, 26
-    BA, X31, S7, S15, S3, N4, B3, SA, K1, B0 = range(10)
-    iota(A("pi"), [[0, 1]], 0, 1)
-    for col, sh, keep in ((BA, 5, 3), (X31, 0, 31), (S7, 0, 7), (S15, 0, 15), (S3, 3, 1), (N4, 4, 1), (B3, 0, 3), (SA, 2, 3), (K1, 1, 3), (B0, 0, 1)):
-        ts(pb(col), A("pi"), sh, ALU.logical_shift_right, keep, ALU.bitwise_and)
-    copy(A("pf", 0, 4), A("pb", 0, 4))
-    copy(A("pf", 4, 10), A("pb", 4, 10))
-    ts(pc(4), pf(BA), 2.0, ALU.mult)
-    ts(pc(5), pf(BA), 2.0, ALU.mult, 1.0, ALU.add)
-    iota(A("ui", 0, 8), [[16, 8]])
-    iota(A("ui", 8, 24), [[16, 2], [32, 4], [0, 2]])
+    O_DIAG, O_EXP, O_NK, O_KF, O_UP, O_DUP, O_MID = 0, 8, 12, 16, 20, 24, 26
+    BLOCK, ROW, SUMS, STEPS, FIRST, QUARTER, WOVEN, AGAIN, SOURCE = range(9)
+
+    def feature(k, c=0, n=1):
+        return A("tf", 32 * k + c, 32 * k + c + n)
+
+    def lay_out(k, pattern, base=0, cm=0):
+        iota(A("fr", 32 * k, 32 * k + 32), pattern, base, cm)
+
+    iota(A("ui"), [[16, 2], [32, 4], [0, 2]])
     copy(A("uo"), A("ui"))
     quant(A("uc"), A("us"), A("uin"))
-    for c0, c1 in ((0, HC), (HC, 3 * HC)):
-        o, w, lst = A("upc", c0, c1), A("uc"), A("uo", c0 // 16, c1 // 16)
-        act(A("ups", c0, c1), ind(A("us"), lst), ACT.Copy)
-        op("V", lambda q, o=o, w=w, lst=lst: q.tensor_copy(v(o).bitcast(dt.uint32), v(w).bitcast(dt.uint32).indirect(v(lst))),
-           _length(o, [ind(w, lst)]), [o], [w, lst])
-    iota(A("yi"), [[0, 4], [1, 32]])
-    ts(A("thr"), A("yi"), pf(X31), ALU.is_gt, -2.0 ** -120, ALU.mult)
-    iota(pat(O_DIAG, 8), [[HC + 32, 4], [16, 2]])
-    ts(offs(O_DIAG, 8), pat(O_DIAG, 8), pf(S15), ALU.add)
-    iota(A("gi"), [[0, 17], [1, 8]])
-    iota(A("gc"), [[0, 2], [1, 8], [0, 8]])
+    for odd in range(2):
+        pick(half("upc", "ups", odd), (A("uc"), A("us")), A("uo", 8 * odd, 8 * odd + 8))
+    lay_out(BLOCK, [[0, 32]], 0, 1)
+    turn(feature(BLOCK, 0, 32), A("fr", 0, 32))
+    iota(A("gg", 0, HC), [[0, 16], [16, 8]])
+    iota(A("gg", HC, C), [[0, 2], [16, 8], [0, 8]])
+    for odd in range(2):
+        e0 = C * odd
+        ts(A("eq", e0, e0 + C), A("gg"), feature(BLOCK, 16 * odd), ALU.is_equal)
+        this, other, prior = A("eq", e0 + 128, e0 + 192), A("eq", e0, e0 + 64), A("eq", e0 + 184, e0 + 248)
+        tt(A("bd", 2 * odd, 512, 8), this, other, ALU.subtract)
+        tt(A("bd", 2 * odd + 4, 512, 8), other, prior, ALU.subtract)
+        for k in range(2):
+            act(A("bt", 2 * odd + k, 512, 4), A("eq", e0, e0 + HC), ACT.Identity, scale=1.0 / 256)
+    copy(A("bd", 1, 512, 2), A("bd", 0, 512, 2))
+    quant(A("dc"), A("ds"), A("bd"))
+    quant(A("bc"), A("bs"), A("bt"))
+    iota(A("yi"), [[0, 4], [1, 32]], 0, -1)
+    ts(A("thr"), A("yi"), feature(BLOCK), ALU.add, 0.0, ALU.is_le)
+    lay_out(ROW, [[0, 2], [1, 16]])
+    turn(feature(ROW, 0, 32), A("fr", 32, 64))
+    iota(A("pat", 0, 8), [[HC + 32, 4], [16, 2]])
+    ts(offs(O_DIAG, 8), A("pat", 0, 8), feature(ROW), ALU.add)
     iota(A("gd"), [[1, 8], [-1, 8]])
-    for odd in range(2):
-        this, other, prior = [A("eq", 192 * odd + 64 * k, 192 * odd + 64 * k + 64) for k in range(3)]
-        ts(this, A("gc", 0, 64), pc(4 + odd), ALU.is_equal)
-        ts(other, A("gi", 0, 64), pc(4 + odd), ALU.is_equal)
-        ts(prior, A("gc", 56, 120), pc(4 + odd), ALU.is_equal)
-        tt(A("x3", HC * odd, HC * odd + HC, 2), this, other, ALU.subtract)
-        tt(A("x3", HC * odd + 1, HC * odd + HC, 2), other, prior, ALU.subtract)
-        for k in range(4):
-            act(A("bd", 512 * odd + k, 512 * odd + 512, 4), A("x3", HC * odd, HC * odd + HC), ACT.Copy)
-    for k in range(4):
-        ts(A("bt", k, 544, 4), A("gi"), pc(5), ALU.is_equal, 1.0 / 256, ALU.mult)
-    for odd in range(2):
-        quant(*half("dc", "ds", odd), A("bd", 512 * odd, 512 * odd + 512))
-        quant(*half("bc", "bs", odd), A("bt", 4 - 4 * odd, 516 - 4 * odd))
     ts(A("thj", 0, HC, 2), A("gd"), 0.0, ALU.is_le, 0.5, ALU.subtract)
     ts(A("thj", 17, HC, 2), A("gd", 8, 64), 0.0, ALU.is_gt, 0.5, ALU.subtract)
     fill(A("thj", 1, 16, 2), 0.5)
     fill(A("ex"), 0.0)
     fill(A("ex", 0, HC, 16), -200.0)
+    fill(A("ex", HC, C, 4), -200.0)
     act(A("rr"), A("ex"), ACT.Exp, more=1.4)
-    fill(A("oo", HC, 288, 144), -400.0)
-    ts(pc(2), pf(S15), 0.0, ALU.is_equal, float(HC - 15), ALU.mult)
-    ts(pc(12), pf(S7), 16.0, ALU.mult, pc(2), ALU.add)
-    ts(offs(O_EXP, 4), A("gc", 0, 4), pc(12), ALU.add, 15.0, ALU.add)
-    for k in range(4):
-        fill(A("ones", 132 * k, 132 * k + 132), 1.0)
+    fill(A("oo", 0, 288, 144), -400.0)
+    fill(A("fl", 6 * 512 + 1, 7 * 512, 2), 0.0)
+    lay_out(SUMS, [[0, 4], [16, 8]], 31)
+    lay_out(STEPS, [[0, 2], [1, 2], [16, 8]])
+    lay_out(FIRST, [[0, 4], [1024, 8]])
+    lay_out(QUARTER, [[0, 8], [256, 4]])
+    lay_out(WOVEN, [[0, 2], [1, 8], [64, 2]])
+    lay_out(AGAIN, [[0, 2], [1, 2], [0, 8]])
+    lay_out(SOURCE, [[0, 2], [128, 4], [0, 4]], 384, -3)
+    turn(feature(SUMS, 0, 7 * 32), A("fr", 32 * SUMS, 288))
+    iota(A("pat", 8, 16), [[8, 8]])
+    ts(offs(O_EXP, 4), feature(ROW, 0, 4), 1000.0, ALU.mult, feature(SUMS), ALU.min)
+    ts(offs(O_KF, 4), A("pat", 8, 12), 0.25, ALU.mult, feature(STEPS), ALU.add)
+    ts(offs(O_NK, 4), offs(O_KF, 4), 16.0, ALU.add)
+    ts(offs(O_UP, 4), offs(O_NK, 4), feature(FIRST), ALU.min)
+    ts(offs(O_DUP, 2), A("pat", 8, 12, 2), feature(SOURCE), ALU.add, 1.0 / 16, ALU.mult)
+    ts(offs(O_MID, 8), A("pat", 8, 16), feature(WOVEN), ALU.add)
+    fill(A("kf", 1, C, 2), 1000.0)
+    fill(A("uu", 0, 272, 136), 4000.0)
+    fill(A("cp"), 0.0)
+    for k in range(2):
+        fill(A("ones", 264 * k, 264 * k + 264), 1.0)
     select(A("ebig"), A("ones"), [[-1, 528]], ALU.is_equal, 3, 4)
 
     def e_(b):
@@ -353,45 +433,26 @@ def rank_program(g, core, T, topo):
 
     for b in range(4):
         quant(*e_(b), A("ebig", 3 - b, 515 - b))
-    iota(A("ci"), [[1, 256]])
-    act(A("iw"), A("ci"), ACT.Identity, scale=1.0 / 65536, bias=pf(S3))
-    iota(pat(O_CD, 4), [[128, 4]])
-    ts(pc(3), pf(S3), 8.0, ALU.mult, pf(B0), ALU.add)
-    ts(pc(8), pf(N4), 16.0, ALU.mult, pc(4), ALU.add)
-    ts(pc(9), pf(K1), 32.0, ALU.mult, pc(3), ALU.add)
-    ts(offs(O_CD, 4), pat(O_CD, 4), pc(8), ALU.add, pc(9), ALU.add)
-    iota(pat(O_NK, 4), [[2, 4]])
-    ts(pc(1), pf(S7), 16.0, ALU.mult, pf(S3), ALU.add)
-    ts(offs(O_NK, 4), pat(O_NK, 4), pc(1), ALU.add, 8.0, ALU.add)
-    ts(offs(O_KF, 4), pat(O_NK, 4), pc(1), ALU.add)
-    ts(pc(14), pf(S7), 0.0, ALU.is_equal, 1000.0, ALU.mult)
-    ts(offs(O_UP, 4), offs(O_NK, 4), pc(14), ALU.add, float(HC), ALU.min)
-    fill(A("kf", 1, C, 2), 1000.0)
-    fill(A("uu", HC, 272, 136), 4000.0)
-    iota(pat(O_DUP, 2), [[1, 2]])
-    ts(pb(12), pf(SA), pf(BA), ALU.subtract, 4.0, ALU.add)
-    ts(pb(11), pb(12), 3, ALU.bitwise_and)
-    ts(pc(13), pb(11), 8.0, ALU.mult, pc(4), ALU.add)
-    ts(offs(O_DUP, 2), pat(O_DUP, 2), pc(13), ALU.add)
-    ts(pc(6), pf(B3), 256.0, ALU.mult)
+    iota(A("ci"), [[HC - 32768, 2], [1, HC]], 32768)
+    act(A("iw"), A("ci"), ACT.Identity, scale=1.0 / 65536, bias=feature(AGAIN))
     quant(A("vc"), A("vs"), A("vin"))
-    copy(A("cand"), ind(A("cdr"), offs(O_CD, 3)))
+    for n in range(2):
+        for k in range(2):
+            copy(A("cand", 24 * n + k, 24 * n + 24, 2), A("cdr", 8 * n + k, 362, 32))
 
-    MIXED, EVEN, ODD = range(3)
-    UNPACKED = (3, 0, 2, 1)
+    EVEN, ODD = range(2)
+    UNPACKED = (0, 1, 0, 1)
+    TILES = ((0, 1, 6), (4, 5, 2, 3))
 
-    def slot(tile, k, c0, c1):
-        return A("fl", 1024 * tile + 4 * c0 + k, 1024 * tile + 4 * c1, 4)
-
-    def place(odd, s, c0, c1):
-        return slot(2 * odd, s, c0, c1) if s < 3 else slot(2 * odd + 1, s - 3, c0, c1)
+    def place(tile, odd, s, c0=0, c1=HC):
+        at = 512 * (tile + s // 2) + 2 * odd + s % 2
+        return A("fl", at + 4 * c0, at - at % 4 + 4 * c1, 4)
 
     def own(b, odd):
         return A("tm", 32 * b + 16 * odd, 32 * b + 16 * odd + 1)
 
-    def signs(b, c0, c1):
-        at = 7 * HC * (c0 // HC) + HC * b
-        return A("sg", at + c0, at + c1)
+    def unweave(out, x0, b, piece):
+        return A(out, x0 + C * piece + b, x0 + C * piece + C, 4)
 
     def state(t, h):
         x0, c0, c1 = 512 * h, HC * h, HC * h + HC
@@ -400,53 +461,63 @@ def rank_program(g, core, T, topo):
             for b in (0, 2, 1, 3):
                 mm(bank(4 * h + b), *e_(b), *half("lc%d" % (t - 1), "ls%d" % (t - 1), h), False, True)
             for b in range(4):
-                move(b < 2, A("xt", x0 + b, x0 + 512, 4), bank(4 * h + b))
+                for a in range(2):
+                    move(b < 2, unweave("xt", x0, b, a), bank(4 * h + b, a, HC, 2))
         quant(*mine, A("xt" if t else "xin", x0, x0 + 512))
         if t < R:
-            for k, kind in ((1, MIXED), (2, ODD), (0, EVEN), (3, EVEN)):
+            mm(bank(4 * h + 1), A("uc"), A("us"), *mine)
+            for k, kind in ((2, ODD), (0, EVEN), (3, EVEN)):
                 mm(bank(4 * h + k), *half("upc", "ups", kind), *mine)
             turn(A("tm", c0, c1), bank(4 * h + 1))
+            pick(half("pc%d" % t, "pz%d" % t, h), mine, offs(O_MID, 8))
 
-    def compare(h, blocks):
-        c0, c1 = HC * h, HC * h + HC
-        for b in blocks:
-            act(signs(b, c0, c1), bank(4 * h + 2), ACT.Sign, scale=-1.0, bias=own(b, 1))
-        for b in blocks:
-            lo, hi = min(max(32 * b, c0), c1), min(max(32 * b + 32, c0), c1)
-            if lo < hi:
-                act(A("sd", lo, hi), bank(4 * h + 3, lo - c0, hi - c0), ACT.Sign, scale=-1.0, bias=own(b, 0))
-            if hi < c1:
-                ts(place(0, b, hi, c1), bank(4 * h, hi - c0, HC), own(b, 0), ALU.is_le)
-                act(place(1, b, hi, c1), signs(b, hi, c1), ACT.Sign, bias=1.0)
-            if c0 < lo:
-                ts(place(0, b - 1, c0, lo), bank(4 * h, 0, lo - c0), own(b, 0), ALU.is_lt)
-                if h == 0 and b - 1 in BELOW:
-                    ts(place(1, b - 1, c0, lo), signs(b, c0, lo), 0.0, ALU.is_gt)
+    def inside(h):
+        for b in range(4):
+            act(A("sg", 512 * h + HC * b, 512 * h + HC * b + HC), bank(4 * h + 2), ACT.Sign, scale=-1.0, bias=own(4 * h + b, 1))
+        for b in range(4):
+            lo, hi, at = 32 * b, 32 * b + 32, 512 * h + HC * b
+            act(A("sd", HC * h + lo, HC * h + hi), bank(4 * h + 3, lo, hi), ACT.Sign, scale=-1.0, bias=own(4 * h + b, 0))
+            if hi < HC:
+                ts(place(2 * h, 0, b, hi, HC), bank(4 * h, hi, HC), own(4 * h + b, 0), ALU.is_le)
+                act(place(2 * h, 1, b, hi, HC), A("sg", at + hi, at + HC), ACT.Sign, bias=1.0)
+            if 0 < lo:
+                ts(place(2 * h, 0, b - 1, 0, lo), bank(4 * h, 0, lo), own(4 * h + b, 0), ALU.is_lt)
+                act(place(2 * h, 1, b - 1, 0, lo), A("sg", at, at + lo), ACT.Relu)
+        tt(place(2 * h, 0, 3), A("sd", HC * h, HC * h + HC), A("thr"), ALU.is_ge)
+        tt(place(2 * h, 1, 3), ind(A("sg", 512 * h, 512 * h + 512), offs(O_DIAG, 8)), A("thr"), ALU.is_ge)
+
+    def across():
+        for odd in range(2):
+            for b in range(4):
+                who, at = ACROSS[odd][b], 1024 + 512 * odd + HC * b
+                if who == "V":
+                    ts(place(4, odd, b), bank(4), own(b, odd), ALU.is_le)
                 else:
-                    act(place(1, b - 1, c0, lo), signs(b, c0, lo), ACT.Relu)
-
-    def diagonal(h):
-        c0, c1 = HC * h, HC * h + HC
-        tt(slot(0, 3, c0, c1), A("sd", c0, c1), A("thr"), ALU.is_gt)
-        tt(slot(2, 3, c0, c1), ind(A("sg", 12 * HC * h, 12 * HC * h + 4 * HC), offs(O_DIAG, 8)), A("thr"), ALU.is_gt)
+                    act(A("sg", at, at + HC), bank(7 - odd), ACT.Sign, scale=-1.0, bias=own(b, odd))
+                    if who == "S":
+                        act(place(4, odd, b), A("sg", at, at + HC), ACT.Sign, bias=1.0)
+                    else:
+                        ts(place(4, odd, b), A("sg", at, at + HC), 0.0, ALU.is_ge)
+                scan(A("su", at - 1024, at - 1024 + HC), A("rr", HC, C), place(4, odd, b), ALU.mult, ALU.subtract)
+            turn(place(6, odd, 0), A("su", 512 * odd + 3, 512 * odd + 512, 4))
 
     def count(h, tiles):
         for tile in tiles:
-            c0 = C * tile + HC * h
+            c0 = HC * tile
             quant(*pair("fc", "fs", c0, c0 + HC), A("fl", 4 * c0, 4 * c0 + 512))
-            mm(bank(4 * h + 1), *pair("fc", "fs", c0, c0 + HC), *half("dc", "ds", tile // 2), tile == 0, tile == 3)
+            mm(bank(4 * h + 1), *pair("fc", "fs", c0, c0 + HC), A("dc"), A("ds"), tile == TILES[h][0], tile == TILES[h][-1])
 
     def places(h):
         c0, c1 = HC * h, HC * h + HC
-        for tile in (0, 2, 1, 3):
-            mm(bank(4 * h + 3), *half("bc", "bs", tile // 2), *pair("fc", "fs", C * tile + c0, C * tile + c1), tile == 0, tile == 3)
-        tt(A("w2", c0, c1), A("iw", c0, c1), bank(4 * h + 3), ALU.add)
+        for tile in TILES[h]:
+            mm(bank(3 - h), A("bc"), A("bs"), *pair("fc", "fs", HC * tile, HC * tile + HC), tile == TILES[h][0], tile == TILES[h][-1])
+        tt(A("w2", c0, c1), A("iw", c0, c1), bank(3 - h), ALU.add)
 
     def order(t, h, donor):
         r0, r1 = RATIOS[h]
         mine, theirs = A("rs%d" % t, r0, r1), A("rl%d" % t, r0, r1)
         tt(A("bf", HC * h, HC * h + HC), bank(4 * h + 1), A("thj"), ALU.is_gt)
-        scan(A("oo", 144 * h, 144 * h + HC), A("rr"), A("bf", HC * h, HC * h + HC), ALU.mult, ALU.add)
+        scan(A("oo", 144 * h + 16, 144 * h + 144), A("rr", 0, HC), A("bf", HC * h, HC * h + HC), ALU.mult, ALU.add)
         act(mine, ind(A("oo", 144 * h, 144 * h + 144), offs(O_EXP, (r1 - r0) // 16)), ACT.Exp, scale=math.log(2.0), bias=-7 * math.log(2.0))
         send(donor, v(theirs), v(mine), mine, "ra%d_%d" % (t, h))
         arrive([theirs], "ra%d_%d" % (t, h), 1)
@@ -454,23 +525,26 @@ def rank_program(g, core, T, topo):
     def leaders(t, h):
         c0, c1, u0, q0, q1 = HC * h, HC * h + HC, 136 * h, 32 * h, 32 * h + 32
         r0, r1 = RATIOS[h]
-        move(h == 0, A("gk", c0, c1), ind(A("w2"), A("cand", 16 * t + 8 * h, 16 * t + 8 * h + 8)))
+        offered = ind(A("w2"), A("cand", 24 * h + 8 * t, 24 * h + 8 * t + 8))
+        ts(A("gf", c0, c1), offered, 192.0 / 256, ALU.is_lt)
+        turn(A("f1", c0, c1), A("gf", c0, c1))
+        act(A("gk", c0, c1), offered, ACT.Copy)
         turn(A("kt", c0, c1), A("gk", c0, c1))
         act(A("kf", c0, c1, 2), ind(A("kt", c0, c1), offs(O_KF, 4)), ACT.Copy)
-        ts(A("f1", c0, c1), A("kt", c0, c1), 192.0 / 256, ALU.is_lt)
         for c in range(0, HC, r1 - r0):
-            scan(A("uu", u0 + c, u0 + c + r1 - r0), A("rl%d" % t, r0, r1), A("f1", c0 + c, c0 + c + r1 - r0), ALU.mult, ALU.add)
+            scan(A("uu", u0 + 8 + c, u0 + 8 + c + r1 - r0), A("rl%d" % t, r0, r1), A("f1", c0 + c, c0 + c + r1 - r0), ALU.mult, ALU.add)
         ts(A("nb", c0, c1, 2), ind(A("uu", u0, u0 + 136), offs(O_UP, 4)), 0.5, ALU.mult, 128.5 + 2.0 ** -9, ALU.add)
         act(A("nb", c0 + 1, c1, 2), ind(A("uu", u0, u0 + 136), offs(O_NK, 4)), ACT.Identity, scale=-0.5, bias=-128.5 - 2.0 ** -9)
         scan(A("ms", c0, c1), A("nb", c0, c1), A("kf", c0, c1), ALU.add, ALU.min)
-        select(A("cp", q0, q0 + 8), A("ms", c0 + 15, c1, 16), [[0, 8]], ALU.is_ge, 0, 0)
-        moves = [(2, 0, 64, 64), (2, 64, 0, 64)] + [(d, 32 * a, 32 * ((a + d) % 4), 32) for d in (1, 3) for a in range(4)]
-        for k, (d, to, fr, n) in enumerate(moves):
-            move(k % 2 == 0, A("cp", q0 + 8 * d, q0 + 8 * d + 8, 1, to, to + n), A("ms", c0 + 15, c1, 16, fr, fr + n))
-        ts(A("dg", q0, q1), ind(A("cp", q0, q1), offs(O_DUP, 2)), 65536.0, ALU.mult)
+        select(A("cp", 2 * q0 + 24, 2 * q0 + 32), A("ms", c0 + 15, c1, 16), [[0, 8]], ALU.is_ge, 0, 0)
+        moves = [(0, 64, 64), (64, 0, 64)] + [(32 * a, 32 * ((a + d) % 4), 32) for d in (1, 3) for a in range(4)]
+        for k, (to, fr, n) in enumerate(moves):
+            at = 2 * q0 + 24 + (fr - to) // 4
+            move(k % 2 == 0, A("cp", at, at + 8, 1, to, to + n), A("ms", c0 + 15, c1, 16, fr, fr + n))
+        ts(A("dg", q0, q1), ind(A("cp", 2 * q0, 2 * q0 + 56), offs(O_DUP, 2)), 65536.0, ALU.mult)
         ts(A("ea", q0, q1), A("dg", q0, q1), C - 1, ALU.bitwise_and)
         turn(A("et", q0, q1), A("ea", q0, q1))
-        ts(A("zo", q0, q1), A("et", q0, q1), pc(6), ALU.add)
+        ts(A("zo", q0, q1), A("et", q0, q1), feature(QUARTER), ALU.add)
 
     def layer(t, h, child):
         x0, q0 = 512 * h, 32 * h
@@ -482,8 +556,8 @@ def rank_program(g, core, T, topo):
         for b in (0, 2, 1, 3):
             mm(bank(4 * h + b), *pair("wq", "wp", 128 * b, 128 * b + 128), *half("zc", "zs", h))
         for b in range(4):
-            for a in range(4):
-                o, i = A("ht", x0 + 128 * a + b, x0 + 128 * a + 128, 4), bank(4 * h + b, a, HC, 4)
+            for a in range(2):
+                o, i = unweave("ht", x0, b, a), bank(4 * h + b, a, HC, 2)
                 if b < 2:
                     ts(o, i, 0.0, ALU.max, 0.015625, ALU.mult)
                 else:
@@ -493,27 +567,26 @@ def rank_program(g, core, T, topo):
         send(child, v(ls), v(hs), hs, "ha%d_%d" % (t, h))
         arrive([lc, ls], "ha%d_%d" % (t, h), 2)
         for b in range(4):
-            mm(bank(4 * h + b), *e_(b), *half("tc%d" % t, "ts%d" % t, h), True, False)
+            mm(bank(4 * h + b), *e_(b), *half("pc%d" % t, "pz%d" % t, h), True, False)
 
     for t in range(R):
         donor, child = T.cores[(rank + 1 + t) % N], T.cores[(rank - 1 - t) % N]
         state(t, 0)
-        compare(0, range(4))
-        diagonal(0)
-        count(0, (0, 2))
+        inside(0)
+        count(0, (0, 1))
         state(t, 1)
-        compare(0, range(4, 8))
-        count(0, (1, 3))
+        across()
+        count(0, (6,))
         order(t, 0, donor)
         places(0)
-        compare(1, range(8))
-        diagonal(1)
-        count(1, (0, 2, 1, 3))
+        count(1, (4, 5))
+        inside(1)
+        count(1, (2, 3))
         order(t, 1, donor)
         places(1)
         for b in range(4):
             mm(bank(UNPACKED[b], 0, C), *e_(b), *pair("tc%d" % t, "ts%d" % t))
-            act(A("dw", C * b, C * b + C), bank(UNPACKED[b], 0, C), ACT.Copy)
+            move(UNPACK[b] == "V", A("dw", C * b, C * b + C), bank(UNPACKED[b], 0, C))
         for h in range(2):
             leaders(t, h)
             layer(t, h, child)

import math
from concourse.mybir import dt, AluOpType as ALU, ActivationFunctionType as ACT

C, R, N, HC = 256, 3, 8, 128
F32, BF, I32, U16, CODE, U8 = "float32", "bfloat16", "int32", "uint16", "float8_e4m3fn_x4", "uint8"
_SIZES = {
    BF: dict(xin=1024, uin=512, vin=512, ones=528, ebig=528, gg=256, gd=64, fr=288, tf=288, bt=512, yi=128, thr=128, sd=256, sg=2048,
             eq=512, bd=512, ex=256, rr=256, thj=128, bf=256, oo=288, fl=3584, su=1024, gf=256, f1=256, nb=256, dw=1024, zt=1024, ht=1024, xt=1024),
    F32: dict(pat=16, ci=256, iw=256, tm=256, w2=256, uu=272, gk=256, kt=256, kf=256, ms=256, cp=128, eb=64, yb=256),
    I32: dict(cdr=368, ui=16, dg=64, ea=64, et=64),
    U16: dict(off=40, uo=16, cand=48, zo=64),
    CODE: dict(uc=128, upc=256, vc=128, wq=512, ec=512, bc=128, dc=128, fc=896, zc=256),
    U8: dict(us=128, ups=256, vs=128, wp=512, es=512, bs=128, ds=128, fs=896, zs=256),
}
SCRATCH = {"ps": ("psum", [128, 4096], F32)}
for _d, _b in _SIZES.items():
    for _k, _n in _b.items():
        SCRATCH[_k] = ("sbuf", [128, _n], _d)
for _t in range(R + 1):
    for _k, _n, _d in (("tc", C, CODE), ("ts", C, U8), ("rs", 96, BF), ("rl", 96, BF), ("hc", C, CODE), ("hs", C, U8), ("lc", C, CODE), ("ls", C, U8),
                       ("pc", C, CODE), ("pz", C, U8)):
        if _t < R or _k[0] == "t":
            SCRATCH["%s%d" % (_k, _t)] = ("sbuf", [128, _n], _d)

SEMAPHORES = ["V", "S", "P", "G", "dx0", "dx1", "du", "dcd", "dw", "dv", "dout", "sent"] + \
    ["%s%d_%d" % (k, t, h) for k in ("ra", "ha") for t in range(R) for h in range(2)]

CYCLE, COLUMN, WAKE, CALL, HOP, LOAD = 0.0009, 0.0006, 0.22, 0.4, 1.25, 1.9
RATIOS = ((0, 32), (32, 96))
MOVES, SLACK = 30000, 0.04
ACROSS = ("VVVV", "SSSS")
UNPACK = "SSSS"


def A(name, c0=0, c1=None, step=1, p0=0, p1=128):
    if c1 is None:
        c1 = SCRATCH[name][1][1]
    return (name, p0, p1, c0, c1, step)


def bank(k, c0=0, c1=HC, step=1):
    return A("ps", 512 * k + c0, 512 * k + c1, step)


def _meet(a, b):
    if a[2] <= b[1] or b[2] <= a[1] or a[4] <= b[3] or b[4] <= a[3]:
        return False
    return (a[3] - b[3]) % math.gcd(a[5], b[5]) == 0


def _width(a):
    return 16 * (a[2][4] - a[2][3]) if a[0] == "ind" else len(range(a[3], a[4], a[5]))


def _length(out, ins, twice=False):
    if any(a[0] == "ind" for a in ins):
        return 0.06 + 1.5 * CYCLE * _width(out)
    narrow = all(SCRATCH[a[0]][2] in (BF, U16) for a in [out] + ins)
    return CYCLE * max(64, _width(out) * (0.5 if narrow else 1) * (2 if twice else 1))


def _touch(ops):
    deps, behind, seen = [], [], {}
    for i, o in enumerate(ops):
        d, k = set(), set()
        mine = [(a, False) for a in o["r"]] + [(a, True) for a in o["w"]]
        for a, wa in mine:
            for j, b, wb in seen.get(a[0], []):
                if a[0] == "ps":
                    if a[3] // 512 == b[3] // 512:
                        if o["q"] != ops[j]["q"]:
                            d.add(j)
                        elif o["q"] == "P":
                            k.add(j)
                elif (wa or wb) and _meet(a, b):
                    d.add(j)
        for a, wa in mine:
            seen.setdefault(a[0], []).append((i, a, wa))
        deps.append(d)
        behind.append(k)
    return deps, behind


def _arrange(ops):
    deps, behind = _touch(ops)
    n, last = len(ops), {}
    for i, o in enumerate(ops):
        if o["q"] is None:
            behind[i] |= set(j for j in range(i) if ops[j].get("to") == o["sem"])
        elif o.get("dma") or "to" in o:
            if o["q"] in last:
                behind[i].add(last[o["q"]])
            last[o["q"]] = i
    before = [{j: ops[j]["c"] for j in behind[i]} for i in range(n)]
    for i in range(n):
        for j in deps[i]:
            before[i][j] = ops[j]["c"] + ops[j].get("lag", 0.0) + WAKE
    after = [{} for _ in ops]
    for i in range(n):
        for j, gap in before[i].items():
            after[j][i] = gap - ops[j]["c"] + ops[i]["c"]
    tail = [o.get("lag", 0.0) for o in ops]

    def lay(order, edges, first):
        at, taken = [0.0] * n, {q: [] for q in "VSPGY"}
        for i in order:
            t, c = max([first[i]] + [at[j] + gap for j, gap in edges[i].items()]), ops[i]["c"]
            if ops[i]["q"] is not None:
                busy, k = taken[ops[i]["q"]], 0
                while k < len(busy) and busy[k][0] < t + c - 1e-9:
                    t = max(t, busy[k][1])
                    k += 1
                busy.insert(k, (t, t + c))
            at[i] = t
        return at

    back = [0.0] * n
    for i in range(n - 1, -1, -1):
        back[i] = max([tail[i]] + [back[j] + gap for j, gap in after[i].items()])
    best = None
    for _ in range(3):
        start = lay(sorted(range(n), key=lambda i: (-back[i] - ops[i]["c"], i)), before, [0.0] * n)
        span = max(start[i] + ops[i]["c"] + tail[i] for i in range(n))
        if best is None or span < best[0]:
            best = (span, start)
        back = lay(sorted(range(n), key=lambda i: (-start[i] - ops[i]["c"], -i)), after, tail)
    if not _ORDER:
        _ORDER.append(_shorten(ops, before, after, tail, best[1]))
    return [ops[i] for i in _ORDER[0]]


_ORDER = []


def _shorten(ops, before, after, tail, start):
    n = len(ops)
    reach, needs = [0] * n, []
    for i in range(n):
        keep, seen = [], 0
        for j in sorted(before[i], reverse=True):
            if not seen >> j & 1 or before[i][j] > ops[j]["c"] + WAKE + 1e-9:
                keep.append((j, before[i][j]))
            seen |= reach[j] | 1 << j
        reach[i] = seen
        needs.append(keep)
    c, q = [o["c"] for o in ops], [o["q"] for o in ops]

    def play(order):
        at, why, last, span, end = [0.0] * n, [None] * n, {}, 0.0, 0
        for i in order:
            t, w = 0.0, None
            for j, gap in needs[i]:
                if at[j] + gap > t:
                    t, w = at[j] + gap, (j, False)
            if q[i] is not None:
                j = last.get(q[i])
                if j is not None and at[j] + c[j] >= t:
                    t, w = at[j] + c[j], (j, True)
                last[q[i]] = i
            at[i], why[i] = t, w
            if t + c[i] + tail[i] > span:
                span, end = t + c[i] + tail[i], i
        return span, at, why, end

    seed = [1]

    def draw():
        seed[0] = seed[0] * 48271 % 2147483647
        return seed[0] / 2147483647

    now = best = play(sorted(range(n), key=lambda i: (start[i], i)))
    for step in range(MOVES):
        pairs, i = [], now[3]
        while now[2][i] is not None:
            j, neighbour = now[2][i]
            if neighbour and not reach[i] >> j & 1:
                pairs.append((j, i))
            i = j
        if not pairs:
            break
        a, b = pairs[int(draw() * len(pairs))]
        order = sorted(range(n), key=lambda i: now[1][i])
        pos = {x: p for p, x in enumerate(order)}
        if draw() < 0.5:
            who, lo, hi = b, max([pos[j] + 1 for j, gap in needs[b]] + [pos[a] - 25, 0]), pos[a]
        else:
            who, lo, hi = a, pos[b], min([pos[j] - 1 for j in after[a]] + [pos[b] + 25, n - 1])
        if lo > hi:
            continue
        order.insert(lo + int(draw() * (hi + 1 - lo)), order.pop(pos[who]))
        new = play(order)
        if new[0] <= now[0] - SLACK * (1 - step / MOVES) * math.log(draw()):
            now = new
            if new[0] < best[0]:
                best = new
    return sorted(range(n), key=lambda i: (best[1][i], i))


def _emit(g, T, ops):
    queues = {"V": g.vector, "S": g.scalar, "P": g.tensor, "G": g, "Y": g.sync}
    deps = _touch(ops)[0]
    clock, known, need = [None] * len(ops), {q: {} for q in queues}, []
    for i, o in enumerate(ops):
        waits = []
        if o["q"] is not None:
            k = known[o["q"]]
            for j in sorted(deps[i], reverse=True):
                e = ops[j]
                key, val = (e["sem"], 0) if "sem" in e else (e["q"], j)
                if k.get(key, -1) >= val:
                    continue
                waits.append(j)
                k[key] = val
                for kk, vv in clock[j].items():
                    if k.get(kk, -1) < vv:
                        k[kk] = vv
            clock[i] = dict(k)
        else:
            clock[i] = {}
        need.append(waits)
    signal = set(j for w in need for j in w if "sem" not in ops[j])
    count, value, total = {}, {}, {}
    for i, o in enumerate(ops):
        if i in signal:
            count[o["q"]] = count.get(o["q"], 0) + 1
            value[i] = count[o["q"]]
        if "sem" in o:
            total[o["sem"]] = total.get(o["sem"], 0) + o["n"]
    for i, o in enumerate(ops):
        if o["q"] is None:
            continue
        q = queues[o["q"]]
        for j in need[i]:
            e = ops[j]
            if "sem" in e:
                q.wait_ge(T.sem[e["sem"]], total[e["sem"]])
            else:
                q.wait_ge(T.sem[e["q"]], value[j])
        ins = o["f"](q)
        if i in signal:
            ins.then_inc(T.sem[o["q"]], 1)
        elif o.get("dma"):
            ins.then_inc(T.sem[o["sem"]], 16)
    for s in ("sent", "dout"):
        g.wait_ge(T.sem[s], total[s])


def rank_program(g, core, T, topo):
    rank = T.rank_of(core)
    if rank is None:
        return
    ops = []

    def v(a):
        if not isinstance(a, tuple):
            return a
        if a[0] == "ind":
            return v(a[1]).indirect(v(a[2]))
        if a[5] == 1:
            return T[a[0]][a[1]:a[2], a[3]:a[4]]
        return T[a[0]][a[1]:a[2], a[3]:a[4]:a[5]]

    def ind(win, offs):
        return ("ind", win, offs)

    def op(q, f, c, w, r, **more):
        reads = []
        for a in r:
            if isinstance(a, tuple):
                reads += [a[1], a[2]] if a[0] == "ind" else [a]
        ops.append(dict(q=q, f=f, c=c, w=list(w), r=reads, **more))

    def copy(out, in_):
        op("V", lambda q: q.tensor_copy(v(out), v(in_)), _length(out, [in_]), [out], [in_])

    def tt(out, a, b, o):
        op("V", lambda q: q.tensor_tensor(v(out), v(a), v(b), o), _length(out, [a, b], "ps" not in (a[0], b[0])), [out], [a, b])

    def ts(out, a, s1, o1, s2=None, o2=None):
        if o2 is None:
            op("V", lambda q: q.tensor_scalar(v(out), v(a), v(s1), None, o1), _length(out, [a]), [out], [a, s1])
        else:
            op("V", lambda q: q.tensor_scalar(v(out), v(a), v(s1), v(s2), o1, o2), _length(out, [a]), [out], [a, s1, s2])

    def scan(out, d0, d1, o0, o1):
        op("V", lambda q: q.tensor_tensor_scan(v(out), v(d0), v(d1), 0.0, o0, o1), _length(out, [d0, d1]), [out], [d0, d1])

    def turn(out, in_):
        op("V", lambda q: q.transpose(v(out), v(in_)), _length(out, [in_]), [out], [in_])

    def fill(out, c):
        op("V", lambda q: q.memset(v(out), c), _length(out, []), [out], [])

    def quant(c, s, in_):
        op("V", lambda q: q.quantize_mx(v(c), v(s), v(in_)), 0.012 + 0.27 * CYCLE * _width(in_), [c, s], [in_])

    def act(out, in_, f, more=0.0, **kw):
        c = _length(out, [in_]) if in_[0] == "ind" else CYCLE * max(64, _width(out))
        op("S", lambda q: q.activation(v(out), v(in_), f, **{k: v(x) for k, x in kw.items()}), c + more, [out], [in_] + list(kw.values()))

    def move(on_vector, out, in_):
        if on_vector:
            copy(out, in_)
        else:
            act(out, in_, ACT.Copy)

    def mm(out, lc, ls, rc, rs, start=True, stop=True):
        op("P", lambda q: q.matmul_mx(v(out), v(lc), v(ls), v(rc), v(rs), start, stop), COLUMN * (_width(out) + 16), [out], [lc, ls, rc, rs])

    def iota(out, pattern, base=0, cm=0):
        c = 0.13 + 2 * CYCLE * _width(out)
        if SCRATCH[out[0]][2] == I32:
            op("G", lambda q: q.iota(v(out), pattern, base, cm), c, [out], [])
        else:
            op("G", lambda q: q.iota(v(out), pattern, base, cm, allow_small_or_imprecise_dtypes=True), c, [out], [])

    def select(out, in_, pattern, o, base, cm):
        op("G", lambda q: q.affine_select(v(out), v(in_), pattern, o, 0.0, base, cm), 0.17 + 2 * CYCLE * _width(out), [out], [in_])

    def dma(q, sem, out, in_, w, r):
        op(q, lambda e: e.dma_start(out, in_), 0.05, w, r, sem=sem, n=16, dma=True, lag=LOAD - 0.2)

    def raw(a):
        return v(a).bitcast(dt.uint8)

    peers = [T.cores[(rank + d) % N] for d in range(1, R + 1)] + [T.cores[(rank - d) % N] for d in range(1, R + 1)]
    mask = topo.mask(core, peers[0])
    for p in peers:
        mask = mask & topo.mask(core, p)
    nen = bin(mask).count("1")

    def send(dst, out, in_, src, sem):
        rid, pid = topo.addr(dst, core)
        length = CALL + (1.0 if sem == "ra0_0" else 0.0)
        op("G", lambda q: q.remote_dma(out, in_, T.sem[sem], T.sem.sent, pid, rid, mask), length, [], [src], sem="sent", n=nen, to=sem)

    def arrive(views, sem, calls):
        op(None, None, HOP, views, [], sem=sem, n=nen * calls)

    def pair(c, s, c0=0, c1=C):
        return A(c, c0, c1), A(s, c0, c1)

    def half(c, s, h):
        return pair(c, s, HC * h, HC * h + HC)

    def offs(o, k):
        return A("off", o, o + k)

    def pick(out, win, lst):
        act(out[1], ind(win[1], lst), ACT.Copy)
        op("V", lambda q: q.tensor_copy(v(out[0]).bitcast(dt.uint32), v(win[0]).bitcast(dt.uint32).indirect(v(lst))),
           _length(out[0], [ind(win[0], lst)]), [out[0]], [win[0], lst])

    dma("Y", "du", T.uin[:, :], T.u[:, :], [A("uin")], [])
    for h in range(2):
        dma("Y", "dx%d" % h, T.xin[:, 512 * h:512 * h + 512], T.x[:, 512 * h:512 * h + 512], [A("xin", 512 * h, 512 * h + 512)], [])
    for k in range(8):
        o = 16 * (k % 2) + 2 * (k // 2)
        dma("Y", "dcd", T.cdr[16 * k:16 * k + 16, 0:362], T.cd[:, o:o + 362], [A("cdr", p0=16 * k, p1=16 * k + 16)], [])
    dma("Y", "dw", raw(A("wq")), T.wc[:, :], [A("wq")], [])
    dma("Y", "dw", T.wp[:, :], T.ws[:, :], [A("wp")], [])
    dma("Y", "dv", T.vin[:, :], T.v[:, :], [A("vin")], [])

    O_DIAG, O_EXP, O_NK, O_KF, O_UP, O_DUP, O_MID = 0, 8, 12, 16, 20, 24, 26
    BLOCK, ROW, SUMS, STEPS, FIRST, QUARTER, WOVEN, AGAIN, SOURCE = range(9)

    def feature(k, c=0, n=1):
        return A("tf", 32 * k + c, 32 * k + c + n)

    def lay_out(k, pattern, base=0, cm=0):
        iota(A("fr", 32 * k, 32 * k + 32), pattern, base, cm)

    iota(A("ui"), [[16, 2], [32, 4], [0, 2]])
    copy(A("uo"), A("ui"))
    quant(A("uc"), A("us"), A("uin"))
    for odd in range(2):
        pick(half("upc", "ups", odd), (A("uc"), A("us")), A("uo", 8 * odd, 8 * odd + 8))
    lay_out(BLOCK, [[0, 32]], 0, 1)
    turn(feature(BLOCK, 0, 32), A("fr", 0, 32))
    iota(A("gg", 0, HC), [[0, 16], [16, 8]])
    iota(A("gg", HC, C), [[0, 2], [16, 8], [0, 8]])
    for odd in range(2):
        e0 = C * odd
        ts(A("eq", e0, e0 + C), A("gg"), feature(BLOCK, 16 * odd), ALU.is_equal)
        this, other, prior = A("eq", e0 + 128, e0 + 192), A("eq", e0, e0 + 64), A("eq", e0 + 184, e0 + 248)
        tt(A("bd", 2 * odd, 512, 8), this, other, ALU.subtract)
        tt(A("bd", 2 * odd + 4, 512, 8), other, prior, ALU.subtract)
        for k in range(2):
            act(A("bt", 2 * odd + k, 512, 4), A("eq", e0, e0 + HC), ACT.Identity, scale=1.0 / 256)
    copy(A("bd", 1, 512, 2), A("bd", 0, 512, 2))
    quant(A("dc"), A("ds"), A("bd"))
    quant(A("bc"), A("bs"), A("bt"))
    iota(A("yi"), [[0, 4], [1, 32]], 0, -1)
    ts(A("thr"), A("yi"), feature(BLOCK), ALU.add, 0.0, ALU.is_le)
    lay_out(ROW, [[0, 2], [1, 16]])
    turn(feature(ROW, 0, 32), A("fr", 32, 64))
    iota(A("pat", 0, 8), [[HC + 32, 4], [16, 2]])
    ts(offs(O_DIAG, 8), A("pat", 0, 8), feature(ROW), ALU.add)
    iota(A("gd"), [[1, 8], [-1, 8]])
    ts(A("thj", 0, HC, 2), A("gd"), 0.0, ALU.is_le, 0.5, ALU.subtract)
    ts(A("thj", 17, HC, 2), A("gd", 8, 64), 0.0, ALU.is_gt, 0.5, ALU.subtract)
    fill(A("thj", 1, 16, 2), 0.5)
    fill(A("ex"), 0.0)
    fill(A("ex", 0, HC, 16), -200.0)
    fill(A("ex", HC, C, 4), -200.0)
    act(A("rr"), A("ex"), ACT.Exp, more=1.4)
    fill(A("oo", 0, 288, 144), -400.0)
    fill(A("fl", 6 * 512 + 1, 7 * 512, 2), 0.0)
    lay_out(SUMS, [[0, 4], [16, 8]], 31)
    lay_out(STEPS, [[0, 2], [1, 2], [16, 8]])
    lay_out(FIRST, [[0, 4], [1024, 8]])
    lay_out(QUARTER, [[0, 8], [256, 4]])
    lay_out(WOVEN, [[0, 2], [1, 8], [64, 2]])
    lay_out(AGAIN, [[0, 2], [1, 2], [0, 8]])
    lay_out(SOURCE, [[0, 2], [128, 4], [0, 4]], 384, -3)
    turn(feature(SUMS, 0, 7 * 32), A("fr", 32 * SUMS, 288))
    iota(A("pat", 8, 16), [[8, 8]])
    ts(offs(O_EXP, 4), feature(ROW, 0, 4), 1000.0, ALU.mult, feature(SUMS), ALU.min)
    ts(offs(O_KF, 4), A("pat", 8, 12), 0.25, ALU.mult, feature(STEPS), ALU.add)
    ts(offs(O_NK, 4), offs(O_KF, 4), 16.0, ALU.add)
    ts(offs(O_UP, 4), offs(O_NK, 4), feature(FIRST), ALU.min)
    ts(offs(O_DUP, 2), A("pat", 8, 12, 2), feature(SOURCE), ALU.add, 1.0 / 16, ALU.mult)
    ts(offs(O_MID, 8), A("pat", 8, 16), feature(WOVEN), ALU.add)
    fill(A("kf", 1, C, 2), 1000.0)
    fill(A("uu", 0, 272, 136), 4000.0)
    fill(A("cp"), 0.0)
    for k in range(2):
        fill(A("ones", 264 * k, 264 * k + 264), 1.0)
    select(A("ebig"), A("ones"), [[-1, 528]], ALU.is_equal, 3, 4)

    def e_(b):
        return pair("ec", "es", 128 * b, 128 * b + 128)

    for b in range(4):
        quant(*e_(b), A("ebig", 3 - b, 515 - b))
    iota(A("ci"), [[HC - 32768, 2], [1, HC]], 32768)
    act(A("iw"), A("ci"), ACT.Identity, scale=1.0 / 65536, bias=feature(AGAIN))
    quant(A("vc"), A("vs"), A("vin"))
    for n in range(2):
        for k in range(2):
            copy(A("cand", 24 * n + k, 24 * n + 24, 2), A("cdr", 8 * n + k, 362, 32))

    EVEN, ODD = range(2)
    UNPACKED = (0, 1, 0, 1)
    TILES = ((0, 1, 6), (4, 5, 2, 3))

    def place(tile, odd, s, c0=0, c1=HC):
        at = 512 * (tile + s // 2) + 2 * odd + s % 2
        return A("fl", at + 4 * c0, at - at % 4 + 4 * c1, 4)

    def own(b, odd):
        return A("tm", 32 * b + 16 * odd, 32 * b + 16 * odd + 1)

    def unweave(out, x0, b, piece):
        return A(out, x0 + C * piece + b, x0 + C * piece + C, 4)

    def state(t, h):
        x0, c0, c1 = 512 * h, HC * h, HC * h + HC
        mine = half("tc%d" % t, "ts%d" % t, h)
        if t > 0:
            for b in (0, 2, 1, 3):
                mm(bank(4 * h + b), *e_(b), *half("lc%d" % (t - 1), "ls%d" % (t - 1), h), False, True)
            for b in range(4):
                for a in range(2):
                    move(b < 2, unweave("xt", x0, b, a), bank(4 * h + b, a, HC, 2))
        quant(*mine, A("xt" if t else "xin", x0, x0 + 512))
        if t < R:
            mm(bank(4 * h + 1), A("uc"), A("us"), *mine)
            for k, kind in ((2, ODD), (0, EVEN), (3, EVEN)):
                mm(bank(4 * h + k), *half("upc", "ups", kind), *mine)
            turn(A("tm", c0, c1), bank(4 * h + 1))
            pick(half("pc%d" % t, "pz%d" % t, h), mine, offs(O_MID, 8))

    def inside(h):
        for b in range(4):
            act(A("sg", 512 * h + HC * b, 512 * h + HC * b + HC), bank(4 * h + 2), ACT.Sign, scale=-1.0, bias=own(4 * h + b, 1))
        for b in range(4):
            lo, hi, at = 32 * b, 32 * b + 32, 512 * h + HC * b
            act(A("sd", HC * h + lo, HC * h + hi), bank(4 * h + 3, lo, hi), ACT.Sign, scale=-1.0, bias=own(4 * h + b, 0))
            if hi < HC:
                ts(place(2 * h, 0, b, hi, HC), bank(4 * h, hi, HC), own(4 * h + b, 0), ALU.is_le)
                act(place(2 * h, 1, b, hi, HC), A("sg", at + hi, at + HC), ACT.Sign, bias=1.0)
            if 0 < lo:
                ts(place(2 * h, 0, b - 1, 0, lo), bank(4 * h, 0, lo), own(4 * h + b, 0), ALU.is_lt)
                act(place(2 * h, 1, b - 1, 0, lo), A("sg", at, at + lo), ACT.Relu)
        tt(place(2 * h, 0, 3), A("sd", HC * h, HC * h + HC), A("thr"), ALU.is_ge)
        tt(place(2 * h, 1, 3), ind(A("sg", 512 * h, 512 * h + 512), offs(O_DIAG, 8)), A("thr"), ALU.is_ge)

    def across():
        for odd in range(2):
            for b in range(4):
                who, at = ACROSS[odd][b], 1024 + 512 * odd + HC * b
                if who == "V":
                    ts(place(4, odd, b), bank(4), own(b, odd), ALU.is_le)
                else:
                    act(A("sg", at, at + HC), bank(7 - odd), ACT.Sign, scale=-1.0, bias=own(b, odd))
                    if who == "S":
                        act(place(4, odd, b), A("sg", at, at + HC), ACT.Sign, bias=1.0)
                    else:
                        ts(place(4, odd, b), A("sg", at, at + HC), 0.0, ALU.is_ge)
                scan(A("su", at - 1024, at - 1024 + HC), A("rr", HC, C), place(4, odd, b), ALU.mult, ALU.subtract)
            turn(place(6, odd, 0), A("su", 512 * odd + 3, 512 * odd + 512, 4))

    def count(h, tiles):
        for tile in tiles:
            c0 = HC * tile
            quant(*pair("fc", "fs", c0, c0 + HC), A("fl", 4 * c0, 4 * c0 + 512))
            mm(bank(4 * h + 1), *pair("fc", "fs", c0, c0 + HC), A("dc"), A("ds"), tile == TILES[h][0], tile == TILES[h][-1])

    def places(h):
        c0, c1 = HC * h, HC * h + HC
        for tile in TILES[h]:
            mm(bank(3 - h), A("bc"), A("bs"), *pair("fc", "fs", HC * tile, HC * tile + HC), tile == TILES[h][0], tile == TILES[h][-1])
        tt(A("w2", c0, c1), A("iw", c0, c1), bank(3 - h), ALU.add)

    def order(t, h, donor):
        r0, r1 = RATIOS[h]
        mine, theirs = A("rs%d" % t, r0, r1), A("rl%d" % t, r0, r1)
        tt(A("bf", HC * h, HC * h + HC), bank(4 * h + 1), A("thj"), ALU.is_gt)
        scan(A("oo", 144 * h + 16, 144 * h + 144), A("rr", 0, HC), A("bf", HC * h, HC * h + HC), ALU.mult, ALU.add)
        act(mine, ind(A("oo", 144 * h, 144 * h + 144), offs(O_EXP, (r1 - r0) // 16)), ACT.Exp, scale=math.log(2.0), bias=-7 * math.log(2.0))
        send(donor, v(theirs), v(mine), mine, "ra%d_%d" % (t, h))
        arrive([theirs], "ra%d_%d" % (t, h), 1)

    def leaders(t, h):
        c0, c1, u0, q0, q1 = HC * h, HC * h + HC, 136 * h, 32 * h, 32 * h + 32
        r0, r1 = RATIOS[h]
        offered = ind(A("w2"), A("cand", 24 * h + 8 * t, 24 * h + 8 * t + 8))
        ts(A("gf", c0, c1), offered, 192.0 / 256, ALU.is_lt)
        turn(A("f1", c0, c1), A("gf", c0, c1))
        act(A("gk", c0, c1), offered, ACT.Copy)
        turn(A("kt", c0, c1), A("gk", c0, c1))
        act(A("kf", c0, c1, 2), ind(A("kt", c0, c1), offs(O_KF, 4)), ACT.Copy)
        for c in range(0, HC, r1 - r0):
            scan(A("uu", u0 + 8 + c, u0 + 8 + c + r1 - r0), A("rl%d" % t, r0, r1), A("f1", c0 + c, c0 + c + r1 - r0), ALU.mult, ALU.add)
        ts(A("nb", c0, c1, 2), ind(A("uu", u0, u0 + 136), offs(O_UP, 4)), 0.5, ALU.mult, 128.5 + 2.0 ** -9, ALU.add)
        act(A("nb", c0 + 1, c1, 2), ind(A("uu", u0, u0 + 136), offs(O_NK, 4)), ACT.Identity, scale=-0.5, bias=-128.5 - 2.0 ** -9)
        scan(A("ms", c0, c1), A("nb", c0, c1), A("kf", c0, c1), ALU.add, ALU.min)
        select(A("cp", 2 * q0 + 24, 2 * q0 + 32), A("ms", c0 + 15, c1, 16), [[0, 8]], ALU.is_ge, 0, 0)
        moves = [(0, 64, 64), (64, 0, 64)] + [(32 * a, 32 * ((a + d) % 4), 32) for d in (1, 3) for a in range(4)]
        for k, (to, fr, n) in enumerate(moves):
            at = 2 * q0 + 24 + (fr - to) // 4
            move(k % 2 == 0, A("cp", at, at + 8, 1, to, to + n), A("ms", c0 + 15, c1, 16, fr, fr + n))
        ts(A("dg", q0, q1), ind(A("cp", 2 * q0, 2 * q0 + 56), offs(O_DUP, 2)), 65536.0, ALU.mult)
        ts(A("ea", q0, q1), A("dg", q0, q1), C - 1, ALU.bitwise_and)
        turn(A("et", q0, q1), A("ea", q0, q1))
        ts(A("zo", q0, q1), A("et", q0, q1), feature(QUARTER), ALU.add)

    def layer(t, h, child):
        x0, q0 = 512 * h, 32 * h
        hc, hs = half("hc%d" % t, "hs%d" % t, h)
        lc, ls = half("lc%d" % t, "ls%d" % t, h)
        for k in range(2):
            move(k == 0, A("zt", x0 + C * k, x0 + C * k + C), ind(A("dw"), A("zo", q0 + 16 * k, q0 + 16 * k + 16)))
        quant(*half("zc", "zs", h), A("zt", x0, x0 + 512))
        for b in (0, 2, 1, 3):
            mm(bank(4 * h + b), *pair("wq", "wp", 128 * b, 128 * b + 128), *half("zc", "zs", h))
        for b in range(4):
            for a in range(2):
                o, i = unweave("ht", x0, b, a), bank(4 * h + b, a, HC, 2)
                if b < 2:
                    ts(o, i, 0.0, ALU.max, 0.015625, ALU.mult)
                else:
                    act(o, i, ACT.Relu, scale=0.015625)
        quant(hc, hs, A("ht", x0, x0 + 512))
        send(child, raw(lc), raw(hc), hc, "ha%d_%d" % (t, h))
        send(child, v(ls), v(hs), hs, "ha%d_%d" % (t, h))
        arrive([lc, ls], "ha%d_%d" % (t, h), 2)
        for b in range(4):
            mm(bank(4 * h + b), *e_(b), *half("pc%d" % t, "pz%d" % t, h), True, False)

    for t in range(R):
        donor, child = T.cores[(rank + 1 + t) % N], T.cores[(rank - 1 - t) % N]
        state(t, 0)
        inside(0)
        count(0, (0, 1))
        state(t, 1)
        across()
        count(0, (6,))
        order(t, 0, donor)
        places(0)
        count(1, (4, 5))
        inside(1)
        count(1, (2, 3))
        order(t, 1, donor)
        places(1)
        for b in range(4):
            mm(bank(UNPACKED[b], 0, C), *e_(b), *pair("tc%d" % t, "ts%d" % t))
            move(UNPACK[b] == "V", A("dw", C * b, C * b + C), bank(UNPACKED[b], 0, C))
        for h in range(2):
            leaders(t, h)
            layer(t, h, child)
    copy(A("eb"), A("et"))
    for n in range(2):
        dma("Y", "dout", T.el[:, HC * n:HC * n + HC], T.eb[0:128:4, 32 * n:32 * n + 32], [], [A("eb")])
    tc, tsc = "tc%d" % R, "ts%d" % R
    for h in range(2):
        c0, c1 = HC * h, HC * h + HC
        state(R, h)
        mm(bank(4 * h), A("vc"), A("vs"), *half(tc, tsc, h))
        dma("Y", "dout", T.oc[:, 4 * c0:4 * c1], raw(A(tc, c0, c1)), [], [A(tc, c0, c1)])
        move(h == 1, A("yb", c0, c1), bank(4 * h))
        dma("S", "dout", T.y[:, c0:c1], T.yb[:, c0:c1], [], [A("yb", c0, c1)])
    for k in range(4):
        dma("Y", "dout", T.osc[4 * k:4 * k + 4, :], T[tsc][32 * k:32 * k + 4, :], [], [A(tsc)])
    _emit(g, T, _arrange(ops))
